import numpy as np, ml_dtypes
CORES = [16,18,20,22]
N = 4
import mx_ref
BF = ml_dtypes.bfloat16
def entries(a):
    return np.ascontiguousarray(a.T).reshape(-1)
def table(e):
    return np.ascontiguousarray(np.reshape(e, (-1, 16)).T).astype(np.int32)
def pick(q, e):
    c = np.concatenate([q[0].reshape(128, -1, 4), np.zeros((128, 1, 4), np.uint8)], axis=1); s = np.concatenate([q[1], np.ones((16, 1), np.uint8)], axis=1)
    return (np.ascontiguousarray(c[:, e].reshape(128, -1)), np.ascontiguousarray(s[:, e]))
def join(*qs):
    return (np.concatenate([q[0] for q in qs], axis=1), np.concatenate([q[1] for q in qs], axis=1))
def put(q, e, v):
    c, s = q[0].reshape(128, -1, 4).copy(), q[1].copy(); c[:, e] = v[0].reshape(128, -1, 4); s[:, e] = v[1]
    return (c.reshape(128, -1), s)
def pk(c, s):
    return (np.ascontiguousarray(c), mx_ref.live(s))
def emit(q):
    return q[0], q[1]
def decode(q):
    o = []
    for b in range(4):
        e = np.zeros((128, 128, 4), np.float32); e[np.arange(128), np.arange(128), b] = 1
        o.append(mx_ref.matmul(mx_ref.quantize(e.reshape(128, 512).astype(BF)), q))
    return np.stack(o, axis=2).reshape(128, -1)
def cut(t, i, w=512):
    return t[:, w * i:w * i + w]
def f(rng, *shape):
    return mx_ref.flush((rng.standard_normal(shape, dtype=np.float32) * np.exp2(rng.integers(-2, 3, shape[:-1] + (1,)))).astype(BF))
def wide(rng, *shape, cols=0):
    v = rng.standard_normal(shape, dtype=np.float32) * np.exp2(rng.integers(-12, 13, shape)).astype(np.float32)
    if cols: v *= np.repeat(np.exp2(rng.integers(-cols, cols + 1, shape[:-2] + (1, shape[-1] // 4))) * (rng.random(shape[:-2] + (1, shape[-1] // 4)) > 0.0625), 4, axis=-1).astype(np.float32)
    return mx_ref.flush(v.astype(BF))
P, M, A, CAPP, R = 512, 128, 64, 32, 3
def big(v):
    v = v.astype(np.float32)
    v[np.abs(v) < np.float32(2.0 ** -16)] = 0
    return v.astype(BF)
def listed(e):
    return np.stack([table(v) for v in e])
def setup_inputs(rng):
    return {"ky": big(f(rng, N, 128, 4 * P)), "nx": listed(rng.integers(0, N * M, (N, P))), "x": big(f(rng, N, 128, 4 * A)), "st": listed(rng.integers(0, N * M, (N, A))), "w": f(rng, N, 128, 512)}
def setup_inputs_spread(rng):
    d = setup_inputs(rng)
    d["ky"] = big(wide(rng, N, 128, 4 * P, cols=6))
    d["x"] = big(wide(rng, N, 128, 4 * A, cols=4))
    return d
def setup_inputs_ties(rng):
    d = setup_inputs(rng)
    o = np.argsort(rng.random((N, M, 4)), axis=2) % 2
    v = d["ky"].reshape(N, 128, M, 4, 4)
    v = np.ascontiguousarray(np.stack([np.take_along_axis(v[r], np.broadcast_to(o[r][None, :, :, None], (128, M, 4, 4)), axis=2) for r in range(N)]))
    for r in range(N): v[r][:, rng.permutation(M)[:M // 8]] = 0
    d["ky"] = v.reshape(N, 128, 4 * P)
    to = np.argsort(rng.random((N, M, N)), axis=2)[:, :, :4]
    d["nx"] = listed((to * M + rng.integers(0, M, (N, M, 4))).reshape(N, P))
    return d
def setup_inputs_crowd(rng):
    d = setup_inputs(rng)
    o, st = rng.permutation(N), np.zeros((N, A), int)
    for i in range(N):
        s, to = o[i], o[(i + 1) % N]
        here = rng.permutation(A) < (CAPP if i % 2 == 0 else A - CAPP // 4)
        near = to * M + (rng.integers(0, M, A) if i % 2 == 0 else np.full(A, int(rng.integers(0, M))))
        far = (to + rng.integers(1, N, A)) % N * M + rng.integers(0, M, A)
        st[s] = np.where(here, near, far)
    d["st"] = listed(st)
    return d
def kept(rng, *shape):
    return 4 * rng.integers(0, M // 4, shape) + rng.integers(0, 3, shape)
def setup_inputs_stay(rng):
    d = setup_inputs(rng)
    o = rng.permutation(N)
    z, z2 = int(o[0]), int(o[1])
    v = np.arange(M)[None, :, None]
    to = np.arange(N)[:, None, None] * M + np.where(v % 2 == 0, v, kept(rng, N, M, 4))
    to[z, 3::4] = o[rng.integers(2, N, (M // 4, 4))] * M + rng.integers(0, M, (M // 4, 4))
    to[z2] = z * M + kept(rng, M, 4)
    d["nx"] = listed(to.reshape(N, P))
    leave = np.zeros((N, A), bool)
    leave[:, :CAPP] = np.argsort(rng.random((N, CAPP)), axis=1) < CAPP // 4
    st = z * M + np.where(leave, 4 * rng.integers(0, M // 4, (N, A)) + 3, kept(rng, N, A))
    n = CAPP + CAPP // 2
    st[:, n:] = z2 * M + rng.integers(0, M, (N, A - n))
    low = rng.permutation(N) < N // 2
    st[low] = np.roll(st[low], A - n, axis=1)
    d["st"] = listed(st)
    return d
def setup_inputs_turn(rng):
    d = setup_inputs(rng)
    sign = rng.choice([-1.0, 1.0], (128, 4))
    top = np.arange(128) < 64
    o = np.argsort(rng.random((N, M, 4)), axis=2).reshape(N, P)
    g = np.where(top[None, :, None], np.exp2(-2.0 * o)[:, None, :], np.exp2(2.0 * o + 2)[:, None, :])
    d["ky"] = big(((1 + rng.random((N, 128, P, 4))) * g[..., None] * sign[None, :, None, :]).reshape(N, 128, 4 * P))
    d["x"] = big(((1 + rng.random((N, 128, A, 4))) * top[None, :, None, None] * sign[None, :, None, :]).reshape(N, 128, 4 * A))
    return d
def check_inputs(d):
    b = []
    for k, lo, hi in (("ky", -16, 24), ("x", -16, 24), ("w", -30, 30)):
        v = np.abs(d[k].astype(np.float32))
        if not (np.isfinite(v).all() and ((v == 0) | (v >= 2.0 ** lo) & (v <= 2.0 ** hi)).all()): b.append("a value of " + k)
    for k in ("nx", "st"):
        if d[k].min() < 0 or d[k].max() >= N * M: b.append("an entry of " + k)
    return b
def served(node):
    ok = np.zeros(N * A, bool)
    for s in range(N):
        at = node[A * s:A * s + A] // M
        for d in range(N): ok[A * s + np.flatnonzero(at == d)[:CAPP]] = True
    return np.flatnonzero(ok)
def reference(ky, nx, x, st, w):
    pieces = [mx_ref.quantize(np.ascontiguousarray(cut(ky[d], i))) for d in range(N) for i in range(P // 128)]
    dk = decode(join(*pieces)).reshape(128, N * P, 4)
    leads = np.concatenate([entries(nx[d]) for d in range(N)])
    q = join(*[mx_ref.quantize(np.ascontiguousarray(x[s])) for s in range(N)])
    node = np.concatenate([entries(st[s]) for s in range(N)])
    e = np.arange(N * A)
    way = [node]
    for t in range(R):
        go = served(node)
        z = np.concatenate([mx_ref.matmul(p, q) for p in pieces])
        four = 4 * node[:, None] + np.arange(4)
        k = 4 * node + np.argmax(z[four, e[:, None]] + np.float32(0), axis=1)
        v = decode(q).reshape(128, N * A, 4) * np.float32(0.5) + dk[:, k] * np.float32(0.5)
        new = mx_ref.quantize(np.ascontiguousarray(v.reshape(128, -1).astype(BF)))
        q = put(q, go, pick(new, go))
        node = node.copy()
        node[go] = leads[k[go]]
        way.append(node)
    oc, osc = np.zeros((N, 128, 4 * A), np.uint8), np.zeros((N, 16, A), np.uint8)
    nd, y = np.zeros((N, R + 1, A), np.float32), np.zeros((N, 128, A), np.float32)
    for s in range(N):
        own = pick(q, np.arange(A * s, A * s + A))
        oc[s], osc[s] = emit(own)
        nd[s] = np.stack(way)[:, A * s:A * s + A]
        y[s] = mx_ref.matmul(mx_ref.quantize(np.ascontiguousarray(w[s])), own)
    return {"oc": oc, "osc": osc, "nd": nd, "y": y}

@@ -1,0 +1,529 @@
+from concourse.bass import DstId, RemoteDMATransfer
+from concourse.mybir import dt, AluOpType as A, AxisListType, ActivationFunctionType as F
+
+NR, CAP, HOPS = 4, 32, 3
+BIG = 1e29
+CUTS = (0, 128, 256, 384, 512)
+
+SCRATCH = {
+    "STW": ("sbuf", [128, 4], "int32"), "STU": ("sbuf", [128, 4], "uint16"),
+    "NXD": ("dram", [128, 4], "int32"), "NXR0": ("dram", [128, 4], "int32"), "NXR1": ("dram", [128, 4], "int32"), "NXR2": ("dram", [128, 4], "int32"),
+    "NXW": ("sbuf", [128, 96], "int32"), "NXV": ("sbuf", [128, 32], "int32"), "NXU": ("sbuf", [128, 128], "uint16"), "NXA": ("sbuf", [128, 2048], "float32"),
+    "NODF": ("sbuf", [128, 512], "float32"), "NODI": ("sbuf", [128, 512], "int32"),
+    "JP": ("sbuf", [128, 128], "int32"), "JPA": ("sbuf", [128, 128], "int32"), "ID": ("sbuf", [128, 128], "bfloat16"),
+    "PI": ("sbuf", [128, 8], "int32"), "THR": ("sbuf", [128, 8], "float32"),
+    "KP": ("sbuf", [128, 8], "int32"), "KP2": ("sbuf", [128, 8], "int32"), "M8": ("sbuf", [128, 8], "float32"),
+    "XI": ("sbuf", [128, 8], "int32"), "XF": ("sbuf", [128, 8], "float32"), "XL": ("sbuf", [128, 2], "uint16"),
+    "IO4": ("sbuf", [128, 8], "int32"), "AW": ("sbuf", [128, 4], "float32"), "IDL": ("sbuf", [128, 2], "uint16"),
+    "TB": ("sbuf", [128, 8], "float32"), "IO": ("sbuf", [128, 16], "float32"), "C16": ("sbuf", [128, 16], "float32"),
+    "D16": ("sbuf", [128, 128], "float32"), "D16B": ("sbuf", [128, 256], "bfloat16"), "NM64": ("sbuf", [128, 64], "float32"),
+    "RS64": ("sbuf", [128, 512], "bfloat16"), "RS16": ("sbuf", [128, 128], "float32"), "RS16B": ("sbuf", [128, 256], "bfloat16"),
+    "AL": ("sbuf", [128, 24], "uint16"),
+    "VS": ("sbuf", [128, 24], "int32"),
+    "VL": ("sbuf", [128, 24], "int32"),
+    "Z4": ("sbuf", [128, 24], "uint16"),
+    "OU": ("sbuf", [128, 24], "uint16"),
+    "OR": ("sbuf", [128, 24], "uint16"),
+    "CL": ("sbuf", [128, 24], "uint16"),
+    "SL": ("sbuf", [128, 24], "uint16"),
+    "BT": ("sbuf", [128, 64], "int32"), "VT": ("sbuf", [128, 64], "int32"), "MK": ("sbuf", [128, 256], "bfloat16"), "PX": ("sbuf", [128, 256], "bfloat16"),
+    "CN": ("sbuf", [128, 512], "bfloat16"), "SC": ("sbuf", [128, 512], "bfloat16"), "VD": ("sbuf", [128, 128], "float32"), "VE": ("sbuf", [128, 128], "float32"),
+    "VDB": ("sbuf", [128, 128], "bfloat16"), "VEB": ("sbuf", [128, 128], "bfloat16"),
+    "MD": ("sbuf", [128, 256], "bfloat16"), "UD": ("sbuf", [128, 256], "bfloat16"), "FF": ("sbuf", [128, 256], "bfloat16"),
+    "WW": ("sbuf", [128, 96], "float32"), "ND": ("sbuf", [128, 256], "float32"),
+    "VA": ("sbuf", [128, 8], "float32"), "VR": ("sbuf", [128, 8], "float32"), "VP": ("sbuf", [128, 8], "float32"), "T8": ("sbuf", [128, 8], "float32"),
+    "ZS": ("sbuf", [128, 512], "float32"), "T64": ("sbuf", [128, 64], "float32"),
+    "RM": ("sbuf", [128, 72], "float32"),
+    "XS": ("sbuf", [128, 512], "bfloat16"), "OF": ("sbuf", [128, 8], "float32"), "OG": ("sbuf", [128, 8], "float32"), "HT": ("sbuf", [128, 512], "bfloat16"),
+    "DK": ("sbuf", [128, 2048], "float32"), "DQ": ("sbuf", [128, 256], "float32"), "GK": ("sbuf", [128, 256], "float32"),
+    "XT": ("sbuf", [128, 512], "bfloat16"), "KT": ("sbuf", [128, 2048], "bfloat16"), "WT": ("sbuf", [128, 512], "bfloat16"),
+    "ET": ("sbuf", [128, 2048], "bfloat16"), "ST": ("sbuf", [128, 512], "bfloat16"), "YS": ("sbuf", [128, 64], "float32"),
+    "pv": ("psum", [128, 2048], "float32"), "pz": ("psum", [128, 1536], "float32"), "px": ("psum", [128, 512], "float32"),
+}
+
+
+def _codes(name, n):
+    SCRATCH["c" + name] = ("sbuf", [128, n], "float8_e4m3fn_x4")
+    SCRATCH["s" + name] = ("sbuf", [128, n], "uint8")
+
+
+for _n, _w in (("KQ", 512), ("EQ", 512), ("SQ", 128), ("WQ", 128), ("XQ", 128), ("HQ3", 128), ("KC", 128)):
+    _codes(_n, _w)
+for _t in range(HOPS):
+    for _n, _w in (("SD", 96), ("LA", 128), ("NW", 128), ("RW", 192 if _t else 256)):
+        _codes(_n + str(_t), _w)
+for _t in range(HOPS + 1):
+    SCRATCH["NN%d" % _t] = ("sbuf", [128, 192], "int32")
+SEMAPHORES = ["cv", "cs", "ct", "cg", "ls", "dst", "dx", "dno", "dnx", "dnd", "nxr", "dky", "dw", "dh3", "dout"]
+for _t in range(HOPS):
+    SEMAPHORES += ["aq%d" % _t, "av%d" % _t, "rq%d" % _t, "rc%d" % _t]
+
+
+def rank_program(g, core, T, topo):
+    me = T.rank_of(core)
+    if me is None:
+        return
+    cores = list(T.cores)
+    eng = {"v": g.vector, "s": g.scalar, "t": g.tensor, "g": g, "y": g.sync}
+    count = {}
+    known = {q: {} for q in eng}
+    seen = {}
+
+    def need(q, deps):
+        for d in deps:
+            if d is None:
+                continue
+            sem, val = d
+            if known[q].get(sem, 0) >= val:
+                continue
+            eng[q].wait_ge(T.sem[sem], int(val))
+            known[q][sem] = val
+            for k, w in seen.get(d, {}).items():
+                if known[q].get(k, 0) < w:
+                    known[q][k] = w
+
+    def done(q, ins, sem, n):
+        count[sem] = count.get(sem, 0) + n
+        ins.then_inc(T.sem[sem], n)
+        tok = (sem, count[sem])
+        seen[tok] = dict(known[q])
+        return tok
+
+    v = g.vector
+    getv = {"copy": v.tensor_copy, "tt": v.tensor_tensor, "ts": v.tensor_scalar, "red": v.tensor_reduce, "scan": v.tensor_tensor_scan,
+            "set": v.memset, "q": v.quantize_mx}
+
+    def V(name, deps, *args):
+        need("v", deps)
+        return done("v", getv[name](*args), "cv", 1)
+
+    def S(out, in_, deps, *scale):
+        need("s", deps)
+        return done("s", g.scalar.activation(out, in_, F.Copy, *scale), "cs", 1)
+
+    def MM(out, lc, ls, rc, rs, start, stop, deps):
+        need("t", deps)
+        return done("t", g.tensor.matmul_mx(out, lc, ls, rc, rs, start, stop), "ct", 1)
+
+    def DMA(q, sem, out, in_, deps=()):
+        need(q, deps)
+        return done(q, eng[q].dma_start(out, in_), sem, 16)
+
+    def IOTA(out, pattern, base, cm, f32=False):
+        if f32:
+            return done("g", g.iota(out, pattern, base, cm, allow_small_or_imprecise_dtypes=True), "cg", 1)
+        return done("g", g.iota(out, pattern, base, cm), "cg", 1)
+
+    peers = [(me + 1 + b) % NR for b in range(NR - 1)]
+
+    def part(s, r):
+        others = sorted((o for o in range(NR) if o != s), key=lambda o: (topo.die(cores[o]) != topo.die(cores[s]), (o - s) % NR))
+        e = topo.engines(cores[s], cores[r])
+        q = len(e) // 4
+        return (e[:q], e[q:2 * q], e[2 * q:])[others.index(r)]
+
+    def bits(es):
+        m = 0
+        for i in es:
+            m |= 1 << i
+        return m
+
+    def coreid(r):
+        rid, pid, _ = topo.addr(cores[r])
+        return DstId(rid=rid, pnc=pid)
+
+    LIST = sum(len(part(r, me)) for r in peers)
+    COLS = 15
+
+    def fused(tr):
+        g.remote_dma_fused(tr, local_sem=T.sem.ls)
+
+    def one(r, m, sem, src, dst):
+        return RemoteDMATransfer(dst_ids=[coreid(r)], dma_engine_mask=m, remote_sem=T.sem[sem], src=src, dst=dst)
+
+    def send(sem, t, dst, src, deps):
+        need("g", deps)
+        fused([one(r, bits(part(me, r)), sem + str(t), L(src, t, 2 * b, 2 * b + 2), L(dst, t, 2 * ((me - r - 1) % NR), 2 * ((me - r - 1) % NR) + 2))
+               for b, r in enumerate(peers)])
+        count["ls"] = count.get("ls", 0) + sum(len(part(me, r)) for r in peers)
+
+    def by(x, a, b):
+        return x[:, a:b].bitcast(dt.uint8)
+
+    def sendcols(sem, dst, src, deps):
+        C, P, DC, DP = T["c" + src], T["s" + src], T["c" + dst], T["s" + dst]
+        need("g", deps)
+        tr = []
+        for b, r in enumerate(peers):
+            e = topo.engines(core, cores[r])[5 * b:5 * b + 5]
+            o = 32 * ((me - r - 1) % NR)
+            i = 32 * b
+            for k in range(4):
+                tr.append(one(r, 1 << e[k], sem, by(C, i + 8 * k, i + 8 * k + 8), by(DC, o + 8 * k, o + 8 * k + 8)))
+            tr.append(one(r, 1 << e[4], sem, P[:, i:i + 32], DP[:, o:o + 32]))
+        fused(tr)
+        count["ls"] = count.get("ls", 0) + 15
+
+    def wd(x, a, b):
+        return x[:, a:b].bitcast(dt.uint32)
+
+    def L(name, t, a, b, step=1):
+        return T[name][:, 8 * t + a:8 * t + b:step]
+
+    off = 128 * (NR - 1 - me)
+    K = {}
+
+    for k in range(8):
+        d_st = DMA("y" if k % 2 == 0 else "s", "dst", T.STW[16 * k:16 * k + 16, 0:4], T.st[:, :])
+    d_nd = DMA("s", "dnd", T.NXD[:, :], T.nx[:, :])
+    d_x = DMA("y", "dx", T.XT[:, 0:256], T.x[:, :])
+    d_ky = DMA("s", "dky", T.KT[:, 0:1024], T.ky[:, 0:1024])
+    d_ky = DMA("y", "dky", T.KT[:, 1024:2048], T.ky[:, 1024:2048])
+    for k in range(8):
+        d_no = DMA("y", "dno", T.NXV[16 * k:16 * k + 16, 0:32], T.nx[:, :])
+    d_w = DMA("y", "dw", T.WT[:, :], T.w[:, :])
+
+    i_pi = IOTA(T.PI[:, 0:1], [[0, 1]], 0, 1)
+    i_ni = IOTA(T.NODI[:, :], [[1, 512]], off, 0)
+    i_jp = IOTA(T.JP[:, :], [[1, 128]], 0, -1)
+    i_kp = IOTA(T.KP[:, :], [[-16, 8]], 0, 1)
+    need("g", [d_nd])
+    e16 = topo.engines(core, cores[peers[0]])
+    fused([RemoteDMATransfer(dst_ids=[coreid(r) for r in peers], dma_engine_mask=bits(e16), remote_sem=T.sem.nxr, srcs=[T.NXD[:, :]],
+                             dsts=[T["NXR%d" % ((me - r - 1) % NR)][:, :] for r in peers])])
+    count["ls"] = len(e16)
+
+    m_rs = V("set", [], T.RS64[:, :], 1.0)
+    k_pj = V("ts", [i_pi], T.XI[:, 4:5], T.PI[:, 0:1], 15, None, A.bitwise_and)
+    m_rs = V("set", [m_rs], T.RS64[:, 0:512:64], 0.0)
+    k_t0 = V("ts", [k_pj], T.THR[:, 0:1], T.XI[:, 4:5], 0.0, None, A.add)
+    k_t1 = V("ts", [k_pj], T.THR[:, 1:2], T.XI[:, 4:5], 16.0, None, A.add)
+    k_th = [k_t0, k_t1]
+    x_a = V("ts", [k_pj], T.XI[:, 0:1], T.XI[:, 4:5], 2, None, A.arith_shift_right)
+    x_u = V("ts", [i_pi], T.XI[:, 3:4], T.PI[:, 0:1], 1.0, None, A.add)
+    x_g = V("ts", [i_pi], T.XI[:, 2:3], T.PI[:, 0:1], 4, None, A.arith_shift_right)
+    x_b = V("ts", [x_a], T.XI[:, 1:2], T.XI[:, 0:1], 4.0, None, A.add)
+    x_u = V("ts", [x_u], T.XI[:, 5:6], T.XI[:, 3:4], 3, None, A.bitwise_and)
+    x_g = V("copy", [x_g], T.XF[:, 0:1], T.XI[:, 2:3])
+    x_m = V("set", [], T.RM[:, 0:8], BIG)
+    x_u = V("ts", [x_u], T.XF[:, 1:2], T.XI[:, 5:6], 16.0, 7.0, A.mult, A.add)
+    m_xt = V("set", [], T.XT[:, 256:512], 0.0)
+    m_r16 = V("set", [], T.RS16B[:, :], 1.0)
+    m_r16f = V("set", [], T.RS16[:, :], 1.0)
+    x_e = V("ts", [x_b, x_g, x_u], T.XF[:, 2:4], T.XI[:, 0:2], T.XF[:, 0:1], T.XF[:, 1:2], A.is_equal, A.mult)
+
+    def lists(t, bt, gap):
+        gap(0)
+        mk = []
+        for b in range(4):
+            mk.append(V("ts", [bt], T.MK[:, 64 * b:64 * b + 64], T.BT[:, :], float(b), None, A.is_equal))
+        gap(1)
+        px = [V("scan", [mk[2 * h + 1], m_rs], T.PX[:, 128 * h:128 * h + 128], T.RS64[:, 0:128], T.MK[:, 128 * h:128 * h + 128], 0.0, A.mult, A.add)
+              for h in range(2)]
+        gap(2)
+        cn = [V("ts", [px[1], k_th[h]], T.CN[:, 256 * h:256 * h + 256], T.PX[:, :], T.THR[:, h:h + 1], None, A.is_le) for h in range(2)]
+        gap(3)
+        sc = [V("scan", [cn[h]], T.SC[:, 256 * h:256 * h + 256], T.RS64[:, 0:256], T.CN[:, 256 * h:256 * h + 256], 0.0, A.mult, A.add) for h in range(2)]
+        gap(4)
+        for h in range(2):
+            al = V("ts", [sc[h]], L("AL", t, h, 8, 2), T.SC[:, 256 * h + 63:256 * h + 256:64], 63.0, None, A.min)
+        gap(5)
+        return al
+
+    def diag(t, al):
+        return V("tt", [K["vt"], al, K["d16"]], T.VDB[:, :], T.VT[:, 0:64].indirect(L("AL", t, 0, 8)), T.D16B[:, 0:128], A.mult)
+
+    def run(vd):
+        return V("scan", [vd, K["r16"]], T.VEB[:, :], T.RS16B[:, 0:128], T.VDB[:, :], 0.0, A.mult, A.add)
+
+    def depart(t, al, held):
+        c, s = T["cRW%d" % t], T["sRW%d" % t]
+        p2 = S(T["sSD%d" % t][:, 0:96], s[:, 128:192].indirect(L("AL", t, 0, 6)), [al, held[-1]])
+        p1 = V("copy", [al, held[0]], wd(T["cSD%d" % t], 0, 96), wd(c, 128, 192).indirect(L("AL", t, 0, 6)))
+        sendcols("aq%d" % t, "LA%d" % t, "SD%d" % t, [p1, p2])
+        return S(T["sLA%d" % t][:, 96:128], s[:, 128:192].indirect(L("AL", t, 6, 8)), [al, held[-1]])
+
+    def mine32(t, al, held):
+        return V("copy", [al, held[0]], wd(T["cLA%d" % t], 96, 128), wd(T["cRW%d" % t], 128, 192).indirect(L("AL", t, 6, 8)))
+
+    def tell(t, ve):
+        vs = V("ts", [ve], L("VS", t, 0, 8), T.VEB[:, 15:128:16], 4.0, None, A.mult)
+        send("av", t, "VL", "VS", [vs])
+        return vs
+
+    def eq(b):
+        return T.cEQ[:, 128 * b:128 * b + 128], T.sEQ[:, 128 * b:128 * b + 128]
+
+    def server(t, own, vs, prev, aside, step):
+        KQ, sKQ = T.cKQ, T.sKQ
+        LA, sLA = T["cLA%d" % t], T["sLA%d" % t]
+        land = [("aq%d" % t, COLS)] + own + [K["kq"]]
+        z = []
+
+        def zout(i):
+            n = CUTS[i + 1] - CUTS[i]
+            return T.pz[:, 512 * i:512 * i + n] if i < 3 else T.px[:, 0:n]
+
+        for i in range(4):
+            a, b = CUTS[i], CUTS[i + 1]
+            z.append(MM(zout(i), LA[:, 0:128], sLA[:, 0:128], KQ[:, a:b], sKQ[:, a:b], True, True, land + [prev["z"][i]]))
+
+        def zcopy(i):
+            return T.ZS[:, CUTS[i]:CUTS[i + 1]], zout(i)
+
+        def half(b):
+            return MM(T.pv[:, 512 * b:512 * b + 128], *eq(b), LA[:, 0:128], sLA[:, 0:128], True, t > 0, [K["eq"], prev["pv"][b]])
+
+        dq = [half(b) for b in range(2)]
+        c0 = S(*zcopy(0), [z[0], prev["t64"]])
+        c2 = S(*zcopy(2), [z[2]])
+        if t > 0:
+            d = [S(T.DQ[:, 128 * b:128 * b + 128], T.pv[:, 512 * b:512 * b + 128], [dq[b], prev["ht"]]) for b in range(2)]
+        aside(3)
+        V("tt", [vs, K["m8"]], T.T8[:, 6:8], L("VS", t, 6, 8), T.M8[:, 6:8], A.mult)
+        V("copy", [vs], T.VA[:, 6:8], L("VS", t, 6, 8))
+        b8 = V("tt", [("av%d" % t, LIST)], T.T8[:, 0:6], L("VL", t, 0, 6), T.M8[:, 0:6], A.mult)
+        va = V("copy", [], T.VA[:, 0:6], L("VL", t, 0, 6))
+        vr = V("tt", [i_tb], T.VR[:, 0:6], L("VL", t, 0, 6), T.TB[:, 0:6], A.add) if t > 0 else None
+        vp = V("red", [b8], T.VP[:, 0:1], T.T8[:, :], AxisListType.X, A.add)
+        c1 = V("copy", [z[1]], *zcopy(1))
+        z4 = V("ts", [vp, i_io4], L("Z4", t, 0, 4), T.IO4[:, 0:4], T.VP[:, 0:1], None, A.add)
+        c3 = V("copy", [z[3]], *zcopy(3))
+        t64 = V("tt", [c0, c1, c2, c3, z4, K["nm"]], T.T64[:, :], T.ZS[:, 0:512].indirect(L("Z4", t, 0, 4)), T.NM64[:, :], A.add)
+        step()
+        rm = V("scan", [t64], T.RM[:, 8:72], T.T64[:, :], T.T64[:, :], -BIG, A.max, A.max)
+        step()
+        xs = V("ts", [rm, x_m, K["xs"], K["xl"]], T.XS[:, 0:32], T.RM[:, 0:56].indirect(T.XL[:, 0:2]), T.RM[:, 71:72], None, A.is_lt)
+        step()
+        xq = V("q", [xs, prev["xm"]], T.cXQ[:, 0:128], T.sXQ[:, 0:128], T.XS[:, :])
+        xm = MM(T.px[:, 0:128], T.cSQ[:, 0:128], T.sSQ[:, 0:128], T.cXQ[:, 0:128], T.sXQ[:, 0:128], True, True, [xq, K["sq"], c3])
+        dq += [half(b) for b in range(2, 4)]
+        aside(0)
+        step()
+        step()
+        if t > 0:
+            og = V("tt", [xm, vr], T.OG[:, 0:6], T.px[:, 0:6], T.VR[:, 0:6], A.add)
+            of = V("tt", [xm, va], T.OF[:, :], T.px[:, 0:8], T.VA[:, :], A.add)
+            told = V("copy", [og], L("OR", t, 0, 6), T.OG[:, 0:6])
+            send("rc", t, "CL", "OR", [told])
+        else:
+            of = V("tt", [xm, va], T.OF[:, :], T.px[:, 0:8], T.VA[:, :], A.add)
+        ou = V("copy", [of], L("OU", t, 0, 8), T.OF[:, :])
+        step()
+        if t == 0:
+            ks = S(T.sKC[:, 0:128], sKQ[:, 0:512].indirect(L("OU", t, 0, 8)), [ou, K["kq"]])
+            nd = V("tt", [ou, K["t3"], K["db"]], T.VD[:, :], T.NXA[:, 1536:2048].indirect(L("OU", t, 0, 8)), T.D16[:, :], A.mult)
+            kc = V("copy", [ou], wd(T.cKC, 0, 128), wd(KQ, 0, 512).indirect(L("OU", t, 0, 8)))
+            ne = V("scan", [nd, K["r16f"]], T.VE[:, :], T.RS16[:, :], T.VD[:, :], 0.0, A.mult, A.add)
+            told = V("ts", [ne], L("OR", t, 0, 8), T.VE[:, 15:128:16], float(-off), None, A.add)
+            send("rc", t, "CL", "OR", [told])
+            aside(1)
+            h = []
+            for b in range(4):
+                km = MM(T.pv[:, 512 * b:512 * b + 128], *eq(b), T.cKC[:, 0:128], T.sKC[:, 0:128], False, True, [kc, ks])
+                o, i = T.HT[:, b:512:4], T.pv[:, 512 * b:512 * b + 128]
+                h.append(S(o, i, [km]) if b % 2 == 0 else V("copy", [km], o, i))
+            ready = h
+            ht = None
+        else:
+            def chosen(b):
+                return T.DK[:, 512 * b:512 * b + 512].indirect(L("OU", t, 0, 8))
+
+            gk = [S(T.GK[:, 128 * b:128 * b + 128], chosen(2 + b), [ou, prev["ht"]] + K["dk"]) for b in range(2)]
+            aside(1)
+            for b in range(2):
+                V("tt", [ou, d[b], prev["nq"]] + K["dk"], T.HT[:, b:512:4], chosen(b), T.DQ[:, 128 * b:128 * b + 128], A.add)
+            ready = [V("tt", [dq[2 + b], gk[b]], T.HT[:, 2 + b:512:4], T.pv[:, 512 * (2 + b):512 * (2 + b) + 128], T.GK[:, 128 * b:128 * b + 128], A.add)
+                     for b in range(2)]
+            h = d + ready
+            ht = ready[1]
+        step()
+        C, P = T["cNW%d" % t], T["sNW%d" % t]
+        nq = V("q", ready, C[:, 0:128], P[:, 0:128], T.HT[:, :])
+        sendcols("rq%d" % t, "RW%d" % t, "NW%d" % t, [nq])
+        prev.update({"z": [c0, c1, c2, of], "pv": h, "t64": t64, "ht": ht, "xm": xm, "of": of, "nq": nq})
+        w1 = V("copy", [nq, K["idl"]], wd(T["cRW%d" % t], 96, 128), wd(C, 96, 128).indirect(T.IDL[:, 0:2]))
+        w2 = S(T["sRW%d" % t][:, 96:128], P[:, 96:128].indirect(T.IDL[:, 0:2]), [nq, K["idl"]])
+        aside(2)
+        return [w1, w2], ou, told
+
+    def where(t):
+        md = V("scan", [K["db"]], T.MD[:, :], T.MK[:, :], T.D16B[:, :], 0.0, A.max, A.mult)
+        yield None
+        ud = V("scan", [md], T.UD[:, :], T.PX[:, :], T.MD[:, :], 0.0, A.max, A.mult)
+        yield None
+        ff = V("scan", [ud, K["r16"]], T.FF[:, :], T.RS16B[:, :], T.UD[:, :], 0.0, A.mult, A.add)
+        yield None
+        w = T.FF[:, 15:256:16]
+        w1 = V("ts", [ff], T.WW[:, 0:16], w, float(CAP), None, A.is_le)
+        w2 = V("ts", [ff], T.WW[:, 16:32], w, 0.0, None, A.is_gt)
+        w3 = V("tt", [ff, K["c16"]], T.WW[:, 32:48], w, T.C16[:, :], A.add)
+        yield None
+        w4 = V("tt", [w1, w2], T.WW[:, 48:64], T.WW[:, 0:16], T.WW[:, 16:32], A.mult)
+        yield None
+        w5 = V("tt", [w4, w3], T.WW[:, 64:80], T.WW[:, 48:64], T.WW[:, 32:48], A.mult)
+        yield None
+        w6 = V("tt", [w5], T.WW[:, 80:88], T.WW[:, 64:72], T.WW[:, 72:80], A.add)
+        yield None
+        w7 = V("tt", [w6], T.WW[:, 88:92], T.WW[:, 80:84], T.WW[:, 84:88], A.add)
+        yield None
+        w8 = V("tt", [w7, K["aw"]], T.WW[:, 92:96], T.WW[:, 88:92], T.AW[:, :], A.add)
+        yield None
+        K["sl"] = V("copy", [w8], L("SL", t, 0, 4), T.WW[:, 92:96])
+        while True:
+            yield None
+
+    def order(t, held, back, deps, c, s, o):
+        h2 = S(s[:, o:o + 64], T["sRW%d" % t][:, 0:192].indirect(L("SL", t, 0, 4)), [held[-1], back[1]] + deps)
+        h1 = V("copy", [held[0], back[0]] + deps, wd(c, o, o + 64), wd(T["cRW%d" % t], 0, 192).indirect(L("SL", t, 0, 4)))
+        return [h1, h2]
+
+    def table(b):
+        return S(T.NXA[:, 512 * b:512 * b + 512], T.NODF[:, 0:512].indirect(T.NXU[:, 32 * b:32 * b + 32]), [K["no"] if b == 3 else K["nu"], K["nf"]])
+
+    def dkc(b):
+        K["dk"].append(S(T.DK[:, 512 * b:512 * b + 512], T.pv[:, 512 * b:512 * b + 512], [K["um"][b]]))
+
+    for b in range(4):
+        m_e = S(T.ET[:, 512 * b:512 * b + 512], T.RS64[:, :], [m_rs], 0.0, 0.0)
+
+    k_st = V("copy", [d_st], T.STU[:, :], T.STW[:, :])
+    start = T.NODI[:, 0:512].indirect(T.STU[:, 0:4])
+    bt = V("ts", [k_st, i_ni], T.BT[:, :], start, 7, 3, A.logical_shift_right, A.bitwise_and)
+
+    def gap0(k):
+        if k == 0:
+            K["node"] = V("copy", [], T.NN0[:, 128:192], start)
+        if k == 1:
+            K["r16"] = V("set", [m_r16], T.RS16B[:, 0:256:16], 0.0)
+            K["jpa"] = V("ts", [i_jp], T.JPA[:, :], T.JP[:, :], 15, None, A.bitwise_and)
+        if k == 2:
+            K["r16f"] = V("set", [m_r16f], T.RS16[:, 0:128:16], 0.0)
+            K["vt"] = V("ts", [K["node"]], T.VT[:, :], T.NN0[:, 128:192], 127, None, A.bitwise_and)
+        if k == 3:
+            K["held"] = [V("q", [d_x, m_xt], T.cRW0[:, 128:256], T.sRW0[:, 128:256], T.XT[:, :])]
+        if k == 4:
+            K["d16"] = V("ts", [K["jpa"]], T.D16B[:, 0:128], T.JPA[:, :], 0.0, None, A.is_equal)
+        if k == 5:
+            K["xl"] = V("copy", [x_e], T.XL[:, 0:2], T.XF[:, 2:4])
+            K["id"] = V("ts", [i_jp], T.ID[:, :], T.JP[:, :], 0.0, 0.5, A.is_equal, A.mult)
+
+    al = lists(0, bt, gap0)
+    held, node = K["held"], K["node"]
+    hq0 = held[0]
+    o2 = depart(0, al, held)
+    vd = diag(0, al)
+    o1 = mine32(0, al, held)
+    vs = tell(0, run(vd))
+    own = [o1, o2]
+    i_io4 = IOTA(T.IO4[:, 0:4], [[1, 4]], 0, 0)
+    i_16 = IOTA(T.IO[:, :], [[32, 4], [-16, 4]], -129, 0, True)
+    i_k16 = IOTA(T.IO4[:, 4:8], [[16, 4]], 0, 0)
+    i_tb = IOTA(T.TB[:, 0:6], [[-512, 3], [0, 2]], 1024, 0, True)
+    K["xs"] = IOTA(T.XS[:, :], [[0, 512]], 0, 0, True)
+    K["nf"] = IOTA(T.NODF[:, :], [[1, 512]], off, 0, True)
+    S(T.D16[:, :], T.D16B[:, 0:128], [K["d16"]])
+    K["db"] = S(T.D16B[:, 128:256], T.D16B[:, 0:128], [K["d16"]])
+    for b in range(4):
+        k_e = S(T.ET[:, 512 * b + b:512 * b + 512:4], T.ID[:, :], [m_e, K["id"]])
+    for b in range(4):
+        k_s = S(T.ST[:, b:512:4], T.D16B[:, 0:128], [K["d16"]])
+    K["kq"] = V("q", [d_ky], T.cKQ[:, 0:512], T.sKQ[:, 0:512], T.KT[:, :])
+    find = where(0)
+    next(find)
+    k_kp = V("ts", [i_kp], T.KP2[:, :], T.KP[:, :], 4, None, A.arith_shift_right)
+    K["nm"] = V("ts", [K["d16"]], T.NM64[:, :], T.D16B[:, 0:64], -1.0, BIG, A.add, A.mult)
+    next(find)
+    K["m8"] = V("ts", [k_kp], T.M8[:, :], T.KP2[:, :], 0.0, None, A.is_equal)
+    K["c16"] = V("ts", [i_16, k_t0], T.C16[:, :], T.IO[:, :], T.THR[:, 0:1], None, A.subtract)
+    next(find)
+    K["no"] = V("copy", [d_no], T.NXU[:, 96:128], T.NXV[:, :])
+    K["eq"] = V("q", [k_e], T.cEQ[:, 0:512], T.sEQ[:, 0:512], T.ET[:, :])
+    K["sq"] = V("q", [k_s], T.cSQ[:, 0:128], T.sSQ[:, 0:128], T.ST[:, :])
+    for b in range(3):
+        for k in range(8):
+            d_nx = DMA("y", "dnx", T.NXW[16 * k:16 * k + 16, 32 * b:32 * b + 32], T["NXR%d" % b][:, :], [("nxr", 3 * len(e16))])
+    DMA("y", "dh3", by(T.cHQ3, 64, 128), by(T.cRW0, 192, 256), [hq0])
+    d_h3 = DMA("y", "dh3", T.sHQ3[:, 64:128], T.sRW0[:, 192:256], [hq0])
+
+    def aside0(k):
+        if k == 3:
+            K["t3"] = table(3)
+        if k == 0:
+            K["idl"] = V("ts", [k_t0, i_k16], T.IDL[:, :], T.IO4[:, 4:6], T.THR[:, 0:1], None, A.add)
+            K["aw"] = V("ts", [k_t0, i_k16], T.AW[:, :], T.IO4[:, 4:8], T.THR[:, 0:1], 128.0, A.add, A.add)
+        if k == 2:
+            K["nu"] = V("copy", [d_nx], T.NXU[:, 0:96], T.NXW[:, :])
+            K["dk"] = []
+            K["um"] = [MM(T.pv[:, 512 * b:512 * b + 512], *eq(b), T.cKQ[:, 0:512], T.sKQ[:, 0:512], True, True, [prev["pv"][b]]) for b in range(4)]
+            for b in range(2):
+                dkc(b)
+            K["nxa"] = [K["t3"], table(0)]
+
+    def aside1(k):
+        if k == 3:
+            K["nxa"].append(table(2))
+        if k == 2:
+            K["wq"] = V("q", [d_w], T.cWQ[:, 0:128], T.sWQ[:, 0:128], T.WT[:, :])
+
+    prev = {"z": [None] * 4, "pv": [None] * 4, "t64": None, "ht": None, "xm": None, "of": None, "nq": None}
+    for t in range(HOPS):
+        n = T["NN%d" % t]
+        if t == 0:
+            back, ou, told = server(0, own, vs, prev, aside0, lambda: next(find))
+            mine, theirs, tabs = T.NODI[:, 0:512].indirect(L("OR", 0, 6, 8)), T.NODI[:, 0:512].indirect(L("CL", 0, 0, 6)), [told]
+        else:
+            find = where(t)
+            next(find)
+            if t == 1:
+                dkc(2)
+                K["dk"].append(V("copy", [K["um"][3]], T.DK[:, 1536:2048], T.pv[:, 1536:2048]))
+                prev["pv"] = K["dk"]
+                K["nxa"].append(table(1))
+            next(find)
+            next(find)
+            back, ou, told = server(t, own, vs, prev, aside1 if t == 1 else lambda k: None, lambda: next(find))
+            mine, theirs, tabs = T.NXA[:, 1536:2048].indirect(L("OU", t, 6, 8)), T.NXA[:, 0:1536].indirect(L("CL", t, 0, 6)), [ou] + K["nxa"]
+        sl = K["sl"]
+        V("copy", tabs, n[:, 96:128], mine)
+        V("ts", [node], T.ND[:, 64 * t:64 * t + 64], n[:, 128:192], float(-off), None, A.add)
+        g1 = V("copy", [("rc%d" % t, LIST)], n[:, 0:96], theirs)
+        byq = n[:, 0:192].indirect(L("SL", t, 0, 4))
+        got = [sl, ("rq%d" % t, COLS)]
+
+        def nodes():
+            return V("copy", [g1, sl, node], T["NN%d" % (t + 1)][:, 128:192], byq)
+
+        if t + 1 == HOPS:
+            node = nodes()
+            nd = V("ts", [node], T.ND[:, 64 * HOPS:64 * HOPS + 64], T["NN%d" % HOPS][:, 128:192], float(-off), None, A.add)
+            DMA("y", "dout", T.nd[:, :], T.ND[0:1, 0:256], [nd])
+            hq = order(t, held, back, got, T.cHQ3, T.sHQ3, 0)
+            break
+        bt = V("ts", [g1, sl, node], T.BT[:, :], byq, 7, 3, A.logical_shift_right, A.bitwise_and)
+
+        def gap(k):
+            if k == 0:
+                K["node"] = nodes()
+            if k == 2:
+                K["vt"] = V("ts", [K["node"]], T.VT[:, :], T["NN%d" % (t + 1)][:, 128:192], 127, None, A.bitwise_and)
+            if k == 5:
+                K["held"] = order(t, held, back, got, T["cRW%d" % (t + 1)], T["sRW%d" % (t + 1)], 128)
+
+        al = lists(t + 1, bt, gap)
+        held, node = K["held"], K["node"]
+        o2 = depart(t + 1, al, held)
+        vd = diag(t + 1, al)
+        ve = run(vd)
+        o1 = mine32(t + 1, al, held)
+        vs = tell(t + 1, ve)
+        own = [o1, o2]
+
+    DMA("y", "dout", T.oc[:, :], by(T.cHQ3, 0, 64), [hq[0]])
+    for k in range(4):
+        DMA("s" if k < 2 else "y", "dout", T.osc[4 * k:4 * k + 4, 0:64], T.sHQ3[32 * k:32 * k + 4, 0:64], [hq[1]])
+    ym = MM(T.px[:, 0:128], T.cWQ[:, 0:128], T.sWQ[:, 0:128], T.cHQ3[:, 0:128], T.sHQ3[:, 0:128], True, True, hq + [K["wq"], d_h3, prev["of"]])
+    yc = V("copy", [ym], T.YS[:, :], T.px[:, 0:64])
+    DMA("y", "dout", T.y[:, :], T.YS[:, :], [yc])
+    for sem in ("dout", "ls", "cv", "cs", "ct", "cg", "dst", "dx", "dky", "dnx", "dno", "dnd", "dw", "dh3"):
+        need("g", [(sem, count[sem])])

@@ -4,40 +4,39 @@ from concourse.mybir import dt, AluOpType as A, AxisListType, ActivationFunction
 NR, CAP, HOPS = 4, 32, 3
 BIG = 1e29
 CUTS = (0, 128, 256, 384, 512)
+HELD = 224
+EW = 514
 
 SCRATCH = {
     "STW": ("sbuf", [128, 4], "int32"), "STU": ("sbuf", [128, 4], "uint16"),
     "NXD": ("dram", [128, 4], "int32"), "NXR0": ("dram", [128, 4], "int32"), "NXR1": ("dram", [128, 4], "int32"), "NXR2": ("dram", [128, 4], "int32"),
     "NXW": ("sbuf", [128, 96], "int32"), "NXV": ("sbuf", [128, 32], "int32"), "NXU": ("sbuf", [128, 128], "uint16"), "NXA": ("sbuf", [128, 2048], "float32"),
     "NODF": ("sbuf", [128, 512], "float32"), "NODI": ("sbuf", [128, 512], "int32"),
-    "JP": ("sbuf", [128, 128], "int32"), "JPA": ("sbuf", [128, 128], "int32"), "ID": ("sbuf", [128, 128], "bfloat16"),
-    "PI": ("sbuf", [128, 8], "int32"), "THR": ("sbuf", [128, 8], "float32"),
-    "KP": ("sbuf", [128, 8], "int32"), "KP2": ("sbuf", [128, 8], "int32"), "M8": ("sbuf", [128, 8], "float32"),
+    "R16": ("sbuf", [128, 256], "bfloat16"), "ID": ("sbuf", [128, 128], "bfloat16"),
+    "PI": ("sbuf", [128, 8], "int32"), "THR": ("sbuf", [128, 8], "float32"), "M8": ("sbuf", [128, 8], "bfloat16"),
     "XI": ("sbuf", [128, 8], "int32"), "XF": ("sbuf", [128, 8], "float32"), "XL": ("sbuf", [128, 2], "uint16"),
-    "IO4": ("sbuf", [128, 8], "int32"), "AW": ("sbuf", [128, 4], "float32"), "IDL": ("sbuf", [128, 2], "uint16"),
-    "TB": ("sbuf", [128, 8], "float32"), "IO": ("sbuf", [128, 16], "float32"), "C16": ("sbuf", [128, 16], "float32"),
-    "D16": ("sbuf", [128, 128], "float32"), "D16B": ("sbuf", [128, 256], "bfloat16"), "NM64": ("sbuf", [128, 64], "float32"),
-    "RS64": ("sbuf", [128, 512], "bfloat16"), "RS16": ("sbuf", [128, 128], "float32"), "RS16B": ("sbuf", [128, 256], "bfloat16"),
-    "AL": ("sbuf", [128, 24], "uint16"),
-    "VS": ("sbuf", [128, 24], "int32"),
-    "VL": ("sbuf", [128, 24], "int32"),
-    "Z4": ("sbuf", [128, 24], "uint16"),
-    "OU": ("sbuf", [128, 24], "uint16"),
-    "OR": ("sbuf", [128, 24], "uint16"),
-    "CL": ("sbuf", [128, 24], "uint16"),
-    "SL": ("sbuf", [128, 24], "uint16"),
+    "IO4": ("sbuf", [128, 8], "int32"), "AW": ("sbuf", [128, 4], "float32"),
+    "IO": ("sbuf", [128, 24], "float32"), "C16": ("sbuf", [128, 16], "float32"),
+    "D16B": ("sbuf", [128, 256], "bfloat16"), "NM64": ("sbuf", [128, 64], "float32"),
+    "RS64": ("sbuf", [128, 576], "bfloat16"), "RS16B": ("sbuf", [128, 256], "bfloat16"),
+    "AL": ("sbuf", [128, 48], "uint16"),
+    "VL": ("sbuf", [128, 48], "float32"),
+    "Z4": ("sbuf", [128, 48], "uint16"),
+    "OU": ("sbuf", [128, 48], "uint16"),
+    "OR": ("sbuf", [128, 48], "uint16"),
+    "SL": ("sbuf", [128, 48], "uint16"),
     "BT": ("sbuf", [128, 64], "int32"), "VT": ("sbuf", [128, 64], "int32"), "MK": ("sbuf", [128, 256], "bfloat16"), "PX": ("sbuf", [128, 256], "bfloat16"),
     "CN": ("sbuf", [128, 512], "bfloat16"), "SC": ("sbuf", [128, 512], "bfloat16"), "VD": ("sbuf", [128, 128], "float32"), "VE": ("sbuf", [128, 128], "float32"),
     "VDB": ("sbuf", [128, 128], "bfloat16"), "VEB": ("sbuf", [128, 128], "bfloat16"),
     "MD": ("sbuf", [128, 256], "bfloat16"), "UD": ("sbuf", [128, 256], "bfloat16"), "FF": ("sbuf", [128, 256], "bfloat16"),
     "WW": ("sbuf", [128, 96], "float32"), "ND": ("sbuf", [128, 256], "float32"),
-    "VA": ("sbuf", [128, 8], "float32"), "VR": ("sbuf", [128, 8], "float32"), "VP": ("sbuf", [128, 8], "float32"), "T8": ("sbuf", [128, 8], "float32"),
+    "VP": ("sbuf", [128, 8], "float32"), "T8": ("sbuf", [128, 8], "float32"),
     "ZS": ("sbuf", [128, 512], "float32"), "T64": ("sbuf", [128, 64], "float32"),
     "RM": ("sbuf", [128, 72], "float32"),
-    "XS": ("sbuf", [128, 512], "bfloat16"), "OF": ("sbuf", [128, 8], "float32"), "OG": ("sbuf", [128, 8], "float32"), "HT": ("sbuf", [128, 512], "bfloat16"),
+    "XS": ("sbuf", [128, 512], "bfloat16"), "OF": ("sbuf", [128, 8], "float32"), "HT": ("sbuf", [128, 512], "bfloat16"),
     "DK": ("sbuf", [128, 2048], "float32"), "DQ": ("sbuf", [128, 256], "float32"), "GK": ("sbuf", [128, 256], "float32"),
     "XT": ("sbuf", [128, 512], "bfloat16"), "KT": ("sbuf", [128, 2048], "bfloat16"), "WT": ("sbuf", [128, 512], "bfloat16"),
-    "ET": ("sbuf", [128, 2048], "bfloat16"), "ST": ("sbuf", [128, 512], "bfloat16"), "YS": ("sbuf", [128, 64], "float32"),
+    "ET": ("sbuf", [128, 2 * EW], "bfloat16"), "ST": ("sbuf", [128, 512], "bfloat16"), "YS": ("sbuf", [128, 64], "float32"),
     "pv": ("psum", [128, 2048], "float32"), "pz": ("psum", [128, 1536], "float32"), "px": ("psum", [128, 512], "float32"),
 }
 
@@ -50,9 +49,8 @@ def _codes(name, n):
 for _n, _w in (("KQ", 512), ("EQ", 512), ("SQ", 128), ("WQ", 128), ("XQ", 128), ("HQ3", 128), ("KC", 128)):
     _codes(_n, _w)
 for _t in range(HOPS):
-    for _n, _w in (("SD", 96), ("LA", 128), ("NW", 128), ("RW", 192 if _t else 256)):
+    for _n, _w in (("LA", 224), ("RW", 288 if _t else 352)):
         _codes(_n + str(_t), _w)
-for _t in range(HOPS + 1):
     SCRATCH["NN%d" % _t] = ("sbuf", [128, 192], "int32")
 SEMAPHORES = ["cv", "cs", "ct", "cg", "ls", "dst", "dx", "dno", "dnx", "dnd", "nxr", "dky", "dw", "dh3", "dout"]
 for _t in range(HOPS):
@@ -97,9 +95,9 @@ def rank_program(g, core, T, topo):
         need("v", deps)
         return done("v", getv[name](*args), "cv", 1)
 
-    def S(out, in_, deps, *scale):
+    def S(out, in_, deps, *scale, f=F.Copy):
         need("s", deps)
-        return done("s", g.scalar.activation(out, in_, F.Copy, *scale), "cs", 1)
+        return done("s", g.scalar.activation(out, in_, f, *scale), "cs", 1)
 
     def MM(out, lc, ls, rc, rs, start, stop, deps):
         need("t", deps)
@@ -114,6 +112,10 @@ def rank_program(g, core, T, topo):
             return done("g", g.iota(out, pattern, base, cm, allow_small_or_imprecise_dtypes=True), "cg", 1)
         return done("g", g.iota(out, pattern, base, cm), "cg", 1)
 
+    def SEL(out, in_, pattern, op, base, cm, deps):
+        need("g", deps)
+        return done("g", g.affine_select(out, in_, pattern, op, 0.0, base, cm), "cg", 1)
+
     peers = [(me + 1 + b) % NR for b in range(NR - 1)]
 
     def part(s, r):
@@ -121,6 +123,13 @@ def rank_program(g, core, T, topo):
         e = topo.engines(cores[s], cores[r])
         q = len(e) // 4
         return (e[:q], e[q:2 * q], e[2 * q:])[others.index(r)]
+
+    def lanes(s, r):
+        others = sorted((o for o in range(NR) if o != s), key=lambda o: (topo.die(cores[o]) == topo.die(cores[s]), (o - s) % NR))
+        e = topo.engines(cores[s], cores[r])
+        q = len(e) // 4
+        ev, od = e[0::2], e[1::2]
+        return ((ev[:q], od[q:]), (ev[q:], od[:q]), (od[:q], ev[:q]))[others.index(r)]
 
     def bits(es):
         m = 0
@@ -133,7 +142,7 @@ def rank_program(g, core, T, topo):
         return DstId(rid=rid, pnc=pid)
 
     LIST = sum(len(part(r, me)) for r in peers)
-    COLS = 15
+    COLS = sum(len(lanes(r, me)[0]) + len(lanes(r, me)[1]) for r in peers)
 
     def fused(tr):
         g.remote_dma_fused(tr, local_sem=T.sem.ls)
@@ -141,36 +150,34 @@ def rank_program(g, core, T, topo):
     def one(r, m, sem, src, dst):
         return RemoteDMATransfer(dst_ids=[coreid(r)], dma_engine_mask=m, remote_sem=T.sem[sem], src=src, dst=dst)
 
-    def send(sem, t, dst, src, deps):
+    def there(r):
+        return (me - r - 1) % NR
+
+    def send(sem, t, name, src, dst, deps):
         need("g", deps)
-        fused([one(r, bits(part(me, r)), sem + str(t), L(src, t, 2 * b, 2 * b + 2), L(dst, t, 2 * ((me - r - 1) % NR), 2 * ((me - r - 1) % NR) + 2))
+        fused([one(r, bits(part(me, r)), sem + str(t), L(name, t, src + 2 * b, src + 2 * b + 2), L(name, t, dst + 2 * there(r), dst + 2 * there(r) + 2))
                for b, r in enumerate(peers)])
         count["ls"] = count.get("ls", 0) + sum(len(part(me, r)) for r in peers)
 
     def by(x, a, b):
         return x[:, a:b].bitcast(dt.uint8)
 
-    def sendcols(sem, dst, src, deps):
-        C, P, DC, DP = T["c" + src], T["s" + src], T["c" + dst], T["s" + dst]
-        need("g", deps)
-        tr = []
-        for b, r in enumerate(peers):
-            e = topo.engines(core, cores[r])[5 * b:5 * b + 5]
-            o = 32 * ((me - r - 1) % NR)
-            i = 32 * b
-            for k in range(4):
-                tr.append(one(r, 1 << e[k], sem, by(C, i + 8 * k, i + 8 * k + 8), by(DC, o + 8 * k, o + 8 * k + 8)))
-            tr.append(one(r, 1 << e[4], sem, P[:, i:i + 32], DP[:, o:o + 32]))
-        fused(tr)
-        count["ls"] = count.get("ls", 0) + 15
+    def sendcols(sem, name, src, dst, codes, scales):
+        C, P = T["c" + name], T["s" + name]
+        need("g", [codes])
+        fused([one(r, bits(lanes(me, r)[0]), sem, by(C, src + 32 * b, src + 32 * b + 32), by(C, dst + 32 * there(r), dst + 32 * there(r) + 32))
+               for b, r in enumerate(peers)])
+        need("g", [scales])
+        fused([one(r, bits(lanes(me, r)[1]), sem, P[:, src + 32 * b:src + 32 * b + 32], P[:, dst + 32 * there(r):dst + 32 * there(r) + 32])
+               for b, r in enumerate(peers)])
+        count["ls"] = count.get("ls", 0) + sum(len(lanes(me, r)[0]) + len(lanes(me, r)[1]) for r in peers)
 
     def wd(x, a, b):
         return x[:, a:b].bitcast(dt.uint32)
 
     def L(name, t, a, b, step=1):
-        return T[name][:, 8 * t + a:8 * t + b:step]
+        return T[name][:, 16 * t + a:16 * t + b:step]
 
-    off = 128 * (NR - 1 - me)
     K = {}
 
     for k in range(8):
@@ -183,45 +190,45 @@ def rank_program(g, core, T, topo):
         d_no = DMA("y", "dno", T.NXV[16 * k:16 * k + 16, 0:32], T.nx[:, :])
     d_w = DMA("y", "dw", T.WT[:, :], T.w[:, :])
 
-    i_pi = IOTA(T.PI[:, 0:1], [[0, 1]], 0, 1)
-    i_ni = IOTA(T.NODI[:, :], [[1, 512]], off, 0)
-    i_jp = IOTA(T.JP[:, :], [[1, 128]], 0, -1)
-    i_kp = IOTA(T.KP[:, :], [[-16, 8]], 0, 1)
+    IOTA(T.PI[:, 0:1], [[0, 1]], 4, 4)
+    i_pi = IOTA(T.PI[:, 1:3], [[-64, 2]], 0, 1)
+    i_ni = IOTA(T.NODI[:, :], [[1, 512]], 0, 0)
+    i_r16 = IOTA(T.R16[:, :], [[0, 16], [1, 16]], 0, 0, True)
     need("g", [d_nd])
     e16 = topo.engines(core, cores[peers[0]])
     fused([RemoteDMATransfer(dst_ids=[coreid(r) for r in peers], dma_engine_mask=bits(e16), remote_sem=T.sem.nxr, srcs=[T.NXD[:, :]],
-                             dsts=[T["NXR%d" % ((me - r - 1) % NR)][:, :] for r in peers])])
+                             dsts=[T["NXR%d" % there(r)][:, :] for r in peers])])
     count["ls"] = len(e16)
 
-    m_rs = V("set", [], T.RS64[:, :], 1.0)
-    k_pj = V("ts", [i_pi], T.XI[:, 4:5], T.PI[:, 0:1], 15, None, A.bitwise_and)
-    m_rs = V("set", [m_rs], T.RS64[:, 0:512:64], 0.0)
+    m_rs = V("set", [], T.RS64[:, 0:EW], 1.0)
+    k_pj = V("ts", [i_pi], T.XI[:, 4:5], T.PI[:, 1:2], 15, None, A.bitwise_and)
+    m_rs = V("set", [m_rs], T.RS64[:, 0:256:64], 0.0)
     k_t0 = V("ts", [k_pj], T.THR[:, 0:1], T.XI[:, 4:5], 0.0, None, A.add)
-    k_t1 = V("ts", [k_pj], T.THR[:, 1:2], T.XI[:, 4:5], 16.0, None, A.add)
-    k_th = [k_t0, k_t1]
-    x_a = V("ts", [k_pj], T.XI[:, 0:1], T.XI[:, 4:5], 2, None, A.arith_shift_right)
-    x_u = V("ts", [i_pi], T.XI[:, 3:4], T.PI[:, 0:1], 1.0, None, A.add)
-    x_g = V("ts", [i_pi], T.XI[:, 2:3], T.PI[:, 0:1], 4, None, A.arith_shift_right)
-    x_b = V("ts", [x_a], T.XI[:, 1:2], T.XI[:, 0:1], 4.0, None, A.add)
-    x_u = V("ts", [x_u], T.XI[:, 5:6], T.XI[:, 3:4], 3, None, A.bitwise_and)
-    x_g = V("copy", [x_g], T.XF[:, 0:1], T.XI[:, 2:3])
-    x_m = V("set", [], T.RM[:, 0:8], BIG)
-    x_u = V("ts", [x_u], T.XF[:, 1:2], T.XI[:, 5:6], 16.0, 7.0, A.mult, A.add)
-    m_xt = V("set", [], T.XT[:, 256:512], 0.0)
-    m_r16 = V("set", [], T.RS16B[:, :], 1.0)
-    m_r16f = V("set", [], T.RS16[:, :], 1.0)
-    x_e = V("ts", [x_b, x_g, x_u], T.XF[:, 2:4], T.XI[:, 0:2], T.XF[:, 0:1], T.XF[:, 1:2], A.is_equal, A.mult)
+    x_g = V("ts", [i_pi], T.XI[:, 0:2], T.PI[:, 1:3], 0xFFF0, None, A.bitwise_and)
+    x_u = V("ts", [i_pi], T.XI[:, 2:4], T.PI[:, 0:2], 12, None, A.bitwise_and)
+    K["xm"] = V("set", [], T.RM[:, 0:1], BIG)
+    x_u = V("ts", [x_u], T.XF[:, 0:2], T.XI[:, 2:4], 4.0, None, A.mult)
+    k_id = SEL(T.ID[:, :], T.RS64[:, 256:384], [[-1, 128]], A.is_equal, 0, 1, [m_rs])
+    k_m = SEL(T.M8[:, :], T.RS64[:, 256:264], [[-16, 8]], A.is_ge, 0, 1, [m_rs])
+    i_io4 = IOTA(T.IO4[:, 0:4], [[1, 4]], 0, 0)
+    K["m8"] = SEL(T.M8[:, :], T.M8[:, :], [[16, 8]], A.is_ge, 15, -1, [k_m])
+
+    m_xt = S(T.XT[:, 256:512], T.RS64[:, 0:256], [m_rs], 0.0, 0.0)
+    for h in range(2):
+        m_e = S(T.ET[:, EW * h:EW * h + EW], T.RS64[:, 0:EW], [m_rs], 0.0, 0.0)
+    K["r16"] = S(T.RS16B[:, :], T.R16[:, :], [i_r16], f=F.Sign)
 
     def lists(t, bt, gap):
         gap(0)
         mk = []
-        for b in range(4):
-            mk.append(V("ts", [bt], T.MK[:, 64 * b:64 * b + 64], T.BT[:, :], float(b), None, A.is_equal))
+        for i in range(4):
+            mk.append(V("ts", [bt], T.MK[:, 64 * i:64 * i + 64], T.BT[:, :], float((me + i) % NR), None, A.is_equal))
         gap(1)
         px = [V("scan", [mk[2 * h + 1], m_rs], T.PX[:, 128 * h:128 * h + 128], T.RS64[:, 0:128], T.MK[:, 128 * h:128 * h + 128], 0.0, A.mult, A.add)
               for h in range(2)]
         gap(2)
-        cn = [V("ts", [px[1], k_th[h]], T.CN[:, 256 * h:256 * h + 256], T.PX[:, :], T.THR[:, h:h + 1], None, A.is_le) for h in range(2)]
+        cn = [V("ts", [px[1], k_t0], T.CN[:, 0:256], T.PX[:, :], T.THR[:, 0:1], None, A.is_le),
+              V("ts", [px[1], k_t0], T.CN[:, 256:512], T.PX[:, :], -16.0, T.THR[:, 0:1], A.add, A.is_le)]
         gap(3)
         sc = [V("scan", [cn[h]], T.SC[:, 256 * h:256 * h + 256], T.RS64[:, 0:256], T.CN[:, 256 * h:256 * h + 256], 0.0, A.mult, A.add) for h in range(2)]
         gap(4)
@@ -238,17 +245,14 @@ def rank_program(g, core, T, topo):
 
     def depart(t, al, held):
         c, s = T["cRW%d" % t], T["sRW%d" % t]
-        p2 = S(T["sSD%d" % t][:, 0:96], s[:, 128:192].indirect(L("AL", t, 0, 6)), [al, held[-1]])
-        p1 = V("copy", [al, held[0]], wd(T["cSD%d" % t], 0, 96), wd(c, 128, 192).indirect(L("AL", t, 0, 6)))
-        sendcols("aq%d" % t, "LA%d" % t, "SD%d" % t, [p1, p2])
-        return S(T["sLA%d" % t][:, 96:128], s[:, 128:192].indirect(L("AL", t, 6, 8)), [al, held[-1]])
-
-    def mine32(t, al, held):
-        return V("copy", [al, held[0]], wd(T["cLA%d" % t], 96, 128), wd(T["cRW%d" % t], 128, 192).indirect(L("AL", t, 6, 8)))
+        p2 = S(T["sLA%d" % t][:, 96:224], s[:, HELD:HELD + 64].indirect(L("AL", t, 0, 8)), [al, held[-1]])
+        p1 = V("copy", [al, held[0]], wd(T["cLA%d" % t], 96, 224), wd(c, HELD, HELD + 64).indirect(L("AL", t, 0, 8)))
+        sendcols("aq%d" % t, "LA%d" % t, 128, 0, p1, p2)
+        return [p1, p2]
 
     def tell(t, ve):
-        vs = V("ts", [ve], L("VS", t, 0, 8), T.VEB[:, 15:128:16], 4.0, None, A.mult)
-        send("av", t, "VL", "VS", [vs])
+        vs = V("ts", [ve], L("VL", t, 8, 16), T.VEB[:, 15:128:16], 4.0, None, A.mult)
+        send("av", t, "VL", 10, 2, [vs])
         return vs
 
     def eq(b):
@@ -280,20 +284,18 @@ def rank_program(g, core, T, topo):
         if t > 0:
             d = [S(T.DQ[:, 128 * b:128 * b + 128], T.pv[:, 512 * b:512 * b + 128], [dq[b], prev["ht"]]) for b in range(2)]
         aside(3)
-        V("tt", [vs, K["m8"]], T.T8[:, 6:8], L("VS", t, 6, 8), T.M8[:, 6:8], A.mult)
-        V("copy", [vs], T.VA[:, 6:8], L("VS", t, 6, 8))
-        b8 = V("tt", [("av%d" % t, LIST)], T.T8[:, 0:6], L("VL", t, 0, 6), T.M8[:, 0:6], A.mult)
-        va = V("copy", [], T.VA[:, 0:6], L("VL", t, 0, 6))
-        vr = V("tt", [i_tb], T.VR[:, 0:6], L("VL", t, 0, 6), T.TB[:, 0:6], A.add) if t > 0 else None
+        b8 = V("tt", [vs, K["m8"], ("av%d" % t, LIST)], T.T8[:, :], L("VL", t, 2, 10), T.M8[:, :], A.mult)
+        if t > 0:
+            step()
         vp = V("red", [b8], T.VP[:, 0:1], T.T8[:, :], AxisListType.X, A.add)
         c1 = V("copy", [z[1]], *zcopy(1))
         z4 = V("ts", [vp, i_io4], L("Z4", t, 0, 4), T.IO4[:, 0:4], T.VP[:, 0:1], None, A.add)
         c3 = V("copy", [z[3]], *zcopy(3))
         t64 = V("tt", [c0, c1, c2, c3, z4, K["nm"]], T.T64[:, :], T.ZS[:, 0:512].indirect(L("Z4", t, 0, 4)), T.NM64[:, :], A.add)
         step()
-        rm = V("scan", [t64], T.RM[:, 8:72], T.T64[:, :], T.T64[:, :], -BIG, A.max, A.max)
+        rm = V("scan", [t64], T.RM[:, 1:65], T.T64[:, :], T.T64[:, :], -BIG, A.max, A.max)
         step()
-        xs = V("ts", [rm, x_m, K["xs"], K["xl"]], T.XS[:, 0:32], T.RM[:, 0:56].indirect(T.XL[:, 0:2]), T.RM[:, 71:72], None, A.is_lt)
+        xs = V("ts", [rm, K["xm"], K["xs"], K["xl"]], T.XS[:, 0:32], T.RM[:, 0:56].indirect(T.XL[:, 0:2]), T.RM[:, 64:65], None, A.is_lt)
         step()
         xq = V("q", [xs, prev["xm"]], T.cXQ[:, 0:128], T.sXQ[:, 0:128], T.XS[:, :])
         xm = MM(T.px[:, 0:128], T.cSQ[:, 0:128], T.sSQ[:, 0:128], T.cXQ[:, 0:128], T.sXQ[:, 0:128], True, True, [xq, K["sq"], c3])
@@ -301,22 +303,21 @@ def rank_program(g, core, T, topo):
         aside(0)
         step()
         step()
+        of = V("tt", [xm], T.OF[:, :], T.px[:, 0:8], L("VL", t, 2, 10), A.add)
+        step()
         if t > 0:
-            og = V("tt", [xm, vr], T.OG[:, 0:6], T.px[:, 0:6], T.VR[:, 0:6], A.add)
-            of = V("tt", [xm, va], T.OF[:, :], T.px[:, 0:8], T.VA[:, :], A.add)
-            told = V("copy", [og], L("OR", t, 0, 6), T.OG[:, 0:6])
-            send("rc", t, "CL", "OR", [told])
-        else:
-            of = V("tt", [xm, va], T.OF[:, :], T.px[:, 0:8], T.VA[:, :], A.add)
+            told = V("ts", [of], L("OR", t, 0, 8), T.OF[:, :], float(512 * me), None, A.add)
+            send("rc", t, "OR", 0, 8, [told])
         ou = V("copy", [of], L("OU", t, 0, 8), T.OF[:, :])
         step()
         if t == 0:
             ks = S(T.sKC[:, 0:128], sKQ[:, 0:512].indirect(L("OU", t, 0, 8)), [ou, K["kq"]])
-            nd = V("tt", [ou, K["t3"], K["db"]], T.VD[:, :], T.NXA[:, 1536:2048].indirect(L("OU", t, 0, 8)), T.D16[:, :], A.mult)
+            nd = V("tt", [ou, K["t3"], K["d16"]], T.VD[:, :], T.NXA[:, 512 * me:512 * me + 512].indirect(L("OU", t, 0, 8)), T.D16B[:, 0:128], A.mult)
             kc = V("copy", [ou], wd(T.cKC, 0, 128), wd(KQ, 0, 512).indirect(L("OU", t, 0, 8)))
-            ne = V("scan", [nd, K["r16f"]], T.VE[:, :], T.RS16[:, :], T.VD[:, :], 0.0, A.mult, A.add)
-            told = V("ts", [ne], L("OR", t, 0, 8), T.VE[:, 15:128:16], float(-off), None, A.add)
-            send("rc", t, "CL", "OR", [told])
+            ne = V("scan", [nd, K["r16"]], T.VE[:, :], T.RS16B[:, 0:128], T.VD[:, :], 0.0, A.mult, A.add)
+            step()
+            told = V("copy", [ne], L("OR", t, 0, 8), T.VE[:, 15:128:16])
+            send("rc", t, "OR", 0, 8, [told])
             aside(1)
             h = []
             for b in range(4):
@@ -337,18 +338,14 @@ def rank_program(g, core, T, topo):
                      for b in range(2)]
             h = d + ready
             ht = ready[1]
-        step()
-        C, P = T["cNW%d" % t], T["sNW%d" % t]
-        nq = V("q", ready, C[:, 0:128], P[:, 0:128], T.HT[:, :])
-        sendcols("rq%d" % t, "RW%d" % t, "NW%d" % t, [nq])
+        nq = V("q", ready, T["cRW%d" % t][:, 0:128], T["sRW%d" % t][:, 0:128], T.HT[:, :])
+        sendcols("rq%d" % t, "RW%d" % t, 0, 128, nq, nq)
         prev.update({"z": [c0, c1, c2, of], "pv": h, "t64": t64, "ht": ht, "xm": xm, "of": of, "nq": nq})
-        w1 = V("copy", [nq, K["idl"]], wd(T["cRW%d" % t], 96, 128), wd(C, 96, 128).indirect(T.IDL[:, 0:2]))
-        w2 = S(T["sRW%d" % t][:, 96:128], P[:, 96:128].indirect(T.IDL[:, 0:2]), [nq, K["idl"]])
         aside(2)
-        return [w1, w2], ou, told
+        return nq, told
 
     def where(t):
-        md = V("scan", [K["db"]], T.MD[:, :], T.MK[:, :], T.D16B[:, :], 0.0, A.max, A.mult)
+        md = V("scan", [K["d16"]], T.MD[:, :], T.MK[:, :], T.D16B[:, :], 0.0, A.max, A.mult)
         yield None
         ud = V("scan", [md], T.UD[:, :], T.PX[:, :], T.MD[:, :], 0.0, A.max, A.mult)
         yield None
@@ -357,8 +354,8 @@ def rank_program(g, core, T, topo):
         w = T.FF[:, 15:256:16]
         w1 = V("ts", [ff], T.WW[:, 0:16], w, float(CAP), None, A.is_le)
         w2 = V("ts", [ff], T.WW[:, 16:32], w, 0.0, None, A.is_gt)
-        w3 = V("tt", [ff, K["c16"]], T.WW[:, 32:48], w, T.C16[:, :], A.add)
         yield None
+        w3 = V("tt", [ff, K["c16"]], T.WW[:, 32:48], w, T.C16[:, :], A.subtract)
         w4 = V("tt", [w1, w2], T.WW[:, 48:64], T.WW[:, 0:16], T.WW[:, 16:32], A.mult)
         yield None
         w5 = V("tt", [w4, w3], T.WW[:, 64:80], T.WW[:, 48:64], T.WW[:, 32:48], A.mult)
@@ -373,95 +370,86 @@ def rank_program(g, core, T, topo):
         while True:
             yield None
 
-    def order(t, held, back, deps, c, s, o):
-        h2 = S(s[:, o:o + 64], T["sRW%d" % t][:, 0:192].indirect(L("SL", t, 0, 4)), [held[-1], back[1]] + deps)
-        h1 = V("copy", [held[0], back[0]] + deps, wd(c, o, o + 64), wd(T["cRW%d" % t], 0, 192).indirect(L("SL", t, 0, 4)))
+    def order(t, held, nq, deps, c, s, o):
+        h2 = S(s[:, o:o + 64], T["sRW%d" % t][:, 96:288].indirect(L("SL", t, 0, 4)), [held[-1], nq] + deps)
+        h1 = V("copy", [held[0], nq] + deps, wd(c, o, o + 64), wd(T["cRW%d" % t], 96, 288).indirect(L("SL", t, 0, 4)))
         return [h1, h2]
 
     def table(b):
-        return S(T.NXA[:, 512 * b:512 * b + 512], T.NODF[:, 0:512].indirect(T.NXU[:, 32 * b:32 * b + 32]), [K["no"] if b == 3 else K["nu"], K["nf"]])
+        r = (me + 1 + b) % NR
+        return S(T.NXA[:, 512 * r:512 * r + 512], T.NODF[:, 0:512].indirect(T.NXU[:, 32 * b:32 * b + 32]), [K["no"] if b == 3 else K["nu"], K["nf"]])
 
     def dkc(b):
         K["dk"].append(S(T.DK[:, 512 * b:512 * b + 512], T.pv[:, 512 * b:512 * b + 512], [K["um"][b]]))
 
-    for b in range(4):
-        m_e = S(T.ET[:, 512 * b:512 * b + 512], T.RS64[:, :], [m_rs], 0.0, 0.0)
-
     k_st = V("copy", [d_st], T.STU[:, :], T.STW[:, :])
+    K["xl"] = V("ts", [x_g, x_u], T.XL[:, 0:2], T.XI[:, 0:2], T.XF[:, 1:2], T.XF[:, 0:1], A.is_equal, A.mult)
     start = T.NODI[:, 0:512].indirect(T.STU[:, 0:4])
-    bt = V("ts", [k_st, i_ni], T.BT[:, :], start, 7, 3, A.logical_shift_right, A.bitwise_and)
+    bt = V("ts", [k_st, i_ni], T.BT[:, :], start, 7, None, A.logical_shift_right)
 
     def gap0(k):
         if k == 0:
             K["node"] = V("copy", [], T.NN0[:, 128:192], start)
         if k == 1:
-            K["r16"] = V("set", [m_r16], T.RS16B[:, 0:256:16], 0.0)
-            K["jpa"] = V("ts", [i_jp], T.JPA[:, :], T.JP[:, :], 15, None, A.bitwise_and)
+            K["d16"] = V("ts", [k_t0, i_r16], T.D16B[:, :], T.R16[:, :], T.THR[:, 0:1], None, A.is_equal)
+            for b in range(4):
+                K["st"] = S(T.ST[:, b:512:4], T.D16B[:, 0:128], [K["d16"]])
+            K["nm"] = S(T.NM64[:, :], T.D16B[:, 0:64], [K["d16"]], -BIG, BIG, f=F.Identity)
         if k == 2:
-            K["r16f"] = V("set", [m_r16f], T.RS16[:, 0:128:16], 0.0)
             K["vt"] = V("ts", [K["node"]], T.VT[:, :], T.NN0[:, 128:192], 127, None, A.bitwise_and)
-        if k == 3:
-            K["held"] = [V("q", [d_x, m_xt], T.cRW0[:, 128:256], T.sRW0[:, 128:256], T.XT[:, :])]
         if k == 4:
-            K["d16"] = V("ts", [K["jpa"]], T.D16B[:, 0:128], T.JPA[:, :], 0.0, None, A.is_equal)
-        if k == 5:
-            K["xl"] = V("copy", [x_e], T.XL[:, 0:2], T.XF[:, 2:4])
-            K["id"] = V("ts", [i_jp], T.ID[:, :], T.JP[:, :], 0.0, 0.5, A.is_equal, A.mult)
+            K["held"] = [V("q", [d_x, m_xt], T.cRW0[:, HELD:HELD + 128], T.sRW0[:, HELD:HELD + 128], T.XT[:, :])]
 
     al = lists(0, bt, gap0)
     held, node = K["held"], K["node"]
     hq0 = held[0]
-    o2 = depart(0, al, held)
+    own = depart(0, al, held)
+    k_e = [S(T.ET[:, EW * h + 2 + h:EW * h + EW:4], T.ID[:, :], [m_e, k_id], 0.0, 0.5) for h in range(2)]
+    K["xs"] = S(T.XS[:, :], T.RS64[:, 0:512], [m_rs], 0.0, 0.0)
     vd = diag(0, al)
-    o1 = mine32(0, al, held)
+    K["sq"] = V("q", [K["st"]], T.cSQ[:, 0:128], T.sSQ[:, 0:128], T.ST[:, :])
     vs = tell(0, run(vd))
-    own = [o1, o2]
-    i_io4 = IOTA(T.IO4[:, 0:4], [[1, 4]], 0, 0)
-    i_16 = IOTA(T.IO[:, :], [[32, 4], [-16, 4]], -129, 0, True)
-    i_k16 = IOTA(T.IO4[:, 4:8], [[16, 4]], 0, 0)
-    i_tb = IOTA(T.TB[:, 0:6], [[-512, 3], [0, 2]], 1024, 0, True)
-    K["xs"] = IOTA(T.XS[:, :], [[0, 512]], 0, 0, True)
-    K["nf"] = IOTA(T.NODF[:, :], [[1, 512]], off, 0, True)
-    S(T.D16[:, :], T.D16B[:, 0:128], [K["d16"]])
-    K["db"] = S(T.D16B[:, 128:256], T.D16B[:, 0:128], [K["d16"]])
-    for b in range(4):
-        k_e = S(T.ET[:, 512 * b + b:512 * b + 512:4], T.ID[:, :], [m_e, K["id"]])
-    for b in range(4):
-        k_s = S(T.ST[:, b:512:4], T.D16B[:, 0:128], [K["d16"]])
+    i_16 = IOTA(T.IO[:, 0:16], [[-32, 4], [16, 4]], 129, 0, True)
+    i_k16 = IOTA(T.IO[:, 16:20], [[16, 4]], 128, 0, True)
+    K["nf"] = IOTA(T.NODF[:, :], [[1, 512]], 0, 0, True)
     K["kq"] = V("q", [d_ky], T.cKQ[:, 0:512], T.sKQ[:, 0:512], T.KT[:, :])
+
+    def unit(b):
+        o = EW * (b % 2) + (2 if b < 2 else 0)
+        K["eq"] = V("q", [k_e[b % 2]], *eq(b), T.ET[:, o:o + 512])
+
     find = where(0)
     next(find)
-    k_kp = V("ts", [i_kp], T.KP2[:, :], T.KP[:, :], 4, None, A.arith_shift_right)
-    K["nm"] = V("ts", [K["d16"]], T.NM64[:, :], T.D16B[:, 0:64], -1.0, BIG, A.add, A.mult)
+    unit(0)
     next(find)
-    K["m8"] = V("ts", [k_kp], T.M8[:, :], T.KP2[:, :], 0.0, None, A.is_equal)
-    K["c16"] = V("ts", [i_16, k_t0], T.C16[:, :], T.IO[:, :], T.THR[:, 0:1], None, A.subtract)
+    unit(2)
     next(find)
+    unit(1)
+    unit(3)
     K["no"] = V("copy", [d_no], T.NXU[:, 96:128], T.NXV[:, :])
-    K["eq"] = V("q", [k_e], T.cEQ[:, 0:512], T.sEQ[:, 0:512], T.ET[:, :])
-    K["sq"] = V("q", [k_s], T.cSQ[:, 0:128], T.sSQ[:, 0:128], T.ST[:, :])
     for b in range(3):
         for k in range(8):
             d_nx = DMA("y", "dnx", T.NXW[16 * k:16 * k + 16, 32 * b:32 * b + 32], T["NXR%d" % b][:, :], [("nxr", 3 * len(e16))])
-    DMA("y", "dh3", by(T.cHQ3, 64, 128), by(T.cRW0, 192, 256), [hq0])
-    d_h3 = DMA("y", "dh3", T.sHQ3[:, 64:128], T.sRW0[:, 192:256], [hq0])
+    DMA("y", "dh3", by(T.cHQ3, 64, 128), by(T.cRW0, HELD + 64, HELD + 128), [hq0])
+    d_h3 = DMA("y", "dh3", T.sHQ3[:, 64:128], T.sRW0[:, HELD + 64:HELD + 128], [hq0])
 
     def aside0(k):
         if k == 3:
+            K["c16"] = S(T.C16[:, :], T.IO[:, 0:16], [i_16, k_t0], T.THR[:, 0:1], f=F.Identity)
+            K["aw"] = S(T.AW[:, :], T.IO[:, 16:20], [i_k16, k_t0], T.THR[:, 0:1], f=F.Identity)
             K["t3"] = table(3)
-        if k == 0:
-            K["idl"] = V("ts", [k_t0, i_k16], T.IDL[:, :], T.IO4[:, 4:6], T.THR[:, 0:1], None, A.add)
-            K["aw"] = V("ts", [k_t0, i_k16], T.AW[:, :], T.IO4[:, 4:8], T.THR[:, 0:1], 128.0, A.add, A.add)
         if k == 2:
             K["nu"] = V("copy", [d_nx], T.NXU[:, 0:96], T.NXW[:, :])
             K["dk"] = []
             K["um"] = [MM(T.pv[:, 512 * b:512 * b + 512], *eq(b), T.cKQ[:, 0:512], T.sKQ[:, 0:512], True, True, [prev["pv"][b]]) for b in range(4)]
             for b in range(2):
                 dkc(b)
-            K["nxa"] = [K["t3"], table(0)]
+            K["nxa"] = [K["t3"]]
 
     def aside1(k):
         if k == 3:
+            K["nxa"].append(table(1))
+        if k == 1:
             K["nxa"].append(table(2))
         if k == 2:
             K["wq"] = V("q", [d_w], T.cWQ[:, 0:128], T.sWQ[:, 0:128], T.WT[:, :])
@@ -470,58 +458,51 @@ def rank_program(g, core, T, topo):
     for t in range(HOPS):
         n = T["NN%d" % t]
         if t == 0:
-            back, ou, told = server(0, own, vs, prev, aside0, lambda: next(find))
-            mine, theirs, tabs = T.NODI[:, 0:512].indirect(L("OR", 0, 6, 8)), T.NODI[:, 0:512].indirect(L("CL", 0, 0, 6)), [told]
+            nq, told = server(0, own, vs, prev, aside0, lambda: next(find))
+            slots, tabs = T.NODI[:, 0:512].indirect(L("OR", 0, 6, 14)), [told]
         else:
-            find = where(t)
-            next(find)
             if t == 1:
                 dkc(2)
+                next(find)
                 K["dk"].append(V("copy", [K["um"][3]], T.DK[:, 1536:2048], T.pv[:, 1536:2048]))
                 prev["pv"] = K["dk"]
-                K["nxa"].append(table(1))
+                K["nxa"].append(table(0))
+            else:
+                next(find)
             next(find)
-            next(find)
-            back, ou, told = server(t, own, vs, prev, aside1 if t == 1 else lambda k: None, lambda: next(find))
-            mine, theirs, tabs = T.NXA[:, 1536:2048].indirect(L("OU", t, 6, 8)), T.NXA[:, 0:1536].indirect(L("CL", t, 0, 6)), [ou] + K["nxa"]
+            nq, told = server(t, own, vs, prev, aside1 if t == 1 else lambda k: None, lambda: next(find))
+            slots, tabs = T.NXA[:, 0:2048].indirect(L("OR", t, 6, 14)), [told] + K["nxa"]
         sl = K["sl"]
-        V("copy", tabs, n[:, 96:128], mine)
-        V("ts", [node], T.ND[:, 64 * t:64 * t + 64], n[:, 128:192], float(-off), None, A.add)
-        g1 = V("copy", [("rc%d" % t, LIST)], n[:, 0:96], theirs)
+        was = V("copy", [node], T.ND[:, 64 * t:64 * t + 64], n[:, 128:192])
+        g1 = V("copy", tabs + [("rc%d" % t, LIST)], n[:, 0:128], slots)
         byq = n[:, 0:192].indirect(L("SL", t, 0, 4))
         got = [sl, ("rq%d" % t, COLS)]
-
-        def nodes():
-            return V("copy", [g1, sl, node], T["NN%d" % (t + 1)][:, 128:192], byq)
-
         if t + 1 == HOPS:
-            node = nodes()
-            nd = V("ts", [node], T.ND[:, 64 * HOPS:64 * HOPS + 64], T["NN%d" % HOPS][:, 128:192], float(-off), None, A.add)
-            DMA("y", "dout", T.nd[:, :], T.ND[0:1, 0:256], [nd])
-            hq = order(t, held, back, got, T.cHQ3, T.sHQ3, 0)
+            nd = V("copy", [g1, sl, node], T.ND[:, 64 * HOPS:64 * HOPS + 64], byq)
+            DMA("y", "dout", T.nd[:, :], T.ND[0:1, 0:256], [nd, was])
+            hq = order(t, held, nq, got, T.cHQ3, T.sHQ3, 0)
             break
-        bt = V("ts", [g1, sl, node], T.BT[:, :], byq, 7, 3, A.logical_shift_right, A.bitwise_and)
+        bt = V("ts", [g1, sl, node], T.BT[:, :], byq, 7, None, A.logical_shift_right)
 
         def gap(k):
             if k == 0:
-                K["node"] = nodes()
+                K["node"] = V("copy", [g1, sl, node], T["NN%d" % (t + 1)][:, 128:192], byq)
             if k == 2:
                 K["vt"] = V("ts", [K["node"]], T.VT[:, :], T["NN%d" % (t + 1)][:, 128:192], 127, None, A.bitwise_and)
-            if k == 5:
-                K["held"] = order(t, held, back, got, T["cRW%d" % (t + 1)], T["sRW%d" % (t + 1)], 128)
+            if k == 4:
+                K["held"] = order(t, held, nq, got, T["cRW%d" % (t + 1)], T["sRW%d" % (t + 1)], HELD)
 
         al = lists(t + 1, bt, gap)
         held, node = K["held"], K["node"]
-        o2 = depart(t + 1, al, held)
+        own = depart(t + 1, al, held)
         vd = diag(t + 1, al)
-        ve = run(vd)
-        o1 = mine32(t + 1, al, held)
-        vs = tell(t + 1, ve)
-        own = [o1, o2]
+        find = where(t + 1)
+        next(find)
+        vs = tell(t + 1, run(vd))
 
     DMA("y", "dout", T.oc[:, :], by(T.cHQ3, 0, 64), [hq[0]])
     for k in range(4):
-        DMA("s" if k < 2 else "y", "dout", T.osc[4 * k:4 * k + 4, 0:64], T.sHQ3[32 * k:32 * k + 4, 0:64], [hq[1]])
+        DMA("s" if k < 3 else "y", "dout", T.osc[4 * k:4 * k + 4, 0:64], T.sHQ3[32 * k:32 * k + 4, 0:64], [hq[1]])
     ym = MM(T.px[:, 0:128], T.cWQ[:, 0:128], T.sWQ[:, 0:128], T.cHQ3[:, 0:128], T.sHQ3[:, 0:128], True, True, hq + [K["wq"], d_h3, prev["of"]])
     yc = V("copy", [ym], T.YS[:, :], T.px[:, 0:64])
     DMA("y", "dout", T.y[:, :], T.YS[:, :], [yc])

@@ -5,36 +5,39 @@ NR, CAP, HOPS = 4, 32, 3
 BIG = 1e29
 CUTS = (0, 128, 256, 384, 512)
 HELD = 224
+FINE = 2.0 ** -15
+COARSE = 1.5 * 2.0 ** 15
+PAD = 1536
 EW = 514
 
 SCRATCH = {
     "STW": ("sbuf", [128, 4], "int32"), "STU": ("sbuf", [128, 4], "uint16"),
     "NXD": ("dram", [128, 4], "int32"), "NXR0": ("dram", [128, 4], "int32"), "NXR1": ("dram", [128, 4], "int32"), "NXR2": ("dram", [128, 4], "int32"),
     "NXW": ("sbuf", [128, 96], "int32"), "NXV": ("sbuf", [128, 32], "int32"), "NXU": ("sbuf", [128, 128], "uint16"), "NXA": ("sbuf", [128, 2048], "float32"),
-    "NODF": ("sbuf", [128, 512], "float32"), "NODI": ("sbuf", [128, 512], "int32"),
+    "NODF": ("sbuf", [128, 512], "float32"),
     "R16": ("sbuf", [128, 256], "bfloat16"), "ID": ("sbuf", [128, 128], "bfloat16"),
-    "PI": ("sbuf", [128, 8], "int32"), "THR": ("sbuf", [128, 8], "float32"), "M8": ("sbuf", [128, 8], "bfloat16"),
-    "XI": ("sbuf", [128, 8], "int32"), "XF": ("sbuf", [128, 8], "float32"), "XL": ("sbuf", [128, 2], "uint16"),
-    "IO4": ("sbuf", [128, 8], "int32"), "AW": ("sbuf", [128, 4], "float32"),
-    "IO": ("sbuf", [128, 24], "float32"), "C16": ("sbuf", [128, 16], "float32"),
+    "PI": ("sbuf", [128, 8], "int32"), "THR": ("sbuf", [128, 8], "float32"),
+    "XI": ("sbuf", [128, 8], "int32"), "XF": ("sbuf", [128, 8], "float32"), "XL": ("sbuf", [128, 8], "uint16"),
+    "IO4": ("sbuf", [128, 8], "int32"), "AW": ("sbuf", [128, 16], "float32"),
+    "IO": ("sbuf", [128, 32], "float32"), "C16": ("sbuf", [128, 16], "float32"),
     "D16B": ("sbuf", [128, 256], "bfloat16"), "NM64": ("sbuf", [128, 64], "float32"),
     "RS64": ("sbuf", [128, 576], "bfloat16"), "RS16B": ("sbuf", [128, 256], "bfloat16"),
+    "RK": ("sbuf", [128, 768], "bfloat16"), "UP": ("sbuf", [128, 128], "bfloat16"),
     "AL": ("sbuf", [128, 48], "uint16"),
     "VL": ("sbuf", [128, 48], "float32"),
     "Z4": ("sbuf", [128, 48], "uint16"),
-    "OU": ("sbuf", [128, 48], "uint16"),
+    "OU": ("sbuf", [128, 16], "uint16"),
     "OR": ("sbuf", [128, 48], "uint16"),
     "SL": ("sbuf", [128, 48], "uint16"),
-    "BT": ("sbuf", [128, 64], "int32"), "VT": ("sbuf", [128, 64], "int32"), "MK": ("sbuf", [128, 256], "bfloat16"), "PX": ("sbuf", [128, 256], "bfloat16"),
-    "CN": ("sbuf", [128, 512], "bfloat16"), "SC": ("sbuf", [128, 512], "bfloat16"), "VD": ("sbuf", [128, 128], "float32"), "VE": ("sbuf", [128, 128], "float32"),
-    "VDB": ("sbuf", [128, 128], "bfloat16"), "VEB": ("sbuf", [128, 128], "bfloat16"),
+    "MK": ("sbuf", [128, 256], "bfloat16"), "PX": ("sbuf", [128, 256], "bfloat16"),
+    "CN": ("sbuf", [128, 544], "bfloat16"), "SC": ("sbuf", [128, 512], "bfloat16"), "VD": ("sbuf", [128, 128], "float32"), "VE": ("sbuf", [128, 128], "float32"),
     "MD": ("sbuf", [128, 256], "bfloat16"), "UD": ("sbuf", [128, 256], "bfloat16"), "FF": ("sbuf", [128, 256], "bfloat16"),
     "WW": ("sbuf", [128, 96], "float32"), "ND": ("sbuf", [128, 256], "float32"),
-    "VP": ("sbuf", [128, 8], "float32"), "T8": ("sbuf", [128, 8], "float32"),
+    "VP": ("sbuf", [128, 16], "float32"),
     "ZS": ("sbuf", [128, 512], "float32"), "T64": ("sbuf", [128, 64], "float32"),
     "RM": ("sbuf", [128, 72], "float32"),
     "XS": ("sbuf", [128, 512], "bfloat16"), "OF": ("sbuf", [128, 8], "float32"), "HT": ("sbuf", [128, 512], "bfloat16"),
-    "DK": ("sbuf", [128, 2048], "float32"), "DQ": ("sbuf", [128, 256], "float32"), "GK": ("sbuf", [128, 256], "float32"),
+    "DK": ("sbuf", [128, PAD + 2048], "float32"), "DQ": ("sbuf", [128, 256], "float32"), "GK": ("sbuf", [128, 256], "float32"),
     "XT": ("sbuf", [128, 512], "bfloat16"), "KT": ("sbuf", [128, 2048], "bfloat16"), "WT": ("sbuf", [128, 512], "bfloat16"),
     "ET": ("sbuf", [128, 2 * EW], "bfloat16"), "ST": ("sbuf", [128, 512], "bfloat16"), "YS": ("sbuf", [128, 64], "float32"),
     "pv": ("psum", [128, 2048], "float32"), "pz": ("psum", [128, 1536], "float32"), "px": ("psum", [128, 512], "float32"),
@@ -51,7 +54,7 @@ for _n, _w in (("KQ", 512), ("EQ", 512), ("SQ", 128), ("WQ", 128), ("XQ", 128), 
 for _t in range(HOPS):
     for _n, _w in (("LA", 224), ("RW", 288 if _t else 352)):
         _codes(_n + str(_t), _w)
-    SCRATCH["NN%d" % _t] = ("sbuf", [128, 192], "int32")
+    SCRATCH["NN%d" % _t] = ("sbuf", [128, 192], "float32")
 SEMAPHORES = ["cv", "cs", "ct", "cg", "ls", "dst", "dx", "dno", "dnx", "dnd", "nxr", "dky", "dw", "dh3", "dout"]
 for _t in range(HOPS):
     SEMAPHORES += ["aq%d" % _t, "av%d" % _t, "rq%d" % _t, "rc%d" % _t]
@@ -192,8 +195,8 @@ def rank_program(g, core, T, topo):
 
     IOTA(T.PI[:, 0:1], [[0, 1]], 4, 4)
     i_pi = IOTA(T.PI[:, 1:3], [[-64, 2]], 0, 1)
-    i_ni = IOTA(T.NODI[:, :], [[1, 512]], 0, 0)
-    i_r16 = IOTA(T.R16[:, :], [[0, 16], [1, 16]], 0, 0, True)
+    K["nf"] = IOTA(T.NODF[:, :], [[1, 512]], 0, 0, True)
+    i_r16 = IOTA(T.R16[:, :], [[0, 16], [1, 16]], 1, 0, True)
     need("g", [d_nd])
     e16 = topo.engines(core, cores[peers[0]])
     fused([RemoteDMATransfer(dst_ids=[coreid(r) for r in peers], dma_engine_mask=bits(e16), remote_sem=T.sem.nxr, srcs=[T.NXD[:, :]],
@@ -201,47 +204,55 @@ def rank_program(g, core, T, topo):
     count["ls"] = len(e16)
 
     m_rs = V("set", [], T.RS64[:, 0:EW], 1.0)
+    m_up = V("set", [], T.MD[:, 0:128], 1.0 / 64)
     k_pj = V("ts", [i_pi], T.XI[:, 4:5], T.PI[:, 1:2], 15, None, A.bitwise_and)
     m_rs = V("set", [m_rs], T.RS64[:, 0:256:64], 0.0)
-    k_t0 = V("ts", [k_pj], T.THR[:, 0:1], T.XI[:, 4:5], 0.0, None, A.add)
+    K["cn"] = V("set", [], T.CN[:, 0:544:272], 0.0)
+    k_t0 = V("ts", [k_pj], T.THR[:, 0:1], T.XI[:, 4:5], 1.0, None, A.add)
+    k_t1 = V("ts", [k_pj], T.THR[:, 1:2], T.XI[:, 4:5], 17.0, None, A.add)
+    K["up"] = V("scan", [m_rs, m_up], T.UP[:, :], T.RS64[:, 0:128], T.MD[:, 0:128], 0.0, A.mult, A.add)
+    K["rk"] = [V("ts", [m_rs, k], T.RK[:, 256 * h:256 * h + 128], T.RS64[:, 0:128], 0.0, T.THR[:, h:h + 1], A.is_equal, A.mult)
+               for h, k in enumerate((k_t0, k_t1))]
     x_g = V("ts", [i_pi], T.XI[:, 0:2], T.PI[:, 1:3], 0xFFF0, None, A.bitwise_and)
     x_u = V("ts", [i_pi], T.XI[:, 2:4], T.PI[:, 0:2], 12, None, A.bitwise_and)
     K["xm"] = V("set", [], T.RM[:, 0:1], BIG)
     x_u = V("ts", [x_u], T.XF[:, 0:2], T.XI[:, 2:4], 4.0, None, A.mult)
     k_id = SEL(T.ID[:, :], T.RS64[:, 256:384], [[-1, 128]], A.is_equal, 0, 1, [m_rs])
-    k_m = SEL(T.M8[:, :], T.RS64[:, 256:264], [[-16, 8]], A.is_ge, 0, 1, [m_rs])
-    i_io4 = IOTA(T.IO4[:, 0:4], [[1, 4]], 0, 0)
-    K["m8"] = SEL(T.M8[:, :], T.M8[:, :], [[16, 8]], A.is_ge, 15, -1, [k_m])
+    i_io4 = IOTA(T.IO4[:, 0:4], [[1, 4]], -512 * me, 0)
 
     m_xt = S(T.XT[:, 256:512], T.RS64[:, 0:256], [m_rs], 0.0, 0.0)
     for h in range(2):
         m_e = S(T.ET[:, EW * h:EW * h + EW], T.RS64[:, 0:EW], [m_rs], 0.0, 0.0)
-    K["r16"] = S(T.RS16B[:, :], T.R16[:, :], [i_r16], f=F.Sign)
+    K["r16"] = S(T.RS16B[:, :], T.R16[:, :], [i_r16], -1.0, f=F.Sign)
 
-    def lists(t, bt, gap):
+    def lists(t, node, gap):
+        n = T["NN%d" % t][:, 128:192]
         gap(0)
-        mk = []
-        for i in range(4):
-            mk.append(V("ts", [bt], T.MK[:, 64 * i:64 * i + 64], T.BT[:, :], float((me + i) % NR), None, A.is_equal))
+        mk = [V("ts", [node], T.MK[:, 64 * i:64 * i + 64], n, COARSE, COARSE + ((me + i) % NR) / 256.0, A.add, A.is_equal) for i in range(4)]
         gap(1)
-        px = [V("scan", [mk[2 * h + 1], m_rs], T.PX[:, 128 * h:128 * h + 128], T.RS64[:, 0:128], T.MK[:, 128 * h:128 * h + 128], 0.0, A.mult, A.add)
-              for h in range(2)]
+        px, sc = {}, {}
+        for u in range(2):
+            for h in range(2):
+                o = 272 * h + 128 * u + 1
+                px[h, u] = V("scan", [mk[2 * u + 1], K["rk"][h]], T.CN[:, o:o + 128], T.RK[:, 256 * h:256 * h + 128], T.MK[:, 128 * u:128 * u + 128],
+                             0.0, A.max, A.subtract)
         gap(2)
-        cn = [V("ts", [px[1], k_t0], T.CN[:, 0:256], T.PX[:, :], T.THR[:, 0:1], None, A.is_le),
-              V("ts", [px[1], k_t0], T.CN[:, 256:512], T.PX[:, :], -16.0, T.THR[:, 0:1], A.add, A.is_le)]
-        gap(3)
-        sc = [V("scan", [cn[h]], T.SC[:, 256 * h:256 * h + 256], T.RS64[:, 0:256], T.CN[:, 256 * h:256 * h + 256], 0.0, A.mult, A.add) for h in range(2)]
+        for u in range(2):
+            for h in range(2):
+                o = 272 * h + 128 * u
+                sc[h] = V("scan", [px[h, u], K["up"], K["cn"]], T.SC[:, 256 * h + 128 * u:256 * h + 128 * u + 128], T.CN[:, o:o + 128], T.UP[:, 0:128],
+                          1.0, A.max, A.min)
         gap(4)
         for h in range(2):
-            al = V("ts", [sc[h]], L("AL", t, h, 8, 2), T.SC[:, 256 * h + 63:256 * h + 256:64], 63.0, None, A.min)
+            al = V("ts", [sc[h]], L("AL", t, h, 8, 2), T.SC[:, 256 * h + 63:256 * h + 256:64], 64.0, -1.0, A.mult, A.add)
         gap(5)
         return al
 
     def diag(t, al):
-        return V("tt", [K["vt"], al, K["d16"]], T.VDB[:, :], T.VT[:, 0:64].indirect(L("AL", t, 0, 8)), T.D16B[:, 0:128], A.mult)
+        return V("tt", [al, K["d16"]], T.VD[:, :], T["NN%d" % t][:, 128:192].indirect(L("AL", t, 0, 8)), T.D16B[:, 0:128], A.mult)
 
     def run(vd):
-        return V("scan", [vd, K["r16"]], T.VEB[:, :], T.RS16B[:, 0:128], T.VDB[:, :], 0.0, A.mult, A.add)
+        return V("scan", [vd, K["r16"]], T.VE[:, :], T.RS16B[:, 0:128], T.VD[:, :], 0.0, A.mult, A.add)
 
     def depart(t, al, held):
         c, s = T["cRW%d" % t], T["sRW%d" % t]
@@ -251,7 +262,7 @@ def rank_program(g, core, T, topo):
         return [p1, p2]
 
     def tell(t, ve):
-        vs = V("ts", [ve], L("VL", t, 8, 16), T.VEB[:, 15:128:16], 4.0, None, A.mult)
+        vs = V("ts", [ve], L("VL", t, 8, 16), T.VE[:, 15:128:16], 4.0 / FINE, 254.0, A.mult, A.add)
         send("av", t, "VL", 10, 2, [vs])
         return vs
 
@@ -284,12 +295,9 @@ def rank_program(g, core, T, topo):
         if t > 0:
             d = [S(T.DQ[:, 128 * b:128 * b + 128], T.pv[:, 512 * b:512 * b + 128], [dq[b], prev["ht"]]) for b in range(2)]
         aside(3)
-        b8 = V("tt", [vs, K["m8"], ("av%d" % t, LIST)], T.T8[:, :], L("VL", t, 2, 10), T.M8[:, :], A.mult)
-        if t > 0:
-            step()
-        vp = V("red", [b8], T.VP[:, 0:1], T.T8[:, :], AxisListType.X, A.add)
+        vp = V("copy", [vs, K["xl"], ("av%d" % t, LIST)], T.VP[:, :], L("VL", t, 0, 10).indirect(T.XL[:, 2:3]))
         c1 = V("copy", [z[1]], *zcopy(1))
-        z4 = V("ts", [vp, i_io4], L("Z4", t, 0, 4), T.IO4[:, 0:4], T.VP[:, 0:1], None, A.add)
+        z4 = V("ts", [vp, i_io4], L("Z4", t, 0, 4), T.IO4[:, 0:4], T.VP[:, 0:1], 511.0, A.add, A.min)
         c3 = V("copy", [z[3]], *zcopy(3))
         t64 = V("tt", [c0, c1, c2, c3, z4, K["nm"]], T.T64[:, :], T.ZS[:, 0:512].indirect(L("Z4", t, 0, 4)), T.NM64[:, :], A.add)
         step()
@@ -302,21 +310,21 @@ def rank_program(g, core, T, topo):
         dq += [half(b) for b in range(2, 4)]
         aside(0)
         step()
-        step()
         of = V("tt", [xm], T.OF[:, :], T.px[:, 0:8], L("VL", t, 2, 10), A.add)
         step()
         if t > 0:
-            told = V("ts", [of], L("OR", t, 0, 8), T.OF[:, :], float(512 * me), None, A.add)
+            ou = told = V("ts", [of], L("OR", t, 0, 8), T.OF[:, :], 512.0 * me, 512.0 * me + 511.0, A.max, A.min)
             send("rc", t, "OR", 0, 8, [told])
-        ou = V("copy", [of], L("OU", t, 0, 8), T.OF[:, :])
+        else:
+            ou = V("ts", [of], T.OU[:, 0:8], T.OF[:, :], -512.0 * me, 511.0, A.add, A.min)
         step()
         if t == 0:
-            ks = S(T.sKC[:, 0:128], sKQ[:, 0:512].indirect(L("OU", t, 0, 8)), [ou, K["kq"]])
-            nd = V("tt", [ou, K["t3"], K["d16"]], T.VD[:, :], T.NXA[:, 512 * me:512 * me + 512].indirect(L("OU", t, 0, 8)), T.D16B[:, 0:128], A.mult)
-            kc = V("copy", [ou], wd(T.cKC, 0, 128), wd(KQ, 0, 512).indirect(L("OU", t, 0, 8)))
-            ne = V("scan", [nd, K["r16"]], T.VE[:, :], T.RS16B[:, 0:128], T.VD[:, :], 0.0, A.mult, A.add)
+            ks = S(T.sKC[:, 0:128], sKQ[:, 0:512].indirect(T.OU[:, 0:8]), [ou, K["kq"]])
+            kc = V("copy", [ou], wd(T.cKC, 0, 128), wd(KQ, 0, 512).indirect(T.OU[:, 0:8]))
+            nd = V("tt", [ou, K["t3"], K["d16"]], T.VD[:, :], T.NXA[:, 512 * me:512 * me + 512].indirect(T.OU[:, 0:8]), T.D16B[:, 0:128], A.mult)
+            ne = run(nd)
             step()
-            told = V("copy", [ne], L("OR", t, 0, 8), T.VE[:, 15:128:16])
+            told = V("ts", [ne], L("OR", t, 0, 8), T.VE[:, 15:128:16], 1.0 / FINE, 63.5, A.mult, A.add)
             send("rc", t, "OR", 0, 8, [told])
             aside(1)
             h = []
@@ -328,7 +336,7 @@ def rank_program(g, core, T, topo):
             ht = None
         else:
             def chosen(b):
-                return T.DK[:, 512 * b:512 * b + 512].indirect(L("OU", t, 0, 8))
+                return T.DK[:, PAD + 512 * (b - me):PAD + 512 * b + 512].indirect(L("OR", t, 0, 8))
 
             gk = [S(T.GK[:, 128 * b:128 * b + 128], chosen(2 + b), [ou, prev["ht"]] + K["dk"]) for b in range(2)]
             aside(1)
@@ -347,26 +355,21 @@ def rank_program(g, core, T, topo):
     def where(t):
         md = V("scan", [K["d16"]], T.MD[:, :], T.MK[:, :], T.D16B[:, :], 0.0, A.max, A.mult)
         yield None
-        ud = V("scan", [md], T.UD[:, :], T.PX[:, :], T.MD[:, :], 0.0, A.max, A.mult)
+        pb = V("scan", [K["rb"]], T.PX[:, :], T.RK[:, 512:768], T.MK[:, :], 0.0, A.max, A.subtract)
+        yield None
+        ud = V("scan", [md, pb], T.UD[:, :], T.PX[:, :], T.MD[:, :], 0.0, A.max, A.mult)
         yield None
         ff = V("scan", [ud, K["r16"]], T.FF[:, :], T.RS16B[:, :], T.UD[:, :], 0.0, A.mult, A.add)
         yield None
-        w = T.FF[:, 15:256:16]
-        w1 = V("ts", [ff], T.WW[:, 0:16], w, float(CAP), None, A.is_le)
-        w2 = V("ts", [ff], T.WW[:, 16:32], w, 0.0, None, A.is_gt)
+        w = T.FF[:, 0:256].indirect(T.XL[:, 4:5])
+        w1 = V("ts", [ff, K["xk"]], T.WW[:, 0:16], w, 64.5 - CAP, None, A.is_gt)
+        w3 = V("tt", [ff, K["c16"]], T.WW[:, 32:48], w, T.C16[:, :], A.add)
         yield None
-        w3 = V("tt", [ff, K["c16"]], T.WW[:, 32:48], w, T.C16[:, :], A.subtract)
-        w4 = V("tt", [w1, w2], T.WW[:, 48:64], T.WW[:, 0:16], T.WW[:, 16:32], A.mult)
+        w5 = V("tt", [w1, w3], T.WW[:, 64:80], T.WW[:, 0:16], T.WW[:, 32:48], A.mult)
         yield None
-        w5 = V("tt", [w4, w3], T.WW[:, 64:80], T.WW[:, 48:64], T.WW[:, 32:48], A.mult)
+        w8 = V("scan", [w5, K["aw"]], T.WW[:, 80:96], T.AW[:, :], T.WW[:, 64:80], 0.0, A.max, A.subtract)
         yield None
-        w6 = V("tt", [w5], T.WW[:, 80:88], T.WW[:, 64:72], T.WW[:, 72:80], A.add)
-        yield None
-        w7 = V("tt", [w6], T.WW[:, 88:92], T.WW[:, 80:84], T.WW[:, 84:88], A.add)
-        yield None
-        w8 = V("tt", [w7, K["aw"]], T.WW[:, 92:96], T.WW[:, 88:92], T.AW[:, :], A.add)
-        yield None
-        K["sl"] = V("copy", [w8], L("SL", t, 0, 4), T.WW[:, 92:96])
+        K["sl"] = V("copy", [w8], L("SL", t, 0, 4), T.WW[:, 83:96:4])
         while True:
             yield None
 
@@ -377,48 +380,54 @@ def rank_program(g, core, T, topo):
 
     def table(b):
         r = (me + 1 + b) % NR
-        return S(T.NXA[:, 512 * r:512 * r + 512], T.NODF[:, 0:512].indirect(T.NXU[:, 32 * b:32 * b + 32]), [K["no"] if b == 3 else K["nu"], K["nf"]])
+        return S(T.NXA[:, 512 * r:512 * r + 512], T.NODF[:, 0:512].indirect(T.NXU[:, 32 * b:32 * b + 32]), [K["no"] if b == 3 else K["nu"], K["nf"]],
+                 -63.5 * FINE, FINE, f=F.Identity)
 
     def dkc(b):
-        K["dk"].append(S(T.DK[:, 512 * b:512 * b + 512], T.pv[:, 512 * b:512 * b + 512], [K["um"][b]]))
+        K["dk"].append(S(T.DK[:, PAD + 512 * b:PAD + 512 * b + 512], T.pv[:, 512 * b:512 * b + 512], [K["um"][b]]))
+
+    def numbered(out, offsets, deps):
+        return V("ts", deps + [K["nf"]], out, T.NODF[:, 0:512].indirect(offsets), FINE, -63.5 * FINE, A.mult, A.add)
 
     k_st = V("copy", [d_st], T.STU[:, :], T.STW[:, :])
-    K["xl"] = V("ts", [x_g, x_u], T.XL[:, 0:2], T.XI[:, 0:2], T.XF[:, 1:2], T.XF[:, 0:1], A.is_equal, A.mult)
-    start = T.NODI[:, 0:512].indirect(T.STU[:, 0:4])
-    bt = V("ts", [k_st, i_ni], T.BT[:, :], start, 7, None, A.logical_shift_right)
+    V("ts", [x_g, x_u], T.XL[:, 0:2], T.XI[:, 0:2], T.XF[:, 1:2], T.XF[:, 0:1], A.is_equal, A.mult)
+    node = numbered(T.NN0[:, 128:192], T.STU[:, 0:4], [k_st])
 
     def gap0(k):
         if k == 0:
-            K["node"] = V("copy", [], T.NN0[:, 128:192], start)
+            K["xl"] = V("ts", [x_g], T.XL[:, 2:3], T.XI[:, 0:1], 1.0 / 16, 2.0, A.mult, A.add)
         if k == 1:
             K["d16"] = V("ts", [k_t0, i_r16], T.D16B[:, :], T.R16[:, :], T.THR[:, 0:1], None, A.is_equal)
             for b in range(4):
                 K["st"] = S(T.ST[:, b:512:4], T.D16B[:, 0:128], [K["d16"]])
             K["nm"] = S(T.NM64[:, :], T.D16B[:, 0:64], [K["d16"]], -BIG, BIG, f=F.Identity)
-        if k == 2:
-            K["vt"] = V("ts", [K["node"]], T.VT[:, :], T.NN0[:, 128:192], 127, None, A.bitwise_and)
         if k == 4:
             K["held"] = [V("q", [d_x, m_xt], T.cRW0[:, HELD:HELD + 128], T.sRW0[:, HELD:HELD + 128], T.XT[:, :])]
 
-    al = lists(0, bt, gap0)
-    held, node = K["held"], K["node"]
+    al = lists(0, node, gap0)
+    held = K["held"]
     hq0 = held[0]
     own = depart(0, al, held)
     k_e = [S(T.ET[:, EW * h + 2 + h:EW * h + EW:4], T.ID[:, :], [m_e, k_id], 0.0, 0.5) for h in range(2)]
     K["xs"] = S(T.XS[:, :], T.RS64[:, 0:512], [m_rs], 0.0, 0.0)
     vd = diag(0, al)
     K["sq"] = V("q", [K["st"]], T.cSQ[:, 0:128], T.sSQ[:, 0:128], T.ST[:, :])
-    vs = tell(0, run(vd))
-    i_16 = IOTA(T.IO[:, 0:16], [[-32, 4], [16, 4]], 129, 0, True)
-    i_k16 = IOTA(T.IO[:, 16:20], [[16, 4]], 128, 0, True)
-    K["nf"] = IOTA(T.NODF[:, :], [[1, 512]], 0, 0, True)
+    ve = run(vd)
+    x_k = V("ts", [k_pj], T.XI[:, 5:6], T.XI[:, 4:5], 68.0, None, A.mult)
+    vs = tell(0, ve)
+    i_16 = IOTA(T.IO[:, 0:16], [[16, 4], [-32, 4]], 63, 0, True)
+    i_k16 = IOTA(T.IO[:, 16:32], [[16, 4], [-1024, 4]], 127, 0, True)
+    x_k = V("ts", [x_k], T.XI[:, 6:7], T.XI[:, 5:6], 0xF0, None, A.bitwise_and)
     K["kq"] = V("q", [d_ky], T.cKQ[:, 0:512], T.sKQ[:, 0:512], T.KT[:, :])
+    K["rb"] = V("ts", [], T.RK[:, 512:768], T.RS64[:, 0:256], 0.0, 65.0, A.is_equal, A.mult)
+    K["xk"] = V("ts", [x_k], T.XL[:, 4:5], T.XI[:, 6:7], 15.0, None, A.add)
 
     def unit(b):
         o = EW * (b % 2) + (2 if b < 2 else 0)
         K["eq"] = V("q", [k_e[b % 2]], *eq(b), T.ET[:, o:o + 512])
 
     find = where(0)
+    next(find)
     next(find)
     unit(0)
     next(find)
@@ -432,11 +441,11 @@ def rank_program(g, core, T, topo):
             d_nx = DMA("y", "dnx", T.NXW[16 * k:16 * k + 16, 32 * b:32 * b + 32], T["NXR%d" % b][:, :], [("nxr", 3 * len(e16))])
     DMA("y", "dh3", by(T.cHQ3, 64, 128), by(T.cRW0, HELD + 64, HELD + 128), [hq0])
     d_h3 = DMA("y", "dh3", T.sHQ3[:, 64:128], T.sRW0[:, HELD + 64:HELD + 128], [hq0])
+    K["c16"] = S(T.C16[:, :], T.IO[:, 0:16], [i_16, k_t0], T.THR[:, 0:1], f=F.Identity)
+    K["aw"] = S(T.AW[:, :], T.IO[:, 16:32], [i_k16, k_t0], T.THR[:, 0:1], f=F.Identity)
 
     def aside0(k):
         if k == 3:
-            K["c16"] = S(T.C16[:, :], T.IO[:, 0:16], [i_16, k_t0], T.THR[:, 0:1], f=F.Identity)
-            K["aw"] = S(T.AW[:, :], T.IO[:, 16:20], [i_k16, k_t0], T.THR[:, 0:1], f=F.Identity)
             K["t3"] = table(3)
         if k == 2:
             K["nu"] = V("copy", [d_nx], T.NXU[:, 0:96], T.NXW[:, :])
@@ -459,46 +468,46 @@ def rank_program(g, core, T, topo):
         n = T["NN%d" % t]
         if t == 0:
             nq, told = server(0, own, vs, prev, aside0, lambda: next(find))
-            slots, tabs = T.NODI[:, 0:512].indirect(L("OR", 0, 6, 14)), [told]
         else:
             if t == 1:
                 dkc(2)
                 next(find)
-                K["dk"].append(V("copy", [K["um"][3]], T.DK[:, 1536:2048], T.pv[:, 1536:2048]))
+                K["dk"].append(V("copy", [K["um"][3]], T.DK[:, PAD + 1536:PAD + 2048], T.pv[:, 1536:2048]))
                 prev["pv"] = K["dk"]
                 K["nxa"].append(table(0))
             else:
                 next(find)
             next(find)
+            next(find)
             nq, told = server(t, own, vs, prev, aside1 if t == 1 else lambda k: None, lambda: next(find))
-            slots, tabs = T.NXA[:, 0:2048].indirect(L("OR", t, 6, 14)), [told] + K["nxa"]
         sl = K["sl"]
-        was = V("copy", [node], T.ND[:, 64 * t:64 * t + 64], n[:, 128:192])
-        g1 = V("copy", tabs + [("rc%d" % t, LIST)], n[:, 0:128], slots)
+        was = S(T.ND[:, 64 * t:64 * t + 64], n[:, 128:192], [node], 63.5, 1.0 / FINE, f=F.Identity)
+        if t == 0:
+            g1 = numbered(n[:, 0:128], L("OR", 0, 6, 14), [told, ("rc0", LIST)])
+        else:
+            g1 = V("copy", [told, ("rc%d" % t, LIST)] + K["nxa"], n[:, 0:128], T.NXA[:, 0:2048].indirect(L("OR", t, 6, 14)))
         byq = n[:, 0:192].indirect(L("SL", t, 0, 4))
         got = [sl, ("rq%d" % t, COLS)]
         if t + 1 == HOPS:
-            nd = V("copy", [g1, sl, node], T.ND[:, 64 * HOPS:64 * HOPS + 64], byq)
+            nd = V("ts", [g1, sl, node], T.ND[:, 64 * HOPS:64 * HOPS + 64], byq, 1.0 / FINE, 63.5, A.mult, A.add)
             DMA("y", "dout", T.nd[:, :], T.ND[0:1, 0:256], [nd, was])
             hq = order(t, held, nq, got, T.cHQ3, T.sHQ3, 0)
             break
-        bt = V("ts", [g1, sl, node], T.BT[:, :], byq, 7, None, A.logical_shift_right)
+        node = V("copy", [g1, sl, node], T["NN%d" % (t + 1)][:, 128:192], byq)
 
         def gap(k):
-            if k == 0:
-                K["node"] = V("copy", [g1, sl, node], T["NN%d" % (t + 1)][:, 128:192], byq)
-            if k == 2:
-                K["vt"] = V("ts", [K["node"]], T.VT[:, :], T["NN%d" % (t + 1)][:, 128:192], 127, None, A.bitwise_and)
             if k == 4:
                 K["held"] = order(t, held, nq, got, T["cRW%d" % (t + 1)], T["sRW%d" % (t + 1)], HELD)
 
-        al = lists(t + 1, bt, gap)
-        held, node = K["held"], K["node"]
+        al = lists(t + 1, node, gap)
+        held = K["held"]
         own = depart(t + 1, al, held)
         vd = diag(t + 1, al)
         find = where(t + 1)
         next(find)
-        vs = tell(t + 1, run(vd))
+        ve = run(vd)
+        next(find)
+        vs = tell(t + 1, ve)
 
     DMA("y", "dout", T.oc[:, :], by(T.cHQ3, 0, 64), [hq[0]])
     for k in range(4):

@@ -1,27 +1,26 @@
 from concourse.bass import DstId, RemoteDMATransfer
-from concourse.mybir import dt, AluOpType as A, AxisListType, ActivationFunctionType as F
+from concourse.mybir import dt, AluOpType as A, ActivationFunctionType as F
 
 NR, CAP, HOPS = 4, 32, 3
 BIG = 1e29
 CUTS = (0, 128, 256, 384, 512)
 HELD = 224
-FINE = 2.0 ** -15
-COARSE = 1.5 * 2.0 ** 15
+FINE = 2.0 ** -7
 PAD = 1536
 EW = 514
 
 SCRATCH = {
-    "STW": ("sbuf", [128, 4], "int32"), "STU": ("sbuf", [128, 4], "uint16"),
+    "STW": ("sbuf", [128, 4], "int32"), "STU": ("sbuf", [128, 4], "uint16"), "STR": ("sbuf", [128, 16], "uint16"),
     "NXD": ("dram", [128, 4], "int32"), "NXR0": ("dram", [128, 4], "int32"), "NXR1": ("dram", [128, 4], "int32"), "NXR2": ("dram", [128, 4], "int32"),
     "NXW": ("sbuf", [128, 96], "int32"), "NXV": ("sbuf", [128, 32], "int32"), "NXU": ("sbuf", [128, 128], "uint16"), "NXA": ("sbuf", [128, 2048], "float32"),
-    "NODF": ("sbuf", [128, 512], "float32"),
+    "NODF": ("sbuf", [128, 512], "float32"), "RB": ("sbuf", [128, 256], "bfloat16"),
     "R16": ("sbuf", [128, 256], "bfloat16"), "ID": ("sbuf", [128, 128], "bfloat16"),
     "PI": ("sbuf", [128, 8], "int32"), "THR": ("sbuf", [128, 8], "float32"),
-    "XI": ("sbuf", [128, 8], "int32"), "XF": ("sbuf", [128, 8], "float32"), "XL": ("sbuf", [128, 8], "uint16"),
+    "XI": ("sbuf", [128, 16], "int32"), "XF": ("sbuf", [128, 8], "float32"), "XL": ("sbuf", [128, 16], "uint16"),
     "IO4": ("sbuf", [128, 8], "int32"), "AW": ("sbuf", [128, 16], "float32"),
     "IO": ("sbuf", [128, 32], "float32"), "C16": ("sbuf", [128, 16], "float32"),
     "D16B": ("sbuf", [128, 256], "bfloat16"), "NM64": ("sbuf", [128, 64], "float32"),
-    "RS64": ("sbuf", [128, 576], "bfloat16"), "RS16B": ("sbuf", [128, 256], "bfloat16"),
+    "RS64": ("sbuf", [128, 256 + EW], "bfloat16"), "RS16B": ("sbuf", [128, 256], "bfloat16"),
     "RK": ("sbuf", [128, 768], "bfloat16"), "UP": ("sbuf", [128, 128], "bfloat16"),
     "AL": ("sbuf", [128, 48], "uint16"),
     "VL": ("sbuf", [128, 48], "float32"),
@@ -55,9 +54,10 @@ for _t in range(HOPS):
     for _n, _w in (("LA", 224), ("RW", 288 if _t else 352)):
         _codes(_n + str(_t), _w)
     SCRATCH["NN%d" % _t] = ("sbuf", [128, 192], "float32")
+    SCRATCH["NK%d" % _t] = ("sbuf", [128, 192], "int32")
 SEMAPHORES = ["cv", "cs", "ct", "cg", "ls", "dst", "dx", "dno", "dnx", "dnd", "nxr", "dky", "dw", "dh3", "dout"]
 for _t in range(HOPS):
-    SEMAPHORES += ["aq%d" % _t, "av%d" % _t, "rq%d" % _t, "rc%d" % _t]
+    SEMAPHORES += ["aq%d" % _t, "av%d" % _t, "rq%d" % _t, "rs%d" % _t, "rc%d" % _t]
 
 
 def rank_program(g, core, T, topo):
@@ -91,8 +91,7 @@ def rank_program(g, core, T, topo):
         return tok
 
     v = g.vector
-    getv = {"copy": v.tensor_copy, "tt": v.tensor_tensor, "ts": v.tensor_scalar, "red": v.tensor_reduce, "scan": v.tensor_tensor_scan,
-            "set": v.memset, "q": v.quantize_mx}
+    getv = {"copy": v.tensor_copy, "tt": v.tensor_tensor, "ts": v.tensor_scalar, "scan": v.tensor_tensor_scan, "set": v.memset, "q": v.quantize_mx}
 
     def V(name, deps, *args):
         need("v", deps)
@@ -132,7 +131,7 @@ def rank_program(g, core, T, topo):
         e = topo.engines(cores[s], cores[r])
         q = len(e) // 4
         ev, od = e[0::2], e[1::2]
-        return ((ev[:q], od[q:]), (ev[q:], od[:q]), (od[:q], ev[:q]))[others.index(r)]
+        return ((ev[:q], od[q:]), (ev[q:], od[:q]), (od, ev))[others.index(r)]
 
     def bits(es):
         m = 0
@@ -145,7 +144,7 @@ def rank_program(g, core, T, topo):
         return DstId(rid=rid, pnc=pid)
 
     LIST = sum(len(part(r, me)) for r in peers)
-    COLS = sum(len(lanes(r, me)[0]) + len(lanes(r, me)[1]) for r in peers)
+    CODES, SCALES = (sum(len(lanes(r, me)[k]) for r in peers) for k in range(2))
 
     def fused(tr):
         g.remote_dma_fused(tr, local_sem=T.sem.ls)
@@ -165,13 +164,13 @@ def rank_program(g, core, T, topo):
     def by(x, a, b):
         return x[:, a:b].bitcast(dt.uint8)
 
-    def sendcols(sem, name, src, dst, codes, scales):
+    def sendcols(sem, sem2, name, src, dst, codes, scales):
         C, P = T["c" + name], T["s" + name]
         need("g", [codes])
         fused([one(r, bits(lanes(me, r)[0]), sem, by(C, src + 32 * b, src + 32 * b + 32), by(C, dst + 32 * there(r), dst + 32 * there(r) + 32))
                for b, r in enumerate(peers)])
         need("g", [scales])
-        fused([one(r, bits(lanes(me, r)[1]), sem, P[:, src + 32 * b:src + 32 * b + 32], P[:, dst + 32 * there(r):dst + 32 * there(r) + 32])
+        fused([one(r, bits(lanes(me, r)[1]), sem2, P[:, src + 32 * b:src + 32 * b + 32], P[:, dst + 32 * there(r):dst + 32 * there(r) + 32])
                for b, r in enumerate(peers)])
         count["ls"] = count.get("ls", 0) + sum(len(lanes(me, r)[0]) + len(lanes(me, r)[1]) for r in peers)
 
@@ -193,50 +192,47 @@ def rank_program(g, core, T, topo):
         d_no = DMA("y", "dno", T.NXV[16 * k:16 * k + 16, 0:32], T.nx[:, :])
     d_w = DMA("y", "dw", T.WT[:, :], T.w[:, :])
 
-    IOTA(T.PI[:, 0:1], [[0, 1]], 4, 4)
-    i_pi = IOTA(T.PI[:, 1:3], [[-64, 2]], 0, 1)
+    IOTA(T.PI[:, 0:2], [[4, 2]], 0, 4)
+    i_pi = IOTA(T.PI[:, 2:4], [[-64, 2]], 0, 1)
+    i_r16 = IOTA(T.R16[:, :], [[0, 16], [1, 16]], 0, 0, True)
     K["nf"] = IOTA(T.NODF[:, :], [[1, 512]], 0, 0, True)
-    i_r16 = IOTA(T.R16[:, :], [[0, 16], [1, 16]], 1, 0, True)
     need("g", [d_nd])
     e16 = topo.engines(core, cores[peers[0]])
     fused([RemoteDMATransfer(dst_ids=[coreid(r) for r in peers], dma_engine_mask=bits(e16), remote_sem=T.sem.nxr, srcs=[T.NXD[:, :]],
                              dsts=[T["NXR%d" % there(r)][:, :] for r in peers])])
     count["ls"] = len(e16)
 
-    m_rs = V("set", [], T.RS64[:, 0:EW], 1.0)
+    m_1 = V("set", [], T.RS64[:, :], 1.0)
     m_up = V("set", [], T.MD[:, 0:128], 1.0 / 64)
-    k_pj = V("ts", [i_pi], T.XI[:, 4:5], T.PI[:, 1:2], 15, None, A.bitwise_and)
-    m_rs = V("set", [m_rs], T.RS64[:, 0:256:64], 0.0)
     K["cn"] = V("set", [], T.CN[:, 0:544:272], 0.0)
-    k_t0 = V("ts", [k_pj], T.THR[:, 0:1], T.XI[:, 4:5], 1.0, None, A.add)
-    k_t1 = V("ts", [k_pj], T.THR[:, 1:2], T.XI[:, 4:5], 17.0, None, A.add)
+    k_pj = V("ts", [i_pi], T.XI[:, 5:6], T.PI[:, 2:3], 15, None, A.bitwise_and)
+    x_3 = V("ts", [i_pi], T.XI[:, 8:9], T.PI[:, 2:3], 3, None, A.bitwise_and)
+    m_rs = V("set", [m_1], T.RS64[:, 0:256:64], 0.0)
+    k_t0 = V("ts", [k_pj], T.THR[:, 0:1], T.XI[:, 5:6], 1.0, None, A.add)
+    k_t1 = V("ts", [k_pj], T.THR[:, 1:2], T.XI[:, 5:6], 17.0, None, A.add)
+    x_3 = V("copy", [x_3], T.XL[:, 8:9], T.XI[:, 8:9])
     K["up"] = V("scan", [m_rs, m_up], T.UP[:, :], T.RS64[:, 0:128], T.MD[:, 0:128], 0.0, A.mult, A.add)
     K["rk"] = [V("ts", [m_rs, k], T.RK[:, 256 * h:256 * h + 128], T.RS64[:, 0:128], 0.0, T.THR[:, h:h + 1], A.is_equal, A.mult)
                for h, k in enumerate((k_t0, k_t1))]
-    x_g = V("ts", [i_pi], T.XI[:, 0:2], T.PI[:, 1:3], 0xFFF0, None, A.bitwise_and)
-    x_u = V("ts", [i_pi], T.XI[:, 2:4], T.PI[:, 0:2], 12, None, A.bitwise_and)
-    K["xm"] = V("set", [], T.RM[:, 0:1], BIG)
-    x_u = V("ts", [x_u], T.XF[:, 0:2], T.XI[:, 2:4], 4.0, None, A.mult)
-    k_id = SEL(T.ID[:, :], T.RS64[:, 256:384], [[-1, 128]], A.is_equal, 0, 1, [m_rs])
+    k_id = SEL(T.ID[:, :], T.RS64[:, 256:384], [[-1, 128]], A.is_equal, 0, 1, [m_1])
     i_io4 = IOTA(T.IO4[:, 0:4], [[1, 4]], -512 * me, 0)
 
-    m_xt = S(T.XT[:, 256:512], T.RS64[:, 0:256], [m_rs], 0.0, 0.0)
+    for i in range(4):
+        K["rc"] = S(T.RB[:, 64 * i:64 * i + 64], T.RS64[:, 256:320], [m_1], float((me + i) % NR), 0.0, f=F.Identity)
+    m_xt = S(T.XT[:, 256:512], T.RS64[:, 256:512], [m_1], 0.0, 0.0)
     for h in range(2):
-        m_e = S(T.ET[:, EW * h:EW * h + EW], T.RS64[:, 0:EW], [m_rs], 0.0, 0.0)
-    K["r16"] = S(T.RS16B[:, :], T.R16[:, :], [i_r16], -1.0, f=F.Sign)
+        m_e = S(T.ET[:, EW * h:EW * h + EW], T.RS64[:, 256:256 + EW], [m_1], 0.0, 0.0)
+    K["r16"] = S(T.RS16B[:, :], T.R16[:, :], [i_r16], f=F.Sign)
 
-    def lists(t, node, gap):
-        n = T["NN%d" % t][:, 128:192]
+    def lists(t, deps, ranks, gap):
         gap(0)
-        mk = [V("ts", [node], T.MK[:, 64 * i:64 * i + 64], n, COARSE, COARSE + ((me + i) % NR) / 256.0, A.add, A.is_equal) for i in range(4)]
-        gap(1)
+        mk = [V("tt", deps, T.MK[:, 128 * u:128 * u + 128], ranks(u), T.RB[:, 128 * u:128 * u + 128], A.is_equal) for u in range(2)]
         px, sc = {}, {}
         for u in range(2):
             for h in range(2):
                 o = 272 * h + 128 * u + 1
-                px[h, u] = V("scan", [mk[2 * u + 1], K["rk"][h]], T.CN[:, o:o + 128], T.RK[:, 256 * h:256 * h + 128], T.MK[:, 128 * u:128 * u + 128],
+                px[h, u] = V("scan", [mk[u], K["rk"][h]], T.CN[:, o:o + 128], T.RK[:, 256 * h:256 * h + 128], T.MK[:, 128 * u:128 * u + 128],
                              0.0, A.max, A.subtract)
-        gap(2)
         for u in range(2):
             for h in range(2):
                 o = 272 * h + 128 * u
@@ -249,7 +245,7 @@ def rank_program(g, core, T, topo):
         return al
 
     def diag(t, al):
-        return V("tt", [al, K["d16"]], T.VD[:, :], T["NN%d" % t][:, 128:192].indirect(L("AL", t, 0, 8)), T.D16B[:, 0:128], A.mult)
+        return V("tt", [al, K["d16"], K["node"]], T.VD[:, :], T["NN%d" % t][:, 128:192].indirect(L("AL", t, 0, 8)), T.D16B[:, 0:128], A.mult)
 
     def run(vd):
         return V("scan", [vd, K["r16"]], T.VE[:, :], T.RS16B[:, 0:128], T.VD[:, :], 0.0, A.mult, A.add)
@@ -258,7 +254,7 @@ def rank_program(g, core, T, topo):
         c, s = T["cRW%d" % t], T["sRW%d" % t]
         p2 = S(T["sLA%d" % t][:, 96:224], s[:, HELD:HELD + 64].indirect(L("AL", t, 0, 8)), [al, held[-1]])
         p1 = V("copy", [al, held[0]], wd(T["cLA%d" % t], 96, 224), wd(c, HELD, HELD + 64).indirect(L("AL", t, 0, 8)))
-        sendcols("aq%d" % t, "LA%d" % t, 128, 0, p1, p2)
+        sendcols("aq%d" % t, "aq%d" % t, "LA%d" % t, 128, 0, p1, p2)
         return [p1, p2]
 
     def tell(t, ve):
@@ -272,7 +268,7 @@ def rank_program(g, core, T, topo):
     def server(t, own, vs, prev, aside, step):
         KQ, sKQ = T.cKQ, T.sKQ
         LA, sLA = T["cLA%d" % t], T["sLA%d" % t]
-        land = [("aq%d" % t, COLS)] + own + [K["kq"]]
+        land = [("aq%d" % t, CODES + SCALES)] + own + [K["kq"]]
         z = []
 
         def zout(i):
@@ -287,13 +283,14 @@ def rank_program(g, core, T, topo):
             return T.ZS[:, CUTS[i]:CUTS[i + 1]], zout(i)
 
         def half(b):
-            return MM(T.pv[:, 512 * b:512 * b + 128], *eq(b), LA[:, 0:128], sLA[:, 0:128], True, t > 0, [K["eq"], prev["pv"][b]])
+            return MM(T.pv[:, 512 * b:512 * b + 128], *eq(b), LA[:, 0:128], sLA[:, 0:128], True, t > 0, [K["eq", b], prev["pv"][b]])
 
         dq = [half(b) for b in range(2)]
         c0 = S(*zcopy(0), [z[0], prev["t64"]])
         c2 = S(*zcopy(2), [z[2]])
         if t > 0:
             d = [S(T.DQ[:, 128 * b:128 * b + 128], T.pv[:, 512 * b:512 * b + 128], [dq[b], prev["ht"]]) for b in range(2)]
+        K["was"] = S(T.ND[:, 64 * t:64 * t + 64], T["NN%d" % t][:, 128:192], [K["node"]], 63.5, 1.0 / FINE, f=F.Identity)
         aside(3)
         vp = V("copy", [vs, K["xl"], ("av%d" % t, LIST)], T.VP[:, :], L("VL", t, 0, 10).indirect(T.XL[:, 2:3]))
         c1 = V("copy", [z[1]], *zcopy(1))
@@ -309,6 +306,8 @@ def rank_program(g, core, T, topo):
         xm = MM(T.px[:, 0:128], T.cSQ[:, 0:128], T.sSQ[:, 0:128], T.cXQ[:, 0:128], T.sXQ[:, 0:128], True, True, [xq, K["sq"], c3])
         dq += [half(b) for b in range(2, 4)]
         aside(0)
+        if t + 1 < HOPS:
+            K["r0"] = V("copy", [K["node"]], T["NK%d" % t][:, 128:192], T["NN%d" % t][:, 128:192])
         step()
         of = V("tt", [xm], T.OF[:, :], T.px[:, 0:8], L("VL", t, 2, 10), A.add)
         step()
@@ -320,8 +319,8 @@ def rank_program(g, core, T, topo):
         step()
         if t == 0:
             ks = S(T.sKC[:, 0:128], sKQ[:, 0:512].indirect(T.OU[:, 0:8]), [ou, K["kq"]])
-            kc = V("copy", [ou], wd(T.cKC, 0, 128), wd(KQ, 0, 512).indirect(T.OU[:, 0:8]))
             nd = V("tt", [ou, K["t3"], K["d16"]], T.VD[:, :], T.NXA[:, 512 * me:512 * me + 512].indirect(T.OU[:, 0:8]), T.D16B[:, 0:128], A.mult)
+            kc = V("copy", [ou], wd(T.cKC, 0, 128), wd(KQ, 0, 512).indirect(T.OU[:, 0:8]))
             ne = run(nd)
             step()
             told = V("ts", [ne], L("OR", t, 0, 8), T.VE[:, 15:128:16], 1.0 / FINE, 63.5, A.mult, A.add)
@@ -346,8 +345,9 @@ def rank_program(g, core, T, topo):
                      for b in range(2)]
             h = d + ready
             ht = ready[1]
+        step()
         nq = V("q", ready, T["cRW%d" % t][:, 0:128], T["sRW%d" % t][:, 0:128], T.HT[:, :])
-        sendcols("rq%d" % t, "RW%d" % t, 0, 128, nq, nq)
+        sendcols("rq%d" % t, "rs%d" % t, "RW%d" % t, 0, 128, nq, nq)
         prev.update({"z": [c0, c1, c2, of], "pv": h, "t64": t64, "ht": ht, "xm": xm, "of": of, "nq": nq})
         aside(2)
         return nq, told
@@ -369,73 +369,86 @@ def rank_program(g, core, T, topo):
         yield None
         w8 = V("scan", [w5, K["aw"]], T.WW[:, 80:96], T.AW[:, :], T.WW[:, 64:80], 0.0, A.max, A.subtract)
         yield None
-        K["sl"] = V("copy", [w8], L("SL", t, 0, 4), T.WW[:, 83:96:4])
+        K["sl"] = V("copy", [w8, K["xj"]], L("SL", t, 0, 16), T.WW[:, 80:96].indirect(T.XL[:, 6:7]))
         while True:
             yield None
 
-    def order(t, held, nq, deps, c, s, o):
-        h2 = S(s[:, o:o + 64], T["sRW%d" % t][:, 96:288].indirect(L("SL", t, 0, 4)), [held[-1], nq] + deps)
-        h1 = V("copy", [held[0], nq] + deps, wd(c, o, o + 64), wd(T["cRW%d" % t], 96, 288).indirect(L("SL", t, 0, 4)))
+    def order(t, held, nq, sl, c, s, o):
+        h2 = S(s[:, o:o + 64], T["sRW%d" % t][:, 96:288].indirect(L("SL", t, 0, 4)), [held[-1], nq, sl, ("rs%d" % t, SCALES)])
+        h1 = V("copy", [held[0], nq, sl, ("rq%d" % t, CODES)], wd(c, o, o + 64), wd(T["cRW%d" % t], 96, 288).indirect(L("SL", t, 0, 4)))
         return [h1, h2]
 
-    def table(b):
+    def table(b, lo=0, hi=512):
         r = (me + 1 + b) % NR
-        return S(T.NXA[:, 512 * r:512 * r + 512], T.NODF[:, 0:512].indirect(T.NXU[:, 32 * b:32 * b + 32]), [K["no"] if b == 3 else K["nu"], K["nf"]],
-                 -63.5 * FINE, FINE, f=F.Identity)
+        return S(T.NXA[:, 512 * r + lo:512 * r + hi], T.NODF[:, 0:512].indirect(T.NXU[:, 32 * b + lo // 16:32 * b + hi // 16]),
+                 [K["no"] if b == 3 else K["nu"], K["nf"]], -63.5 * FINE, FINE, f=F.Identity)
 
     def dkc(b):
         K["dk"].append(S(T.DK[:, PAD + 512 * b:PAD + 512 * b + 512], T.pv[:, 512 * b:512 * b + 512], [K["um"][b]]))
 
-    def numbered(out, offsets, deps):
-        return V("ts", deps + [K["nf"]], out, T.NODF[:, 0:512].indirect(offsets), FINE, -63.5 * FINE, A.mult, A.add)
-
-    k_st = V("copy", [d_st], T.STU[:, :], T.STW[:, :])
-    V("ts", [x_g, x_u], T.XL[:, 0:2], T.XI[:, 0:2], T.XF[:, 1:2], T.XF[:, 0:1], A.is_equal, A.mult)
-    node = numbered(T.NN0[:, 128:192], T.STU[:, 0:4], [k_st])
+    k_sr = V("ts", [d_st, x_3], T.STR[:, :], T.STW[:, 0:4].indirect(T.XL[:, 8:9]), FINE, -63.5 * FINE, A.mult, A.add)
 
     def gap0(k):
         if k == 0:
-            K["xl"] = V("ts", [x_g], T.XL[:, 2:3], T.XI[:, 0:1], 1.0 / 16, 2.0, A.mult, A.add)
-        if k == 1:
-            K["d16"] = V("ts", [k_t0, i_r16], T.D16B[:, :], T.R16[:, :], T.THR[:, 0:1], None, A.is_equal)
-            for b in range(4):
-                K["st"] = S(T.ST[:, b:512:4], T.D16B[:, 0:128], [K["d16"]])
-            K["nm"] = S(T.NM64[:, :], T.D16B[:, 0:64], [K["d16"]], -BIG, BIG, f=F.Identity)
+            k_st = V("copy", [d_st], T.STU[:, :], T.STW[:, :])
+            K["d16"] = V("ts", [k_t0, i_r16], T.D16B[:, :], T.R16[:, :], 1.0, T.THR[:, 0:1], A.add, A.is_equal)
+            K["node"] = S(T.NN0[:, 128:192], T.NODF[:, 0:512].indirect(T.STU[:, 0:4]), [k_st, K["nf"]], -63.5 * FINE, FINE, f=F.Identity)
         if k == 4:
             K["held"] = [V("q", [d_x, m_xt], T.cRW0[:, HELD:HELD + 128], T.sRW0[:, HELD:HELD + 128], T.XT[:, :])]
+        if k == 5:
+            K["xg"] = V("ts", [i_pi], T.XI[:, 0:2], T.PI[:, 2:4], 0xFFF0, None, A.bitwise_and)
+            K["xv"] = V("ts", [i_pi], T.XI[:, 2:5], T.PI[:, 0:3], 12, None, A.bitwise_and)
 
-    al = lists(0, node, gap0)
-    held = K["held"]
+    al = lists(0, [k_sr, i_r16, K["rc"]], lambda u: T.R16[:, 0:16].indirect(T.STR[:, 8 * u:8 * u + 8]), gap0)
+    node, held, x_g, x_v = K["node"], K["held"], K["xg"], K["xv"]
     hq0 = held[0]
     own = depart(0, al, held)
     k_e = [S(T.ET[:, EW * h + 2 + h:EW * h + EW:4], T.ID[:, :], [m_e, k_id], 0.0, 0.5) for h in range(2)]
+    for b in range(4):
+        K["st"] = S(T.ST[:, b:512:4], T.D16B[:, 0:128], [K["d16"]])
+    K["nm"] = S(T.NM64[:, :], T.D16B[:, 0:64], [K["d16"]], -BIG, BIG, f=F.Identity)
     K["xs"] = S(T.XS[:, :], T.RS64[:, 0:512], [m_rs], 0.0, 0.0)
     vd = diag(0, al)
-    K["sq"] = V("q", [K["st"]], T.cSQ[:, 0:128], T.sSQ[:, 0:128], T.ST[:, :])
+    K["xm"] = V("set", [], T.RM[:, 0:1], BIG)
+    x_u = V("ts", [x_v], T.XF[:, 0:2], T.XI[:, 3:5], 4.0, None, A.mult)
     ve = run(vd)
-    x_k = V("ts", [k_pj], T.XI[:, 5:6], T.XI[:, 4:5], 68.0, None, A.mult)
+    V("ts", [x_g, x_u], T.XL[:, 0:2], T.XI[:, 0:2], T.XF[:, 1:2], T.XF[:, 0:1], A.is_equal, A.mult)
+    K["xl"] = V("ts", [x_g], T.XL[:, 2:3], T.XI[:, 0:1], 1.0 / 16, 2.0, A.mult, A.add)
     vs = tell(0, ve)
     i_16 = IOTA(T.IO[:, 0:16], [[16, 4], [-32, 4]], 63, 0, True)
     i_k16 = IOTA(T.IO[:, 16:32], [[16, 4], [-1024, 4]], 127, 0, True)
-    x_k = V("ts", [x_k], T.XI[:, 6:7], T.XI[:, 5:6], 0xF0, None, A.bitwise_and)
     K["kq"] = V("q", [d_ky], T.cKQ[:, 0:512], T.sKQ[:, 0:512], T.KT[:, :])
-    K["rb"] = V("ts", [], T.RK[:, 512:768], T.RS64[:, 0:256], 0.0, 65.0, A.is_equal, A.mult)
-    K["xk"] = V("ts", [x_k], T.XL[:, 4:5], T.XI[:, 6:7], 15.0, None, A.add)
 
     def unit(b):
         o = EW * (b % 2) + (2 if b < 2 else 0)
-        K["eq"] = V("q", [k_e[b % 2]], *eq(b), T.ET[:, o:o + 512])
+        K["eq", b] = V("q", [k_e[b % 2]], *eq(b), T.ET[:, o:o + 512])
 
-    find = where(0)
-    next(find)
-    next(find)
-    unit(0)
-    next(find)
-    unit(2)
-    next(find)
-    unit(1)
-    unit(3)
     K["no"] = V("copy", [d_no], T.NXU[:, 96:128], T.NXV[:, :])
+    unit(0)
+    unit(1)
+    K["sq"] = V("q", [K["st"]], T.cSQ[:, 0:128], T.sSQ[:, 0:128], T.ST[:, :])
+    find = where(0)
+    K["rb"] = V("ts", [], T.RK[:, 512:768], T.RS64[:, 0:256], 0.0, 65.0, A.is_equal, A.mult)
+    next(find)
+
+    def links0():
+        unit(2)
+        next(find)
+        yield None
+        unit(3)
+        x_k = V("ts", [k_pj], T.XI[:, 6:7], T.XI[:, 5:6], 68.0, None, A.mult)
+        yield None
+        next(find)
+        x_k = V("ts", [x_k], T.XI[:, 7:8], T.XI[:, 6:7], 0xF0, None, A.bitwise_and)
+        yield None
+        next(find)
+        K["xk"] = V("ts", [x_k], T.XL[:, 4:5], T.XI[:, 7:8], 15.0, None, A.add)
+        K["xj"] = V("ts", [x_v], T.XL[:, 6:7], T.XI[:, 2:3], 3.0, None, A.add)
+        yield None
+        while True:
+            yield next(find)
+
+    rest = links0()
     for b in range(3):
         for k in range(8):
             d_nx = DMA("y", "dnx", T.NXW[16 * k:16 * k + 16, 32 * b:32 * b + 32], T["NXR%d" % b][:, :], [("nxr", 3 * len(e16))])
@@ -445,6 +458,8 @@ def rank_program(g, core, T, topo):
     K["aw"] = S(T.AW[:, :], T.IO[:, 16:32], [i_k16, k_t0], T.THR[:, 0:1], f=F.Identity)
 
     def aside0(k):
+        if k == 1:
+            next(find)
         if k == 3:
             K["t3"] = table(3)
         if k == 2:
@@ -457,49 +472,49 @@ def rank_program(g, core, T, topo):
 
     def aside1(k):
         if k == 3:
-            K["nxa"].append(table(1))
+            K["nxa"] += [table(1, 256, 512), table(2, 0, 256)]
         if k == 1:
-            K["nxa"].append(table(2))
-        if k == 2:
+            K["nxa"].append(table(2, 256, 512))
+        if k == 0:
             K["wq"] = V("q", [d_w], T.cWQ[:, 0:128], T.sWQ[:, 0:128], T.WT[:, :])
 
     prev = {"z": [None] * 4, "pv": [None] * 4, "t64": None, "ht": None, "xm": None, "of": None, "nq": None}
     for t in range(HOPS):
         n = T["NN%d" % t]
         if t == 0:
-            nq, told = server(0, own, vs, prev, aside0, lambda: next(find))
+            nq, told = server(0, own, vs, prev, aside0, lambda: next(rest))
         else:
             if t == 1:
                 dkc(2)
                 next(find)
                 K["dk"].append(V("copy", [K["um"][3]], T.DK[:, PAD + 1536:PAD + 2048], T.pv[:, 1536:2048]))
                 prev["pv"] = K["dk"]
-                K["nxa"].append(table(0))
+                K["nxa"] += [table(0), table(1, 0, 256)]
             else:
                 next(find)
             next(find)
             next(find)
             nq, told = server(t, own, vs, prev, aside1 if t == 1 else lambda k: None, lambda: next(find))
         sl = K["sl"]
-        was = S(T.ND[:, 64 * t:64 * t + 64], n[:, 128:192], [node], 63.5, 1.0 / FINE, f=F.Identity)
-        if t == 0:
-            g1 = numbered(n[:, 0:128], L("OR", 0, 6, 14), [told, ("rc0", LIST)])
-        else:
-            g1 = V("copy", [told, ("rc%d" % t, LIST)] + K["nxa"], n[:, 0:128], T.NXA[:, 0:2048].indirect(L("OR", t, 6, 14)))
+        tab, tabs, scale, bias = (T.NODF[:, 0:512], [], FINE, -63.5 * FINE) if t == 0 else (T.NXA[:, 0:2048], K["nxa"], 1.0, 0.0)
+        slots, tabs = tab.indirect(L("OR", t, 6, 14)), tabs + [told, ("rc%d" % t, LIST)]
         byq = n[:, 0:192].indirect(L("SL", t, 0, 4))
-        got = [sl, ("rq%d" % t, COLS)]
         if t + 1 == HOPS:
+            g1 = V("copy", tabs, n[:, 0:128], slots)
             nd = V("ts", [g1, sl, node], T.ND[:, 64 * HOPS:64 * HOPS + 64], byq, 1.0 / FINE, 63.5, A.mult, A.add)
-            DMA("y", "dout", T.nd[:, :], T.ND[0:1, 0:256], [nd, was])
-            hq = order(t, held, nq, got, T.cHQ3, T.sHQ3, 0)
+            DMA("y", "dout", T.nd[:, :], T.ND[0:1, 0:256], [nd, K["was"]])
+            hq = order(t, held, nq, sl, T.cHQ3, T.sHQ3, 0)
             break
-        node = V("copy", [g1, sl, node], T["NN%d" % (t + 1)][:, 128:192], byq)
+        nk = T["NK%d" % t]
+        g1 = S(n[:, 0:128], slots, tabs, bias, scale, f=F.Identity)
+        r1 = V("ts", tabs, nk[:, 0:128], slots, scale, bias, A.mult, A.add)
+        node = K["node"] = S(T["NN%d" % (t + 1)][:, 128:192], byq, [g1, sl, node])
 
         def gap(k):
             if k == 4:
-                K["held"] = order(t, held, nq, got, T["cRW%d" % (t + 1)], T["sRW%d" % (t + 1)], HELD)
+                K["held"] = order(t, held, nq, sl, T["cRW%d" % (t + 1)], T["sRW%d" % (t + 1)], HELD)
 
-        al = lists(t + 1, node, gap)
+        al = lists(t + 1, [K["r0"], r1, sl], lambda u: nk[:, 0:192].indirect(L("SL", t, 8 * u, 8 * u + 8)), gap)
         held = K["held"]
         own = depart(t + 1, al, held)
         vd = diag(t + 1, al)

@@ -3,40 +3,42 @@ from concourse.mybir import dt, AluOpType as A, ActivationFunctionType as F
 
 NR, CAP, HOPS = 4, 32, 3
 BIG = 1e29
-CUTS = (0, 128, 256, 384, 512)
+CUTS = (0, 192, 384, 512)
 HELD = 224
 FINE = 2.0 ** -7
+WHOLE = 1.5 * 2.0 ** 23
 PAD = 1536
 EW = 514
 
 SCRATCH = {
-    "STW": ("sbuf", [128, 4], "int32"), "STU": ("sbuf", [128, 4], "uint16"), "STR": ("sbuf", [128, 16], "uint16"),
+    "STW": ("sbuf", [128, 4], "int32"), "STU": ("sbuf", [128, 4], "uint16"), "STR": ("sbuf", [128, 4], "uint16"),
     "NXD": ("dram", [128, 4], "int32"), "NXR0": ("dram", [128, 4], "int32"), "NXR1": ("dram", [128, 4], "int32"), "NXR2": ("dram", [128, 4], "int32"),
     "NXW": ("sbuf", [128, 96], "int32"), "NXV": ("sbuf", [128, 32], "int32"), "NXU": ("sbuf", [128, 128], "uint16"), "NXA": ("sbuf", [128, 2048], "float32"),
-    "NODF": ("sbuf", [128, 512], "float32"), "RB": ("sbuf", [128, 256], "bfloat16"),
+    "NODF": ("sbuf", [128, 512], "float32"), "NODR": ("sbuf", [128, 512], "float32"),
     "R16": ("sbuf", [128, 256], "bfloat16"), "ID": ("sbuf", [128, 128], "bfloat16"),
-    "PI": ("sbuf", [128, 8], "int32"), "THR": ("sbuf", [128, 8], "float32"),
-    "XI": ("sbuf", [128, 16], "int32"), "XF": ("sbuf", [128, 8], "float32"), "XL": ("sbuf", [128, 16], "uint16"),
-    "IO4": ("sbuf", [128, 8], "int32"), "AW": ("sbuf", [128, 16], "float32"),
+    "PI": ("sbuf", [128, 4], "int32"), "THR": ("sbuf", [128, 8], "float32"),
+    "XI": ("sbuf", [128, 8], "int32"), "XF": ("sbuf", [128, 4], "float32"), "XL": ("sbuf", [128, 8], "uint16"),
+    "IO4": ("sbuf", [128, 4], "int32"), "IQ": ("sbuf", [128, 4], "float32"), "AW": ("sbuf", [128, 16], "float32"),
     "IO": ("sbuf", [128, 32], "float32"), "C16": ("sbuf", [128, 16], "float32"),
     "D16B": ("sbuf", [128, 256], "bfloat16"), "NM64": ("sbuf", [128, 64], "float32"),
     "RS64": ("sbuf", [128, 256 + EW], "bfloat16"), "RS16B": ("sbuf", [128, 256], "bfloat16"),
     "RK": ("sbuf", [128, 768], "bfloat16"), "UP": ("sbuf", [128, 128], "bfloat16"),
+    "M8": ("sbuf", [128, 8], "float32"), "TB": ("sbuf", [128, 512], "bfloat16"),
     "AL": ("sbuf", [128, 48], "uint16"),
     "VL": ("sbuf", [128, 48], "float32"),
     "Z4": ("sbuf", [128, 48], "uint16"),
-    "OU": ("sbuf", [128, 16], "uint16"),
+    "OU": ("sbuf", [128, 8], "uint16"),
     "OR": ("sbuf", [128, 48], "uint16"),
     "SL": ("sbuf", [128, 48], "uint16"),
     "MK": ("sbuf", [128, 256], "bfloat16"), "PX": ("sbuf", [128, 256], "bfloat16"),
     "CN": ("sbuf", [128, 544], "bfloat16"), "SC": ("sbuf", [128, 512], "bfloat16"), "VD": ("sbuf", [128, 128], "float32"), "VE": ("sbuf", [128, 128], "float32"),
     "MD": ("sbuf", [128, 256], "bfloat16"), "UD": ("sbuf", [128, 256], "bfloat16"), "FF": ("sbuf", [128, 256], "bfloat16"),
     "WW": ("sbuf", [128, 96], "float32"), "ND": ("sbuf", [128, 256], "float32"),
-    "VP": ("sbuf", [128, 16], "float32"),
+    "VP": ("sbuf", [128, 16], "float32"), "VU": ("sbuf", [128, 8], "uint16"), "VB": ("sbuf", [128, 256], "bfloat16"),
     "ZS": ("sbuf", [128, 512], "float32"), "T64": ("sbuf", [128, 64], "float32"),
-    "RM": ("sbuf", [128, 72], "float32"),
-    "XS": ("sbuf", [128, 512], "bfloat16"), "OF": ("sbuf", [128, 8], "float32"), "HT": ("sbuf", [128, 512], "bfloat16"),
-    "DK": ("sbuf", [128, PAD + 2048], "float32"), "DQ": ("sbuf", [128, 256], "float32"), "GK": ("sbuf", [128, 256], "float32"),
+    "RM": ("sbuf", [128, 64], "float32"),
+    "HT": ("sbuf", [128, 512], "bfloat16"),
+    "DK": ("sbuf", [128, PAD + 2048], "float32"), "DQ": ("sbuf", [128, 320], "float32"), "GK": ("sbuf", [128, 192], "float32"),
     "XT": ("sbuf", [128, 512], "bfloat16"), "KT": ("sbuf", [128, 2048], "bfloat16"), "WT": ("sbuf", [128, 512], "bfloat16"),
     "ET": ("sbuf", [128, 2 * EW], "bfloat16"), "ST": ("sbuf", [128, 512], "bfloat16"), "YS": ("sbuf", [128, 64], "float32"),
     "pv": ("psum", [128, 2048], "float32"), "pz": ("psum", [128, 1536], "float32"), "px": ("psum", [128, 512], "float32"),
@@ -54,8 +56,8 @@ for _t in range(HOPS):
     for _n, _w in (("LA", 224), ("RW", 288 if _t else 352)):
         _codes(_n + str(_t), _w)
     SCRATCH["NN%d" % _t] = ("sbuf", [128, 192], "float32")
-    SCRATCH["NK%d" % _t] = ("sbuf", [128, 192], "int32")
-SEMAPHORES = ["cv", "cs", "ct", "cg", "ls", "dst", "dx", "dno", "dnx", "dnd", "nxr", "dky", "dw", "dh3", "dout"]
+    SCRATCH["NK%d" % _t] = ("sbuf", [128, 192], "float32")
+SEMAPHORES = ["cv", "cs", "ct", "cg", "ls", "dst", "dx", "dno", "dnx", "dn0", "dnd", "nxr", "dk0", "dk1", "dk2", "dw", "dh3", "dout"]
 for _t in range(HOPS):
     SEMAPHORES += ["aq%d" % _t, "av%d" % _t, "rq%d" % _t, "rs%d" % _t, "rc%d" % _t]
 
@@ -186,14 +188,11 @@ def rank_program(g, core, T, topo):
         d_st = DMA("y" if k % 2 == 0 else "s", "dst", T.STW[16 * k:16 * k + 16, 0:4], T.st[:, :])
     d_nd = DMA("s", "dnd", T.NXD[:, :], T.nx[:, :])
     d_x = DMA("y", "dx", T.XT[:, 0:256], T.x[:, :])
-    d_ky = DMA("s", "dky", T.KT[:, 0:1024], T.ky[:, 0:1024])
-    d_ky = DMA("y", "dky", T.KT[:, 1024:2048], T.ky[:, 1024:2048])
+    d_ky = [DMA("sys"[i], "dk%d" % i, T.KT[:, 4 * CUTS[i]:4 * CUTS[i + 1]], T.ky[:, 4 * CUTS[i]:4 * CUTS[i + 1]]) for i in range(3)]
     for k in range(8):
         d_no = DMA("y", "dno", T.NXV[16 * k:16 * k + 16, 0:32], T.nx[:, :])
-    d_w = DMA("y", "dw", T.WT[:, :], T.w[:, :])
 
-    IOTA(T.PI[:, 0:2], [[4, 2]], 0, 4)
-    i_pi = IOTA(T.PI[:, 2:4], [[-64, 2]], 0, 1)
+    i_pi = IOTA(T.PI[:, 0:1], [[0, 1]], 0, 1)
     i_r16 = IOTA(T.R16[:, :], [[0, 16], [1, 16]], 0, 0, True)
     K["nf"] = IOTA(T.NODF[:, :], [[1, 512]], 0, 0, True)
     need("g", [d_nd])
@@ -204,35 +203,40 @@ def rank_program(g, core, T, topo):
 
     m_1 = V("set", [], T.RS64[:, :], 1.0)
     m_up = V("set", [], T.MD[:, 0:128], 1.0 / 64)
+    k_pj = V("ts", [i_pi], T.XI[:, 5:6], T.PI[:, 0:1], 15, None, A.bitwise_and)
     K["cn"] = V("set", [], T.CN[:, 0:544:272], 0.0)
-    k_pj = V("ts", [i_pi], T.XI[:, 5:6], T.PI[:, 2:3], 15, None, A.bitwise_and)
-    x_3 = V("ts", [i_pi], T.XI[:, 8:9], T.PI[:, 2:3], 3, None, A.bitwise_and)
+    V("set", [], T.TB[64:128, 384:512], 0.0)
     m_rs = V("set", [m_1], T.RS64[:, 0:256:64], 0.0)
     k_t0 = V("ts", [k_pj], T.THR[:, 0:1], T.XI[:, 5:6], 1.0, None, A.add)
     k_t1 = V("ts", [k_pj], T.THR[:, 1:2], T.XI[:, 5:6], 17.0, None, A.add)
-    x_3 = V("copy", [x_3], T.XL[:, 8:9], T.XI[:, 8:9])
+    x_g = V("ts", [i_pi], T.XI[:, 0:1], T.PI[:, 0:1], 0xFFF0, None, A.bitwise_and)
     K["up"] = V("scan", [m_rs, m_up], T.UP[:, :], T.RS64[:, 0:128], T.MD[:, 0:128], 0.0, A.mult, A.add)
     K["rk"] = [V("ts", [m_rs, k], T.RK[:, 256 * h:256 * h + 128], T.RS64[:, 0:128], 0.0, T.THR[:, h:h + 1], A.is_equal, A.mult)
                for h, k in enumerate((k_t0, k_t1))]
     k_id = SEL(T.ID[:, :], T.RS64[:, 256:384], [[-1, 128]], A.is_equal, 0, 1, [m_1])
-    i_io4 = IOTA(T.IO4[:, 0:4], [[1, 4]], -512 * me, 0)
+    IOTA(T.TB[0:32, 384:512], [[0, 8], [2, 16]], 0, 0, True)
 
-    for i in range(4):
-        K["rc"] = S(T.RB[:, 64 * i:64 * i + 64], T.RS64[:, 256:320], [m_1], float((me + i) % NR), 0.0, f=F.Identity)
     m_xt = S(T.XT[:, 256:512], T.RS64[:, 256:512], [m_1], 0.0, 0.0)
-    for h in range(2):
-        m_e = S(T.ET[:, EW * h:EW * h + EW], T.RS64[:, 256:256 + EW], [m_1], 0.0, 0.0)
-    K["r16"] = S(T.RS16B[:, :], T.R16[:, :], [i_r16], f=F.Sign)
+
+    def zero(h):
+        return S(T.ET[:, EW * h:EW * h + EW], T.RS64[:, 256:256 + EW], [m_1], 0.0, 0.0)
 
     def lists(t, deps, ranks, gap):
         gap(0)
-        mk = [V("tt", deps, T.MK[:, 128 * u:128 * u + 128], ranks(u), T.RB[:, 128 * u:128 * u + 128], A.is_equal) for u in range(2)]
+        mk = {}
+        for r in (0, 3, 1, 2):
+            i = (r - me) % NR
+            if r in (0, 3):
+                mk[i] = S(T.MK[:, 64 * i:64 * i + 64], ranks, deps, *((1.0, -1.0) if r == 0 else (-2.0, 1.0)), f=F.Relu)
+            else:
+                mk[i] = V("ts", deps, T.MK[:, 64 * i:64 * i + 64], ranks, float(r), None, A.is_equal)
+        gap(1)
         px, sc = {}, {}
         for u in range(2):
             for h in range(2):
                 o = 272 * h + 128 * u + 1
-                px[h, u] = V("scan", [mk[u], K["rk"][h]], T.CN[:, o:o + 128], T.RK[:, 256 * h:256 * h + 128], T.MK[:, 128 * u:128 * u + 128],
-                             0.0, A.max, A.subtract)
+                px[h, u] = V("scan", [mk[2 * u], mk[2 * u + 1], K["rk"][h]], T.CN[:, o:o + 128], T.RK[:, 256 * h:256 * h + 128],
+                             T.MK[:, 128 * u:128 * u + 128], 0.0, A.max, A.subtract)
         for u in range(2):
             for h in range(2):
                 o = 272 * h + 128 * u
@@ -252,13 +256,19 @@ def rank_program(g, core, T, topo):
 
     def depart(t, al, held):
         c, s = T["cRW%d" % t], T["sRW%d" % t]
-        p2 = S(T["sLA%d" % t][:, 96:224], s[:, HELD:HELD + 64].indirect(L("AL", t, 0, 8)), [al, held[-1]])
-        p1 = V("copy", [al, held[0]], wd(T["cLA%d" % t], 96, 224), wd(c, HELD, HELD + 64).indirect(L("AL", t, 0, 8)))
-        sendcols("aq%d" % t, "aq%d" % t, "LA%d" % t, 128, 0, p1, p2)
-        return [p1, p2]
+
+        def pick(a, b, scales):
+            if scales:
+                return S(T["sLA%d" % t][:, 96 + 16 * a:96 + 16 * b], s[:, HELD:HELD + 64].indirect(L("AL", t, a, b)), [al, held[-1]])
+            return V("copy", [al, held[0]], wd(T["cLA%d" % t], 96 + 16 * a, 96 + 16 * b), wd(c, HELD, HELD + 64).indirect(L("AL", t, a, b)))
+
+        p2 = pick(2, 8, True)
+        sendcols("aq%d" % t, "aq%d" % t, "LA%d" % t, 128, 0, pick(2, 8, False), p2)
+        p2 = pick(0, 2, True)
+        return lambda: [p2, pick(0, 2, False)]
 
     def tell(t, ve):
-        vs = V("ts", [ve], L("VL", t, 8, 16), T.VE[:, 15:128:16], 4.0 / FINE, 254.0, A.mult, A.add)
+        vs = V("ts", [ve], L("VL", t, 8, 16), T.VE[:, 15:128:16], 1.0 / FINE, 63.5, A.mult, A.add)
         send("av", t, "VL", 10, 2, [vs])
         return vs
 
@@ -268,16 +278,13 @@ def rank_program(g, core, T, topo):
     def server(t, own, vs, prev, aside, step):
         KQ, sKQ = T.cKQ, T.sKQ
         LA, sLA = T["cLA%d" % t], T["sLA%d" % t]
-        land = [("aq%d" % t, CODES + SCALES)] + own + [K["kq"]]
-        z = []
+        land = [("aq%d" % t, CODES + SCALES)] + own
 
         def zout(i):
-            n = CUTS[i + 1] - CUTS[i]
-            return T.pz[:, 512 * i:512 * i + n] if i < 3 else T.px[:, 0:n]
+            return T.pz[:, 512 * i:512 * i + CUTS[i + 1] - CUTS[i]]
 
-        for i in range(4):
-            a, b = CUTS[i], CUTS[i + 1]
-            z.append(MM(zout(i), LA[:, 0:128], sLA[:, 0:128], KQ[:, a:b], sKQ[:, a:b], True, True, land + [prev["z"][i]]))
+        z = [MM(zout(i), LA[:, 0:128], sLA[:, 0:128], KQ[:, CUTS[i]:CUTS[i + 1]], sKQ[:, CUTS[i]:CUTS[i + 1]], True, True,
+                land + [prev["z"][i], K["kq", i]]) for i in range(3)]
 
         def zcopy(i):
             return T.ZS[:, CUTS[i]:CUTS[i + 1]], zout(i)
@@ -285,40 +292,48 @@ def rank_program(g, core, T, topo):
         def half(b):
             return MM(T.pv[:, 512 * b:512 * b + 128], *eq(b), LA[:, 0:128], sLA[:, 0:128], True, t > 0, [K["eq", b], prev["pv"][b]])
 
-        dq = [half(b) for b in range(2)]
-        c0 = S(*zcopy(0), [z[0], prev["t64"]])
-        c2 = S(*zcopy(2), [z[2]])
+        dq = [half(b) for b in range(4 if t else 2)]
+        c1 = S(*zcopy(1), [z[1], prev["t64"]])
         if t > 0:
             d = [S(T.DQ[:, 128 * b:128 * b + 128], T.pv[:, 512 * b:512 * b + 128], [dq[b], prev["ht"]]) for b in range(2)]
+            d3 = S(T.DQ[:, 256:320], T.pv[:, 1536:1600], [dq[3]])
         K["was"] = S(T.ND[:, 64 * t:64 * t + 64], T["NN%d" % t][:, 128:192], [K["node"]], 63.5, 1.0 / FINE, f=F.Identity)
         aside(3)
-        vp = V("copy", [vs, K["xl"], ("av%d" % t, LIST)], T.VP[:, :], L("VL", t, 0, 10).indirect(T.XL[:, 2:3]))
-        c1 = V("copy", [z[1]], *zcopy(1))
-        z4 = V("ts", [vp, i_io4], L("Z4", t, 0, 4), T.IO4[:, 0:4], T.VP[:, 0:1], 511.0, A.add, A.min)
-        c3 = V("copy", [z[3]], *zcopy(3))
-        t64 = V("tt", [c0, c1, c2, c3, z4, K["nm"]], T.T64[:, :], T.ZS[:, 0:512].indirect(L("Z4", t, 0, 4)), T.NM64[:, :], A.add)
+        mine = (128.0 * me, 128.0 * me + 127.0, A.max, A.min)
+        vp = V("ts", [vs, K["xl"], ("av%d" % t, LIST)], T.VP[:, :], L("VL", t, 0, 10).indirect(T.XL[:, 2:3]), *mine)
+        vu = V("ts", [], T.VU[:, :], L("VL", t, 2, 10), *mine)
+        c0 = V("copy", [z[0]], *zcopy(0))
+        z4 = V("ts", [vp, K["iq"]], L("Z4", t, 0, 4), T.IQ[:, :], T.VP[:, 0:1], 4.0, A.add, A.mult)
+        c2 = V("copy", [z[2]], *zcopy(2))
+        vu = V("tt", [vu, K["tb"]], T.VB[:, 0:128], T.TB[:, 384 - 128 * me:512].indirect(T.VU[:, :]), T.D16B[:, 0:128], A.mult)
+        t64 = V("tt", [c0, c1, c2, z4, K["nm"]], T.T64[:, :], T.ZS[:, 0:512].indirect(L("Z4", t, 0, 4)), T.NM64[:, :], A.add)
+        vu = V("scan", [vu], T.VB[:, 128:256], T.RS16B[:, 0:128], T.VB[:, 0:128], 0.0, A.mult, A.add)
+        if t == 0:
+            step()
+        rm = V("scan", [t64], T.RM[:, :], T.T64[:, :], T.T64[:, :], -BIG, A.max, A.max)
+        if t == 0:
+            step()
+        V("copy", [vu], T.XT[:, 3:32:4], T.VB[:, 143:256:16])
+        for c in range(3):
+            xs = V("ts", [rm, K["m8"]], T.XT[:, c:32:4], T.M8[:, :], T.RM[:, 16 * c + 15:16 * c + 16], T.RM[:, 63:64], A.add, A.is_lt)
         step()
-        rm = V("scan", [t64], T.RM[:, 1:65], T.T64[:, :], T.T64[:, :], -BIG, A.max, A.max)
-        step()
-        xs = V("ts", [rm, K["xm"], K["xs"], K["xl"]], T.XS[:, 0:32], T.RM[:, 0:56].indirect(T.XL[:, 0:2]), T.RM[:, 64:65], None, A.is_lt)
-        step()
-        xq = V("q", [xs, prev["xm"]], T.cXQ[:, 0:128], T.sXQ[:, 0:128], T.XS[:, :])
-        xm = MM(T.px[:, 0:128], T.cSQ[:, 0:128], T.sSQ[:, 0:128], T.cXQ[:, 0:128], T.sXQ[:, 0:128], True, True, [xq, K["sq"], c3])
-        dq += [half(b) for b in range(2, 4)]
+        xq = V("q", [xs, prev["xm"]], T.cXQ[:, 0:128], T.sXQ[:, 0:128], T.XT[:, :])
+        xm = MM(T.px[:, 0:128], T.cSQ[:, 0:128], T.sSQ[:, 0:128], T.cXQ[:, 0:128], T.sXQ[:, 0:128], True, True, [xq, K["sq"], prev["ou"]])
+        dq += [half(b) for b in range(len(dq), 4)]
         aside(0)
         if t + 1 < HOPS:
-            K["r0"] = V("copy", [K["node"]], T["NK%d" % t][:, 128:192], T["NN%d" % t][:, 128:192])
+            K["r0"] = V("ts", [K["node"]], T["NK%d" % t][:, 128:192], T["NN%d" % t][:, 128:192], WHOLE, WHOLE, A.add, A.subtract)
         step()
-        of = V("tt", [xm], T.OF[:, :], T.px[:, 0:8], L("VL", t, 2, 10), A.add)
         step()
         if t > 0:
-            ou = told = V("ts", [of], L("OR", t, 0, 8), T.OF[:, :], 512.0 * me, 512.0 * me + 511.0, A.max, A.min)
+            ou = told = V("ts", [xm], L("OR", t, 0, 8), T.px[:, 0:8], 512.0 * me, None, A.add)
             send("rc", t, "OR", 0, 8, [told])
         else:
-            ou = V("ts", [of], T.OU[:, 0:8], T.OF[:, :], -512.0 * me, 511.0, A.add, A.min)
+            ou = V("copy", [xm], T.OU[:, 0:8], T.px[:, 0:8])
         step()
         if t == 0:
-            ks = S(T.sKC[:, 0:128], sKQ[:, 0:512].indirect(T.OU[:, 0:8]), [ou, K["kq"]])
+            ks = S(T.sKC[:, 0:128], sKQ[:, 0:512].indirect(T.OU[:, 0:8]), [ou])
+            aside(4)
             nd = V("tt", [ou, K["t3"], K["d16"]], T.VD[:, :], T.NXA[:, 512 * me:512 * me + 512].indirect(T.OU[:, 0:8]), T.D16B[:, 0:128], A.mult)
             kc = V("copy", [ou], wd(T.cKC, 0, 128), wd(KQ, 0, 512).indirect(T.OU[:, 0:8]))
             ne = run(nd)
@@ -331,24 +346,27 @@ def rank_program(g, core, T, topo):
                 km = MM(T.pv[:, 512 * b:512 * b + 128], *eq(b), T.cKC[:, 0:128], T.sKC[:, 0:128], False, True, [kc, ks])
                 o, i = T.HT[:, b:512:4], T.pv[:, 512 * b:512 * b + 128]
                 h.append(S(o, i, [km]) if b % 2 == 0 else V("copy", [km], o, i))
+                if b == 1:
+                    step()
             ready = h
             ht = None
         else:
-            def chosen(b):
-                return T.DK[:, PAD + 512 * (b - me):PAD + 512 * b + 512].indirect(L("OR", t, 0, 8))
+            def chosen(b, lo, hi):
+                return T.DK[:, PAD + 512 * (b - me):PAD + 512 * b + 512].indirect(L("OR", t, lo, hi))
 
-            gk = [S(T.GK[:, 128 * b:128 * b + 128], chosen(2 + b), [ou, prev["ht"]] + K["dk"]) for b in range(2)]
+            gk = [S(T.GK[:, 0:128], chosen(2, 0, 8), [ou, prev["ht"]] + K["dk"]), S(T.GK[:, 128:192], chosen(3, 4, 8), [])]
             aside(1)
             for b in range(2):
-                V("tt", [ou, d[b], prev["nq"]] + K["dk"], T.HT[:, b:512:4], chosen(b), T.DQ[:, 128 * b:128 * b + 128], A.add)
-            ready = [V("tt", [dq[2 + b], gk[b]], T.HT[:, 2 + b:512:4], T.pv[:, 512 * (2 + b):512 * (2 + b) + 128], T.GK[:, 128 * b:128 * b + 128], A.add)
-                     for b in range(2)]
+                V("tt", [ou, d[b], prev["nq"]] + K["dk"], T.HT[:, b:512:4], chosen(b, 0, 8), T.DQ[:, 128 * b:128 * b + 128], A.add)
+            V("tt", [d3], T.HT[:, 3:256:4], chosen(3, 0, 4), T.DQ[:, 256:320], A.add)
+            ready = [V("tt", [dq[2], gk[0]], T.HT[:, 2:512:4], T.pv[:, 1024:1152], T.GK[:, 0:128], A.add),
+                     V("tt", [dq[3], gk[1]], T.HT[:, 259:512:4], T.pv[:, 1600:1664], T.GK[:, 128:192], A.add)]
             h = d + ready
             ht = ready[1]
         step()
         nq = V("q", ready, T["cRW%d" % t][:, 0:128], T["sRW%d" % t][:, 0:128], T.HT[:, :])
         sendcols("rq%d" % t, "rs%d" % t, "RW%d" % t, 0, 128, nq, nq)
-        prev.update({"z": [c0, c1, c2, of], "pv": h, "t64": t64, "ht": ht, "xm": xm, "of": of, "nq": nq})
+        prev.update({"z": [c0, c1, c2], "pv": h, "t64": t64, "ht": ht, "xm": xm, "ou": ou, "nq": nq})
         aside(2)
         return nq, told
 
@@ -369,7 +387,7 @@ def rank_program(g, core, T, topo):
         yield None
         w8 = V("scan", [w5, K["aw"]], T.WW[:, 80:96], T.AW[:, :], T.WW[:, 64:80], 0.0, A.max, A.subtract)
         yield None
-        K["sl"] = V("copy", [w8, K["xj"]], L("SL", t, 0, 16), T.WW[:, 80:96].indirect(T.XL[:, 6:7]))
+        K["sl"] = V("copy", [w8], L("SL", t, 0, 4), T.WW[:, 83:96:4])
         while True:
             yield None
 
@@ -381,94 +399,107 @@ def rank_program(g, core, T, topo):
     def table(b, lo=0, hi=512):
         r = (me + 1 + b) % NR
         return S(T.NXA[:, 512 * r + lo:512 * r + hi], T.NODF[:, 0:512].indirect(T.NXU[:, 32 * b + lo // 16:32 * b + hi // 16]),
-                 [K["no"] if b == 3 else K["nu"], K["nf"]], -63.5 * FINE, FINE, f=F.Identity)
+                 [K["nu", b], K["nf"]], -63.5 * FINE, FINE, f=F.Identity)
 
     def dkc(b):
         K["dk"].append(S(T.DK[:, PAD + 512 * b:PAD + 512 * b + 512], T.pv[:, 512 * b:512 * b + 512], [K["um"][b]]))
 
-    k_sr = V("ts", [d_st, x_3], T.STR[:, :], T.STW[:, 0:4].indirect(T.XL[:, 8:9]), FINE, -63.5 * FINE, A.mult, A.add)
+    k_sr = V("ts", [d_st], T.STR[:, :], T.STW[:, :], FINE, -63.5 * FINE, A.mult, A.add)
 
     def gap0(k):
         if k == 0:
-            k_st = V("copy", [d_st], T.STU[:, :], T.STW[:, :])
+            K["su"] = V("copy", [d_st], T.STU[:, :], T.STW[:, :])
             K["d16"] = V("ts", [k_t0, i_r16], T.D16B[:, :], T.R16[:, :], 1.0, T.THR[:, 0:1], A.add, A.is_equal)
-            K["node"] = S(T.NN0[:, 128:192], T.NODF[:, 0:512].indirect(T.STU[:, 0:4]), [k_st, K["nf"]], -63.5 * FINE, FINE, f=F.Identity)
+        if k == 1:
+            K["ez"] = zero(0)
+            K["r16"] = S(T.RS16B[:, :], T.R16[:, :], [i_r16], f=F.Sign)
+            K["node"] = S(T.NN0[:, 128:192], T.NODF[:, 0:512].indirect(T.STU[:, 0:4]), [K["su"], K["nf"]], -63.5 * FINE, FINE, f=F.Identity)
         if k == 4:
             K["held"] = [V("q", [d_x, m_xt], T.cRW0[:, HELD:HELD + 128], T.sRW0[:, HELD:HELD + 128], T.XT[:, :])]
         if k == 5:
-            K["xg"] = V("ts", [i_pi], T.XI[:, 0:2], T.PI[:, 2:4], 0xFFF0, None, A.bitwise_and)
-            K["xv"] = V("ts", [i_pi], T.XI[:, 2:5], T.PI[:, 0:3], 12, None, A.bitwise_and)
+            K["xu"] = V("ts", [x_g], T.XF[:, 0:1], T.XI[:, 0:1], 1.0 / 16, None, A.mult)
+            K["xl"] = V("ts", [x_g], T.XL[:, 2:3], T.XI[:, 0:1], 1.0 / 16, 2.0, A.mult, A.add)
 
-    al = lists(0, [k_sr, i_r16, K["rc"]], lambda u: T.R16[:, 0:16].indirect(T.STR[:, 8 * u:8 * u + 8]), gap0)
-    node, held, x_g, x_v = K["node"], K["held"], K["xg"], K["xv"]
+    al = lists(0, [k_sr, i_r16], T.R16[:, 0:16].indirect(T.STR[:, :]), gap0)
+    node, held = K["node"], K["held"]
     hq0 = held[0]
     own = depart(0, al, held)
-    k_e = [S(T.ET[:, EW * h + 2 + h:EW * h + EW:4], T.ID[:, :], [m_e, k_id], 0.0, 0.5) for h in range(2)]
+    k_e = [S(T.ET[:, EW * h + 2 + h:EW * h + EW:4], T.ID[:, :], [zero(1) if h else K["ez"], k_id], 0.0, 0.5) for h in range(2)]
     for b in range(4):
         K["st"] = S(T.ST[:, b:512:4], T.D16B[:, 0:128], [K["d16"]])
     K["nm"] = S(T.NM64[:, :], T.D16B[:, 0:64], [K["d16"]], -BIG, BIG, f=F.Identity)
-    K["xs"] = S(T.XS[:, :], T.RS64[:, 0:512], [m_rs], 0.0, 0.0)
+    K["rb"] = S(T.RK[:, 512:768], T.RS64[:, 0:256], [m_rs], 65.0, -65.0, f=F.Identity)
     vd = diag(0, al)
-    K["xm"] = V("set", [], T.RM[:, 0:1], BIG)
-    x_u = V("ts", [x_v], T.XF[:, 0:2], T.XI[:, 3:5], 4.0, None, A.mult)
-    ve = run(vd)
-    V("ts", [x_g, x_u], T.XL[:, 0:2], T.XI[:, 0:2], T.XF[:, 1:2], T.XF[:, 0:1], A.is_equal, A.mult)
-    K["xl"] = V("ts", [x_g], T.XL[:, 2:3], T.XI[:, 0:1], 1.0 / 16, 2.0, A.mult, A.add)
-    vs = tell(0, ve)
+    K["m8"] = V("ts", [K["xu"]], T.M8[:, :], T.R16[:, 0:8], T.XF[:, 0:1], BIG, A.not_equal, A.mult)
+    vs = tell(0, run(vd))
+    own = own()
+    i_io4 = IOTA(T.IO4[:, 0:4], [[1, 4]], -512 * me, 0)
+    need("g", [i_io4])
+    K["tb"] = IOTA(T.TB[32:64, 384:512], [[32, 8], [0, 16]], 0, 0, True)
+    need("g", [K["tb"]])
     i_16 = IOTA(T.IO[:, 0:16], [[16, 4], [-32, 4]], 63, 0, True)
     i_k16 = IOTA(T.IO[:, 16:32], [[16, 4], [-1024, 4]], 127, 0, True)
-    K["kq"] = V("q", [d_ky], T.cKQ[:, 0:512], T.sKQ[:, 0:512], T.KT[:, :])
+    K["nr"] = IOTA(T.NODR[:, :], [[1, 4], [0, 128]], 0, 0, True)
+
+    def keys(i):
+        K["kq", i] = V("q", [d_ky[i]], T.cKQ[:, CUTS[i]:CUTS[i + 1]], T.sKQ[:, CUTS[i]:CUTS[i + 1]], T.KT[:, 4 * CUTS[i]:4 * CUTS[i + 1]])
 
     def unit(b):
         o = EW * (b % 2) + (2 if b < 2 else 0)
         K["eq", b] = V("q", [k_e[b % 2]], *eq(b), T.ET[:, o:o + 512])
 
-    K["no"] = V("copy", [d_no], T.NXU[:, 96:128], T.NXV[:, :])
+    keys(0)
+    keys(1)
     unit(0)
     unit(1)
-    K["sq"] = V("q", [K["st"]], T.cSQ[:, 0:128], T.sSQ[:, 0:128], T.ST[:, :])
+    x_k = V("ts", [k_pj], T.XI[:, 6:7], T.XI[:, 5:6], 68.0, None, A.mult)
+    keys(2)
+    K["iq"] = V("ts", [i_io4], T.IQ[:, :], T.IO4[:, 0:4], 0.25, None, A.mult)
+    x_k = V("ts", [x_k], T.XI[:, 7:8], T.XI[:, 6:7], 0xF0, None, A.bitwise_and)
+    K["nu", 3] = V("copy", [d_no], T.NXU[:, 96:128], T.NXV[:, :])
     find = where(0)
-    K["rb"] = V("ts", [], T.RK[:, 512:768], T.RS64[:, 0:256], 0.0, 65.0, A.is_equal, A.mult)
-    next(find)
 
     def links0():
         unit(2)
-        next(find)
         yield None
         unit(3)
-        x_k = V("ts", [k_pj], T.XI[:, 6:7], T.XI[:, 5:6], 68.0, None, A.mult)
         yield None
-        next(find)
-        x_k = V("ts", [x_k], T.XI[:, 7:8], T.XI[:, 6:7], 0xF0, None, A.bitwise_and)
+        K["sq"] = V("q", [K["st"]], T.cSQ[:, 0:128], T.sSQ[:, 0:128], T.ST[:, :])
         yield None
+        for _ in range(3):
+            yield next(find)
         next(find)
         K["xk"] = V("ts", [x_k], T.XL[:, 4:5], T.XI[:, 7:8], 15.0, None, A.add)
-        K["xj"] = V("ts", [x_v], T.XL[:, 6:7], T.XI[:, 2:3], 3.0, None, A.add)
         yield None
         while True:
             yield next(find)
 
     rest = links0()
+    d_nx = {}
     for b in range(3):
         for k in range(8):
-            d_nx = DMA("y", "dnx", T.NXW[16 * k:16 * k + 16, 32 * b:32 * b + 32], T["NXR%d" % b][:, :], [("nxr", 3 * len(e16))])
+            d_nx[b] = DMA("y", "dnx" if b else "dn0", T.NXW[16 * k:16 * k + 16, 32 * b:32 * b + 32], T["NXR%d" % b][:, :],
+                          [("nxr", 3 * len(e16))] + ([("av0", LIST), ("aq0", CODES + SCALES)] if b else []))
+    d_w = DMA("y", "dw", T.WT[:, :], T.w[:, :])
     DMA("y", "dh3", by(T.cHQ3, 64, 128), by(T.cRW0, HELD + 64, HELD + 128), [hq0])
     d_h3 = DMA("y", "dh3", T.sHQ3[:, 64:128], T.sRW0[:, HELD + 64:HELD + 128], [hq0])
-    K["c16"] = S(T.C16[:, :], T.IO[:, 0:16], [i_16, k_t0], T.THR[:, 0:1], f=F.Identity)
-    K["aw"] = S(T.AW[:, :], T.IO[:, 16:32], [i_k16, k_t0], T.THR[:, 0:1], f=F.Identity)
 
     def aside0(k):
+        if k == 3:
+            K["c16"] = S(T.C16[:, :], T.IO[:, 0:16], [i_16, k_t0], T.THR[:, 0:1], f=F.Identity)
+            K["aw"] = S(T.AW[:, :], T.IO[:, 16:32], [i_k16, k_t0], T.THR[:, 0:1], f=F.Identity)
+            K["t3"] = table(3)
+        if k == 0:
+            K["nu", 0] = V("copy", [d_nx[0]], T.NXU[:, 0:32], T.NXW[:, 0:32])
+            K["nxa"] = [K["t3"], table(0, 0, 256)]
+        if k == 4:
+            K["nxa"].append(table(0, 256, 512))
         if k == 1:
             next(find)
-        if k == 3:
-            K["t3"] = table(3)
         if k == 2:
-            K["nu"] = V("copy", [d_nx], T.NXU[:, 0:96], T.NXW[:, :])
+            next(find)
             K["dk"] = []
             K["um"] = [MM(T.pv[:, 512 * b:512 * b + 512], *eq(b), T.cKQ[:, 0:512], T.sKQ[:, 0:512], True, True, [prev["pv"][b]]) for b in range(4)]
-            for b in range(2):
-                dkc(b)
-            K["nxa"] = [K["t3"]]
 
     def aside1(k):
         if k == 3:
@@ -478,21 +509,21 @@ def rank_program(g, core, T, topo):
         if k == 0:
             K["wq"] = V("q", [d_w], T.cWQ[:, 0:128], T.sWQ[:, 0:128], T.WT[:, :])
 
-    prev = {"z": [None] * 4, "pv": [None] * 4, "t64": None, "ht": None, "xm": None, "of": None, "nq": None}
+    prev = {"z": [None] * 3, "pv": [None] * 4, "t64": None, "ht": None, "xm": None, "ou": None, "nq": None}
     for t in range(HOPS):
         n = T["NN%d" % t]
         if t == 0:
             nq, told = server(0, own, vs, prev, aside0, lambda: next(rest))
         else:
             if t == 1:
+                dkc(1)
                 dkc(2)
                 next(find)
                 K["dk"].append(V("copy", [K["um"][3]], T.DK[:, PAD + 1536:PAD + 2048], T.pv[:, 1536:2048]))
                 prev["pv"] = K["dk"]
-                K["nxa"] += [table(0), table(1, 0, 256)]
+                K["nxa"].append(table(1, 0, 256))
             else:
                 next(find)
-            next(find)
             next(find)
             nq, told = server(t, own, vs, prev, aside1 if t == 1 else lambda k: None, lambda: next(find))
         sl = K["sl"]
@@ -507,15 +538,23 @@ def rank_program(g, core, T, topo):
             break
         nk = T["NK%d" % t]
         g1 = S(n[:, 0:128], slots, tabs, bias, scale, f=F.Identity)
-        r1 = V("ts", tabs, nk[:, 0:128], slots, scale, bias, A.mult, A.add)
-        node = K["node"] = S(T["NN%d" % (t + 1)][:, 128:192], byq, [g1, sl, node])
+        if t == 0:
+            r1 = V("copy", tabs + [K["nr"]], nk[:, 0:128], T.NODR[:, 0:512].indirect(L("OR", t, 6, 14)))
+        else:
+            r1 = V("ts", tabs, nk[:, 0:128], slots, WHOLE, WHOLE, A.add, A.subtract)
 
         def gap(k):
+            if k == 1:
+                if t == 0:
+                    dkc(0)
+                K["node"] = S(T["NN%d" % (t + 1)][:, 128:192], byq, [g1, sl, node])
             if k == 4:
                 K["held"] = order(t, held, nq, sl, T["cRW%d" % (t + 1)], T["sRW%d" % (t + 1)], HELD)
+            if k == 5 and t == 0:
+                K["nu", 1] = K["nu", 2] = V("copy", [d_nx[2]], T.NXU[:, 32:96], T.NXW[:, 32:96])
 
-        al = lists(t + 1, [K["r0"], r1, sl], lambda u: nk[:, 0:192].indirect(L("SL", t, 8 * u, 8 * u + 8)), gap)
-        held = K["held"]
+        al = lists(t + 1, [K["r0"], r1, sl], nk[:, 0:192].indirect(L("SL", t, 0, 4)), gap)
+        node, held = K["node"], K["held"]
         own = depart(t + 1, al, held)
         vd = diag(t + 1, al)
         find = where(t + 1)
@@ -523,12 +562,13 @@ def rank_program(g, core, T, topo):
         ve = run(vd)
         next(find)
         vs = tell(t + 1, ve)
+        own = own()
 
     DMA("y", "dout", T.oc[:, :], by(T.cHQ3, 0, 64), [hq[0]])
     for k in range(4):
         DMA("s" if k < 3 else "y", "dout", T.osc[4 * k:4 * k + 4, 0:64], T.sHQ3[32 * k:32 * k + 4, 0:64], [hq[1]])
-    ym = MM(T.px[:, 0:128], T.cWQ[:, 0:128], T.sWQ[:, 0:128], T.cHQ3[:, 0:128], T.sHQ3[:, 0:128], True, True, hq + [K["wq"], d_h3, prev["of"]])
+    ym = MM(T.px[:, 0:128], T.cWQ[:, 0:128], T.sWQ[:, 0:128], T.cHQ3[:, 0:128], T.sHQ3[:, 0:128], True, True, hq + [K["wq"], d_h3, prev["ou"]])
     yc = V("copy", [ym], T.YS[:, :], T.px[:, 0:64])
     DMA("y", "dout", T.y[:, :], T.YS[:, :], [yc])
-    for sem in ("dout", "ls", "cv", "cs", "ct", "cg", "dst", "dx", "dky", "dnx", "dno", "dnd", "dw", "dh3"):
+    for sem in ("dout", "ls", "cv", "cs", "ct", "cg", "dst", "dx", "dk0", "dk1", "dk2", "dnx", "dn0", "dno", "dnd", "dw", "dh3"):
         need("g", [(sem, count[sem])])

from concourse.bass import DstId, RemoteDMATransfer
from concourse.mybir import dt, AluOpType as A, ActivationFunctionType as F

NR, CAP, HOPS = 4, 32, 3
BIG = 1e29
CUTS = (0, 192, 384, 512)
HELD = 224
FINE = 2.0 ** -7
WHOLE = 1.5 * 2.0 ** 23
PAD = 1536
EW = 514

SCRATCH = {
    "STW": ("sbuf", [128, 4], "int32"), "STU": ("sbuf", [128, 4], "uint16"), "STR": ("sbuf", [128, 4], "uint16"),
    "NXD": ("dram", [128, 4], "int32"), "NXR0": ("dram", [128, 4], "int32"), "NXR1": ("dram", [128, 4], "int32"), "NXR2": ("dram", [128, 4], "int32"),
    "NXW": ("sbuf", [128, 96], "int32"), "NXV": ("sbuf", [128, 32], "int32"), "NXU": ("sbuf", [128, 128], "uint16"), "NXA": ("sbuf", [128, 2048], "float32"),
    "NODF": ("sbuf", [128, 512], "float32"), "NODR": ("sbuf", [128, 512], "float32"),
    "R16": ("sbuf", [128, 256], "bfloat16"), "ID": ("sbuf", [128, 128], "bfloat16"),
    "PI": ("sbuf", [128, 4], "int32"), "THR": ("sbuf", [128, 8], "float32"),
    "XI": ("sbuf", [128, 8], "int32"), "XF": ("sbuf", [128, 4], "float32"), "XL": ("sbuf", [128, 8], "uint16"),
    "IO4": ("sbuf", [128, 4], "int32"), "IQ": ("sbuf", [128, 4], "float32"), "AW": ("sbuf", [128, 16], "float32"),
    "IO": ("sbuf", [128, 32], "float32"), "C16": ("sbuf", [128, 16], "float32"),
    "D16B": ("sbuf", [128, 256], "bfloat16"), "NM64": ("sbuf", [128, 64], "float32"),
    "RS64": ("sbuf", [128, 256 + EW], "bfloat16"), "RS16B": ("sbuf", [128, 256], "bfloat16"),
    "RK": ("sbuf", [128, 768], "bfloat16"), "UP": ("sbuf", [128, 128], "bfloat16"),
    "M8": ("sbuf", [128, 8], "float32"), "TB": ("sbuf", [128, 512], "bfloat16"),
    "AL": ("sbuf", [128, 48], "uint16"),
    "VL": ("sbuf", [128, 48], "float32"),
    "Z4": ("sbuf", [128, 48], "uint16"),
    "OU": ("sbuf", [128, 8], "uint16"),
    "OR": ("sbuf", [128, 48], "uint16"),
    "SL": ("sbuf", [128, 48], "uint16"),
    "MK": ("sbuf", [128, 256], "bfloat16"), "PX": ("sbuf", [128, 256], "bfloat16"),
    "CN": ("sbuf", [128, 544], "bfloat16"), "SC": ("sbuf", [128, 512], "bfloat16"), "VD": ("sbuf", [128, 128], "float32"), "VE": ("sbuf", [128, 128], "float32"),
    "MD": ("sbuf", [128, 256], "bfloat16"), "UD": ("sbuf", [128, 256], "bfloat16"), "FF": ("sbuf", [128, 256], "bfloat16"),
    "WW": ("sbuf", [128, 96], "float32"), "ND": ("sbuf", [128, 256], "float32"),
    "VP": ("sbuf", [128, 16], "float32"), "VU": ("sbuf", [128, 8], "uint16"), "VB": ("sbuf", [128, 256], "bfloat16"),
    "ZS": ("sbuf", [128, 512], "float32"), "T64": ("sbuf", [128, 64], "float32"),
    "RM": ("sbuf", [128, 64], "float32"),
    "HT": ("sbuf", [128, 512], "bfloat16"),
    "DK": ("sbuf", [128, PAD + 2048], "float32"), "DQ": ("sbuf", [128, 320], "float32"), "GK": ("sbuf", [128, 192], "float32"),
    "XT": ("sbuf", [128, 512], "bfloat16"), "KT": ("sbuf", [128, 2048], "bfloat16"), "WT": ("sbuf", [128, 512], "bfloat16"),
    "ET": ("sbuf", [128, 2 * EW], "bfloat16"), "ST": ("sbuf", [128, 512], "bfloat16"), "YS": ("sbuf", [128, 64], "float32"),
    "pv": ("psum", [128, 2048], "float32"), "pz": ("psum", [128, 1536], "float32"), "px": ("psum", [128, 512], "float32"),
}


def _codes(name, n):
    SCRATCH["c" + name] = ("sbuf", [128, n], "float8_e4m3fn_x4")
    SCRATCH["s" + name] = ("sbuf", [128, n], "uint8")


for _n, _w in (("KQ", 512), ("EQ", 512), ("SQ", 128), ("WQ", 128), ("XQ", 128), ("HQ3", 128), ("KC", 128)):
    _codes(_n, _w)
for _t in range(HOPS):
    for _n, _w in (("LA", 224), ("RW", 288 if _t else 352)):
        _codes(_n + str(_t), _w)
    SCRATCH["NN%d" % _t] = ("sbuf", [128, 192], "float32")
    SCRATCH["NK%d" % _t] = ("sbuf", [128, 192], "float32")
SEMAPHORES = ["cv", "cs", "ct", "cg", "ls", "dst", "dx", "dno", "dnx", "dn0", "dnd", "nxr", "dk0", "dk1", "dk2", "dw", "dh3", "dout"]
for _t in range(HOPS):
    SEMAPHORES += ["aq%d" % _t, "av%d" % _t, "rq%d" % _t, "rs%d" % _t, "rc%d" % _t]


def rank_program(g, core, T, topo):
    me = T.rank_of(core)
    if me is None:
        return
    cores = list(T.cores)
    eng = {"v": g.vector, "s": g.scalar, "t": g.tensor, "g": g, "y": g.sync}
    count = {}
    known = {q: {} for q in eng}
    seen = {}

    def need(q, deps):
        for d in deps:
            if d is None:
                continue
            sem, val = d
            if known[q].get(sem, 0) >= val:
                continue
            eng[q].wait_ge(T.sem[sem], int(val))
            known[q][sem] = val
            for k, w in seen.get(d, {}).items():
                if known[q].get(k, 0) < w:
                    known[q][k] = w

    def done(q, ins, sem, n):
        count[sem] = count.get(sem, 0) + n
        ins.then_inc(T.sem[sem], n)
        tok = (sem, count[sem])
        seen[tok] = dict(known[q])
        return tok

    v = g.vector
    getv = {"copy": v.tensor_copy, "tt": v.tensor_tensor, "ts": v.tensor_scalar, "scan": v.tensor_tensor_scan, "set": v.memset, "q": v.quantize_mx}

    def V(name, deps, *args):
        need("v", deps)
        return done("v", getv[name](*args), "cv", 1)

    def S(out, in_, deps, *scale, f=F.Copy):
        need("s", deps)
        return done("s", g.scalar.activation(out, in_, f, *scale), "cs", 1)

    def MM(out, lc, ls, rc, rs, start, stop, deps):
        need("t", deps)
        return done("t", g.tensor.matmul_mx(out, lc, ls, rc, rs, start, stop), "ct", 1)

    def DMA(q, sem, out, in_, deps=()):
        need(q, deps)
        return done(q, eng[q].dma_start(out, in_), sem, 16)

    def IOTA(out, pattern, base, cm, f32=False):
        if f32:
            return done("g", g.iota(out, pattern, base, cm, allow_small_or_imprecise_dtypes=True), "cg", 1)
        return done("g", g.iota(out, pattern, base, cm), "cg", 1)

    def SEL(out, in_, pattern, op, base, cm, deps):
        need("g", deps)
        return done("g", g.affine_select(out, in_, pattern, op, 0.0, base, cm), "cg", 1)

    peers = [(me + 1 + b) % NR for b in range(NR - 1)]

    def part(s, r):
        others = sorted((o for o in range(NR) if o != s), key=lambda o: (topo.die(cores[o]) != topo.die(cores[s]), (o - s) % NR))
        e = topo.engines(cores[s], cores[r])
        q = len(e) // 4
        return (e[:q], e[q:2 * q], e[2 * q:])[others.index(r)]

    def lanes(s, r):
        others = sorted((o for o in range(NR) if o != s), key=lambda o: (topo.die(cores[o]) == topo.die(cores[s]), (o - s) % NR))
        e = topo.engines(cores[s], cores[r])
        q = len(e) // 4
        ev, od = e[0::2], e[1::2]
        return ((ev[:q], od[q:]), (ev[q:], od[:q]), (od, ev))[others.index(r)]

    def bits(es):
        m = 0
        for i in es:
            m |= 1 << i
        return m

    def coreid(r):
        rid, pid, _ = topo.addr(cores[r])
        return DstId(rid=rid, pnc=pid)

    LIST = sum(len(part(r, me)) for r in peers)
    CODES, SCALES = (sum(len(lanes(r, me)[k]) for r in peers) for k in range(2))

    def fused(tr):
        g.remote_dma_fused(tr, local_sem=T.sem.ls)

    def one(r, m, sem, src, dst):
        return RemoteDMATransfer(dst_ids=[coreid(r)], dma_engine_mask=m, remote_sem=T.sem[sem], src=src, dst=dst)

    def there(r):
        return (me - r - 1) % NR

    def send(sem, t, name, src, dst, deps):
        need("g", deps)
        fused([one(r, bits(part(me, r)), sem + str(t), L(name, t, src + 2 * b, src + 2 * b + 2), L(name, t, dst + 2 * there(r), dst + 2 * there(r) + 2))
               for b, r in enumerate(peers)])
        count["ls"] = count.get("ls", 0) + sum(len(part(me, r)) for r in peers)

    def by(x, a, b):
        return x[:, a:b].bitcast(dt.uint8)

    def sendcols(sem, sem2, name, src, dst, codes, scales):
        C, P = T["c" + name], T["s" + name]
        need("g", [codes])
        fused([one(r, bits(lanes(me, r)[0]), sem, by(C, src + 32 * b, src + 32 * b + 32), by(C, dst + 32 * there(r), dst + 32 * there(r) + 32))
               for b, r in enumerate(peers)])
        need("g", [scales])
        fused([one(r, bits(lanes(me, r)[1]), sem2, P[:, src + 32 * b:src + 32 * b + 32], P[:, dst + 32 * there(r):dst + 32 * there(r) + 32])
               for b, r in enumerate(peers)])
        count["ls"] = count.get("ls", 0) + sum(len(lanes(me, r)[0]) + len(lanes(me, r)[1]) for r in peers)

    def wd(x, a, b):
        return x[:, a:b].bitcast(dt.uint32)

    def L(name, t, a, b, step=1):
        return T[name][:, 16 * t + a:16 * t + b:step]

    K = {}

    for k in range(8):
        d_st = DMA("y" if k % 2 == 0 else "s", "dst", T.STW[16 * k:16 * k + 16, 0:4], T.st[:, :])
    d_nd = DMA("s", "dnd", T.NXD[:, :], T.nx[:, :])
    d_x = DMA("y", "dx", T.XT[:, 0:256], T.x[:, :])
    d_ky = [DMA("sys"[i], "dk%d" % i, T.KT[:, 4 * CUTS[i]:4 * CUTS[i + 1]], T.ky[:, 4 * CUTS[i]:4 * CUTS[i + 1]]) for i in range(3)]
    for k in range(8):
        d_no = DMA("y", "dno", T.NXV[16 * k:16 * k + 16, 0:32], T.nx[:, :])

    i_pi = IOTA(T.PI[:, 0:1], [[0, 1]], 0, 1)
    i_r16 = IOTA(T.R16[:, :], [[0, 16], [1, 16]], 0, 0, True)
    K["nf"] = IOTA(T.NODF[:, :], [[1, 512]], 0, 0, True)
    need("g", [d_nd])
    e16 = topo.engines(core, cores[peers[0]])
    fused([RemoteDMATransfer(dst_ids=[coreid(r) for r in peers], dma_engine_mask=bits(e16), remote_sem=T.sem.nxr, srcs=[T.NXD[:, :]],
                             dsts=[T["NXR%d" % there(r)][:, :] for r in peers])])
    count["ls"] = len(e16)

    m_1 = V("set", [], T.RS64[:, :], 1.0)
    m_up = V("set", [], T.MD[:, 0:128], 1.0 / 64)
    k_pj = V("ts", [i_pi], T.XI[:, 5:6], T.PI[:, 0:1], 15, None, A.bitwise_and)
    K["cn"] = V("set", [], T.CN[:, 0:544:272], 0.0)
    V("set", [], T.TB[64:128, 384:512], 0.0)
    m_rs = V("set", [m_1], T.RS64[:, 0:256:64], 0.0)
    k_t0 = V("ts", [k_pj], T.THR[:, 0:1], T.XI[:, 5:6], 1.0, None, A.add)
    k_t1 = V("ts", [k_pj], T.THR[:, 1:2], T.XI[:, 5:6], 17.0, None, A.add)
    x_g = V("ts", [i_pi], T.XI[:, 0:1], T.PI[:, 0:1], 0xFFF0, None, A.bitwise_and)
    K["up"] = V("scan", [m_rs, m_up], T.UP[:, :], T.RS64[:, 0:128], T.MD[:, 0:128], 0.0, A.mult, A.add)
    K["rk"] = [V("ts", [m_rs, k], T.RK[:, 256 * h:256 * h + 128], T.RS64[:, 0:128], 0.0, T.THR[:, h:h + 1], A.is_equal, A.mult)
               for h, k in enumerate((k_t0, k_t1))]
    k_id = SEL(T.ID[:, :], T.RS64[:, 256:384], [[-1, 128]], A.is_equal, 0, 1, [m_1])
    IOTA(T.TB[0:32, 384:512], [[0, 8], [2, 16]], 0, 0, True)

    m_xt = S(T.XT[:, 256:512], T.RS64[:, 256:512], [m_1], 0.0, 0.0)

    def zero(h):
        return S(T.ET[:, EW * h:EW * h + EW], T.RS64[:, 256:256 + EW], [m_1], 0.0, 0.0)

    def lists(t, deps, ranks, gap):
        gap(0)
        mk = {}
        for r in (0, 3, 1, 2):
            i = (r - me) % NR
            if r in (0, 3):
                mk[i] = S(T.MK[:, 64 * i:64 * i + 64], ranks, deps, *((1.0, -1.0) if r == 0 else (-2.0, 1.0)), f=F.Relu)
            else:
                mk[i] = V("ts", deps, T.MK[:, 64 * i:64 * i + 64], ranks, float(r), None, A.is_equal)
        gap(1)
        px, sc = {}, {}
        for u in range(2):
            for h in range(2):
                o = 272 * h + 128 * u + 1
                px[h, u] = V("scan", [mk[2 * u], mk[2 * u + 1], K["rk"][h]], T.CN[:, o:o + 128], T.RK[:, 256 * h:256 * h + 128],
                             T.MK[:, 128 * u:128 * u + 128], 0.0, A.max, A.subtract)
        for u in range(2):
            for h in range(2):
                o = 272 * h + 128 * u
                sc[h] = V("scan", [px[h, u], K["up"], K["cn"]], T.SC[:, 256 * h + 128 * u:256 * h + 128 * u + 128], T.CN[:, o:o + 128], T.UP[:, 0:128],
                          1.0, A.max, A.min)
        gap(4)
        for h in range(2):
            al = V("ts", [sc[h]], L("AL", t, h, 8, 2), T.SC[:, 256 * h + 63:256 * h + 256:64], 64.0, -1.0, A.mult, A.add)
        gap(5)
        return al

    def diag(t, al):
        return V("tt", [al, K["d16"], K["node"]], T.VD[:, :], T["NN%d" % t][:, 128:192].indirect(L("AL", t, 0, 8)), T.D16B[:, 0:128], A.mult)

    def run(vd):
        return V("scan", [vd, K["r16"]], T.VE[:, :], T.RS16B[:, 0:128], T.VD[:, :], 0.0, A.mult, A.add)

    def depart(t, al, held):
        c, s = T["cRW%d" % t], T["sRW%d" % t]

        def pick(a, b, scales):
            if scales:
                return S(T["sLA%d" % t][:, 96 + 16 * a:96 + 16 * b], s[:, HELD:HELD + 64].indirect(L("AL", t, a, b)), [al, held[-1]])
            return V("copy", [al, held[0]], wd(T["cLA%d" % t], 96 + 16 * a, 96 + 16 * b), wd(c, HELD, HELD + 64).indirect(L("AL", t, a, b)))

        p2 = pick(2, 8, True)
        sendcols("aq%d" % t, "aq%d" % t, "LA%d" % t, 128, 0, pick(2, 8, False), p2)
        p2 = pick(0, 2, True)
        return lambda: [p2, pick(0, 2, False)]

    def tell(t, ve):
        vs = V("ts", [ve], L("VL", t, 8, 16), T.VE[:, 15:128:16], 1.0 / FINE, 63.5, A.mult, A.add)
        send("av", t, "VL", 10, 2, [vs])
        return vs

    def eq(b):
        return T.cEQ[:, 128 * b:128 * b + 128], T.sEQ[:, 128 * b:128 * b + 128]

    def server(t, own, vs, prev, aside, step):
        KQ, sKQ = T.cKQ, T.sKQ
        LA, sLA = T["cLA%d" % t], T["sLA%d" % t]
        land = [("aq%d" % t, CODES + SCALES)] + own

        def zout(i):
            return T.pz[:, 512 * i:512 * i + CUTS[i + 1] - CUTS[i]]

        z = [MM(zout(i), LA[:, 0:128], sLA[:, 0:128], KQ[:, CUTS[i]:CUTS[i + 1]], sKQ[:, CUTS[i]:CUTS[i + 1]], True, True,
                land + [prev["z"][i], K["kq", i]]) for i in range(3)]

        def zcopy(i):
            return T.ZS[:, CUTS[i]:CUTS[i + 1]], zout(i)

        def half(b):
            return MM(T.pv[:, 512 * b:512 * b + 128], *eq(b), LA[:, 0:128], sLA[:, 0:128], True, t > 0, [K["eq", b], prev["pv"][b]])

        dq = [half(b) for b in range(4 if t else 2)]
        c1 = S(*zcopy(1), [z[1], prev["t64"]])
        if t > 0:
            d = [S(T.DQ[:, 128 * b:128 * b + 128], T.pv[:, 512 * b:512 * b + 128], [dq[b], prev["ht"]]) for b in range(2)]
            d3 = S(T.DQ[:, 256:320], T.pv[:, 1536:1600], [dq[3]])
        K["was"] = S(T.ND[:, 64 * t:64 * t + 64], T["NN%d" % t][:, 128:192], [K["node"]], 63.5, 1.0 / FINE, f=F.Identity)
        aside(3)
        mine = (128.0 * me, 128.0 * me + 127.0, A.max, A.min)
        vp = V("ts", [vs, K["xl"], ("av%d" % t, LIST)], T.VP[:, :], L("VL", t, 0, 10).indirect(T.XL[:, 2:3]), *mine)
        vu = V("ts", [], T.VU[:, :], L("VL", t, 2, 10), *mine)
        c0 = V("copy", [z[0]], *zcopy(0))
        z4 = V("ts", [vp, K["iq"]], L("Z4", t, 0, 4), T.IQ[:, :], T.VP[:, 0:1], 4.0, A.add, A.mult)
        c2 = V("copy", [z[2]], *zcopy(2))
        vu = V("tt", [vu, K["tb"]], T.VB[:, 0:128], T.TB[:, 384 - 128 * me:512].indirect(T.VU[:, :]), T.D16B[:, 0:128], A.mult)
        t64 = V("tt", [c0, c1, c2, z4, K["nm"]], T.T64[:, :], T.ZS[:, 0:512].indirect(L("Z4", t, 0, 4)), T.NM64[:, :], A.add)
        vu = V("scan", [vu], T.VB[:, 128:256], T.RS16B[:, 0:128], T.VB[:, 0:128], 0.0, A.mult, A.add)
        if t == 0:
            step()
        rm = V("scan", [t64], T.RM[:, :], T.T64[:, :], T.T64[:, :], -BIG, A.max, A.max)
        if t == 0:
            step()
        V("copy", [vu], T.XT[:, 3:32:4], T.VB[:, 143:256:16])
        for c in range(3):
            xs = V("ts", [rm, K["m8"]], T.XT[:, c:32:4], T.M8[:, :], T.RM[:, 16 * c + 15:16 * c + 16], T.RM[:, 63:64], A.add, A.is_lt)
        step()
        xq = V("q", [xs, prev["xm"]], T.cXQ[:, 0:128], T.sXQ[:, 0:128], T.XT[:, :])
        xm = MM(T.px[:, 0:128], T.cSQ[:, 0:128], T.sSQ[:, 0:128], T.cXQ[:, 0:128], T.sXQ[:, 0:128], True, True, [xq, K["sq"], prev["ou"]])
        dq += [half(b) for b in range(len(dq), 4)]
        aside(0)
        if t + 1 < HOPS:
            K["r0"] = V("ts", [K["node"]], T["NK%d" % t][:, 128:192], T["NN%d" % t][:, 128:192], WHOLE, WHOLE, A.add, A.subtract)
        step()
        step()
        if t > 0:
            ou = told = V("ts", [xm], L("OR", t, 0, 8), T.px[:, 0:8], 512.0 * me, None, A.add)
            send("rc", t, "OR", 0, 8, [told])
        else:
            ou = V("copy", [xm], T.OU[:, 0:8], T.px[:, 0:8])
        step()
        if t == 0:
            ks = S(T.sKC[:, 0:128], sKQ[:, 0:512].indirect(T.OU[:, 0:8]), [ou])
            aside(4)
            nd = V("tt", [ou, K["t3"], K["d16"]], T.VD[:, :], T.NXA[:, 512 * me:512 * me + 512].indirect(T.OU[:, 0:8]), T.D16B[:, 0:128], A.mult)
            kc = V("copy", [ou], wd(T.cKC, 0, 128), wd(KQ, 0, 512).indirect(T.OU[:, 0:8]))
            ne = run(nd)
            step()
            told = V("ts", [ne], L("OR", t, 0, 8), T.VE[:, 15:128:16], 1.0 / FINE, 63.5, A.mult, A.add)
            send("rc", t, "OR", 0, 8, [told])
            aside(1)
            h = []
            for b in range(4):
                km = MM(T.pv[:, 512 * b:512 * b + 128], *eq(b), T.cKC[:, 0:128], T.sKC[:, 0:128], False, True, [kc, ks])
                o, i = T.HT[:, b:512:4], T.pv[:, 512 * b:512 * b + 128]
                h.append(S(o, i, [km]) if b % 2 == 0 else V("copy", [km], o, i))
                if b == 1:
                    step()
            ready = h
            ht = None
        else:
            def chosen(b, lo, hi):
                return T.DK[:, PAD + 512 * (b - me):PAD + 512 * b + 512].indirect(L("OR", t, lo, hi))

            gk = [S(T.GK[:, 0:128], chosen(2, 0, 8), [ou, prev["ht"]] + K["dk"]), S(T.GK[:, 128:192], chosen(3, 4, 8), [])]
            aside(1)
            for b in range(2):
                V("tt", [ou, d[b], prev["nq"]] + K["dk"], T.HT[:, b:512:4], chosen(b, 0, 8), T.DQ[:, 128 * b:128 * b + 128], A.add)
            V("tt", [d3], T.HT[:, 3:256:4], chosen(3, 0, 4), T.DQ[:, 256:320], A.add)
            ready = [V("tt", [dq[2], gk[0]], T.HT[:, 2:512:4], T.pv[:, 1024:1152], T.GK[:, 0:128], A.add),
                     V("tt", [dq[3], gk[1]], T.HT[:, 259:512:4], T.pv[:, 1600:1664], T.GK[:, 128:192], A.add)]
            h = d + ready
            ht = ready[1]
        step()
        nq = V("q", ready, T["cRW%d" % t][:, 0:128], T["sRW%d" % t][:, 0:128], T.HT[:, :])
        sendcols("rq%d" % t, "rs%d" % t, "RW%d" % t, 0, 128, nq, nq)
        prev.update({"z": [c0, c1, c2], "pv": h, "t64": t64, "ht": ht, "xm": xm, "ou": ou, "nq": nq})
        aside(2)
        return nq, told

    def where(t):
        md = V("scan", [K["d16"]], T.MD[:, :], T.MK[:, :], T.D16B[:, :], 0.0, A.max, A.mult)
        yield None
        pb = V("scan", [K["rb"]], T.PX[:, :], T.RK[:, 512:768], T.MK[:, :], 0.0, A.max, A.subtract)
        yield None
        ud = V("scan", [md, pb], T.UD[:, :], T.PX[:, :], T.MD[:, :], 0.0, A.max, A.mult)
        yield None
        ff = V("scan", [ud, K["r16"]], T.FF[:, :], T.RS16B[:, :], T.UD[:, :], 0.0, A.mult, A.add)
        yield None
        w = T.FF[:, 0:256].indirect(T.XL[:, 4:5])
        w1 = V("ts", [ff, K["xk"]], T.WW[:, 0:16], w, 64.5 - CAP, None, A.is_gt)
        w3 = V("tt", [ff, K["c16"]], T.WW[:, 32:48], w, T.C16[:, :], A.add)
        yield None
        w5 = V("tt", [w1, w3], T.WW[:, 64:80], T.WW[:, 0:16], T.WW[:, 32:48], A.mult)
        yield None
        w8 = V("scan", [w5, K["aw"]], T.WW[:, 80:96], T.AW[:, :], T.WW[:, 64:80], 0.0, A.max, A.subtract)
        yield None
        K["sl"] = V("copy", [w8], L("SL", t, 0, 4), T.WW[:, 83:96:4])
        while True:
            yield None

    def order(t, held, nq, sl, c, s, o):
        h2 = S(s[:, o:o + 64], T["sRW%d" % t][:, 96:288].indirect(L("SL", t, 0, 4)), [held[-1], nq, sl, ("rs%d" % t, SCALES)])
        h1 = V("copy", [held[0], nq, sl, ("rq%d" % t, CODES)], wd(c, o, o + 64), wd(T["cRW%d" % t], 96, 288).indirect(L("SL", t, 0, 4)))
        return [h1, h2]

    def table(b, lo=0, hi=512):
        r = (me + 1 + b) % NR
        return S(T.NXA[:, 512 * r + lo:512 * r + hi], T.NODF[:, 0:512].indirect(T.NXU[:, 32 * b + lo // 16:32 * b + hi // 16]),
                 [K["nu", b], K["nf"]], -63.5 * FINE, FINE, f=F.Identity)

    def dkc(b):
        K["dk"].append(S(T.DK[:, PAD + 512 * b:PAD + 512 * b + 512], T.pv[:, 512 * b:512 * b + 512], [K["um"][b]]))

    k_sr = V("ts", [d_st], T.STR[:, :], T.STW[:, :], FINE, -63.5 * FINE, A.mult, A.add)

    def gap0(k):
        if k == 0:
            K["su"] = V("copy", [d_st], T.STU[:, :], T.STW[:, :])
            K["d16"] = V("ts", [k_t0, i_r16], T.D16B[:, :], T.R16[:, :], 1.0, T.THR[:, 0:1], A.add, A.is_equal)
        if k == 1:
            K["ez"] = zero(0)
            K["r16"] = S(T.RS16B[:, :], T.R16[:, :], [i_r16], f=F.Sign)
            K["node"] = S(T.NN0[:, 128:192], T.NODF[:, 0:512].indirect(T.STU[:, 0:4]), [K["su"], K["nf"]], -63.5 * FINE, FINE, f=F.Identity)
        if k == 4:
            K["held"] = [V("q", [d_x, m_xt], T.cRW0[:, HELD:HELD + 128], T.sRW0[:, HELD:HELD + 128], T.XT[:, :])]
        if k == 5:
            K["xu"] = V("ts", [x_g], T.XF[:, 0:1], T.XI[:, 0:1], 1.0 / 16, None, A.mult)
            K["xl"] = V("ts", [x_g], T.XL[:, 2:3], T.XI[:, 0:1], 1.0 / 16, 2.0, A.mult, A.add)

    al = lists(0, [k_sr, i_r16], T.R16[:, 0:16].indirect(T.STR[:, :]), gap0)
    node, held = K["node"], K["held"]
    hq0 = held[0]
    own = depart(0, al, held)
    k_e = [S(T.ET[:, EW * h + 2 + h:EW * h + EW:4], T.ID[:, :], [zero(1) if h else K["ez"], k_id], 0.0, 0.5) for h in range(2)]
    for b in range(4):
        K["st"] = S(T.ST[:, b:512:4], T.D16B[:, 0:128], [K["d16"]])
    K["nm"] = S(T.NM64[:, :], T.D16B[:, 0:64], [K["d16"]], -BIG, BIG, f=F.Identity)
    K["rb"] = S(T.RK[:, 512:768], T.RS64[:, 0:256], [m_rs], 65.0, -65.0, f=F.Identity)
    vd = diag(0, al)
    K["m8"] = V("ts", [K["xu"]], T.M8[:, :], T.R16[:, 0:8], T.XF[:, 0:1], BIG, A.not_equal, A.mult)
    vs = tell(0, run(vd))
    own = own()
    i_io4 = IOTA(T.IO4[:, 0:4], [[1, 4]], -512 * me, 0)
    need("g", [i_io4])
    K["tb"] = IOTA(T.TB[32:64, 384:512], [[32, 8], [0, 16]], 0, 0, True)
    need("g", [K["tb"]])
    i_16 = IOTA(T.IO[:, 0:16], [[16, 4], [-32, 4]], 63, 0, True)
    i_k16 = IOTA(T.IO[:, 16:32], [[16, 4], [-1024, 4]], 127, 0, True)
    K["nr"] = IOTA(T.NODR[:, :], [[1, 4], [0, 128]], 0, 0, True)

    def keys(i):
        K["kq", i] = V("q", [d_ky[i]], T.cKQ[:, CUTS[i]:CUTS[i + 1]], T.sKQ[:, CUTS[i]:CUTS[i + 1]], T.KT[:, 4 * CUTS[i]:4 * CUTS[i + 1]])

    def unit(b):
        o = EW * (b % 2) + (2 if b < 2 else 0)
        K["eq", b] = V("q", [k_e[b % 2]], *eq(b), T.ET[:, o:o + 512])

    keys(0)
    keys(1)
    unit(0)
    unit(1)
    x_k = V("ts", [k_pj], T.XI[:, 6:7], T.XI[:, 5:6], 68.0, None, A.mult)
    keys(2)
    K["iq"] = V("ts", [i_io4], T.IQ[:, :], T.IO4[:, 0:4], 0.25, None, A.mult)
    x_k = V("ts", [x_k], T.XI[:, 7:8], T.XI[:, 6:7], 0xF0, None, A.bitwise_and)
    K["nu", 3] = V("copy", [d_no], T.NXU[:, 96:128], T.NXV[:, :])
    find = where(0)

    def links0():
        unit(2)
        yield None
        unit(3)
        yield None
        K["sq"] = V("q", [K["st"]], T.cSQ[:, 0:128], T.sSQ[:, 0:128], T.ST[:, :])
        yield None
        for _ in range(3):
            yield next(find)
        next(find)
        K["xk"] = V("ts", [x_k], T.XL[:, 4:5], T.XI[:, 7:8], 15.0, None, A.add)
        yield None
        while True:
            yield next(find)

    rest = links0()
    d_nx = {}
    for b in range(3):
        for k in range(8):
            d_nx[b] = DMA("y", "dnx" if b else "dn0", T.NXW[16 * k:16 * k + 16, 32 * b:32 * b + 32], T["NXR%d" % b][:, :],
                          [("nxr", 3 * len(e16))] + ([("av0", LIST), ("aq0", CODES + SCALES)] if b else []))
    d_w = DMA("y", "dw", T.WT[:, :], T.w[:, :])
    DMA("y", "dh3", by(T.cHQ3, 64, 128), by(T.cRW0, HELD + 64, HELD + 128), [hq0])
    d_h3 = DMA("y", "dh3", T.sHQ3[:, 64:128], T.sRW0[:, HELD + 64:HELD + 128], [hq0])

    def aside0(k):
        if k == 3:
            K["c16"] = S(T.C16[:, :], T.IO[:, 0:16], [i_16, k_t0], T.THR[:, 0:1], f=F.Identity)
            K["aw"] = S(T.AW[:, :], T.IO[:, 16:32], [i_k16, k_t0], T.THR[:, 0:1], f=F.Identity)
            K["t3"] = table(3)
        if k == 0:
            K["nu", 0] = V("copy", [d_nx[0]], T.NXU[:, 0:32], T.NXW[:, 0:32])
            K["nxa"] = [K["t3"], table(0, 0, 256)]
        if k == 4:
            K["nxa"].append(table(0, 256, 512))
        if k == 1:
            next(find)
        if k == 2:
            next(find)
            K["dk"] = []
            K["um"] = [MM(T.pv[:, 512 * b:512 * b + 512], *eq(b), T.cKQ[:, 0:512], T.sKQ[:, 0:512], True, True, [prev["pv"][b]]) for b in range(4)]

    def aside1(k):
        if k == 3:
            K["nxa"] += [table(1, 256, 512), table(2, 0, 256)]
        if k == 1:
            K["nxa"].append(table(2, 256, 512))
        if k == 0:
            K["wq"] = V("q", [d_w], T.cWQ[:, 0:128], T.sWQ[:, 0:128], T.WT[:, :])

    prev = {"z": [None] * 3, "pv": [None] * 4, "t64": None, "ht": None, "xm": None, "ou": None, "nq": None}
    for t in range(HOPS):
        n = T["NN%d" % t]
        if t == 0:
            nq, told = server(0, own, vs, prev, aside0, lambda: next(rest))
        else:
            if t == 1:
                dkc(1)
                dkc(2)
                next(find)
                K["dk"].append(V("copy", [K["um"][3]], T.DK[:, PAD + 1536:PAD + 2048], T.pv[:, 1536:2048]))
                prev["pv"] = K["dk"]
                K["nxa"].append(table(1, 0, 256))
            else:
                next(find)
            next(find)
            nq, told = server(t, own, vs, prev, aside1 if t == 1 else lambda k: None, lambda: next(find))
        sl = K["sl"]
        tab, tabs, scale, bias = (T.NODF[:, 0:512], [], FINE, -63.5 * FINE) if t == 0 else (T.NXA[:, 0:2048], K["nxa"], 1.0, 0.0)
        slots, tabs = tab.indirect(L("OR", t, 6, 14)), tabs + [told, ("rc%d" % t, LIST)]
        byq = n[:, 0:192].indirect(L("SL", t, 0, 4))
        if t + 1 == HOPS:
            g1 = V("copy", tabs, n[:, 0:128], slots)
            nd = V("ts", [g1, sl, node], T.ND[:, 64 * HOPS:64 * HOPS + 64], byq, 1.0 / FINE, 63.5, A.mult, A.add)
            DMA("y", "dout", T.nd[:, :], T.ND[0:1, 0:256], [nd, K["was"]])
            hq = order(t, held, nq, sl, T.cHQ3, T.sHQ3, 0)
            break
        nk = T["NK%d" % t]
        g1 = S(n[:, 0:128], slots, tabs, bias, scale, f=F.Identity)
        if t == 0:
            r1 = V("copy", tabs + [K["nr"]], nk[:, 0:128], T.NODR[:, 0:512].indirect(L("OR", t, 6, 14)))
        else:
            r1 = V("ts", tabs, nk[:, 0:128], slots, WHOLE, WHOLE, A.add, A.subtract)

        def gap(k):
            if k == 1:
                if t == 0:
                    dkc(0)
                K["node"] = S(T["NN%d" % (t + 1)][:, 128:192], byq, [g1, sl, node])
            if k == 4:
                K["held"] = order(t, held, nq, sl, T["cRW%d" % (t + 1)], T["sRW%d" % (t + 1)], HELD)
            if k == 5 and t == 0:
                K["nu", 1] = K["nu", 2] = V("copy", [d_nx[2]], T.NXU[:, 32:96], T.NXW[:, 32:96])

        al = lists(t + 1, [K["r0"], r1, sl], nk[:, 0:192].indirect(L("SL", t, 0, 4)), gap)
        node, held = K["node"], K["held"]
        own = depart(t + 1, al, held)
        vd = diag(t + 1, al)
        find = where(t + 1)
        next(find)
        ve = run(vd)
        next(find)
        vs = tell(t + 1, ve)
        own = own()

    DMA("y", "dout", T.oc[:, :], by(T.cHQ3, 0, 64), [hq[0]])
    for k in range(4):
        DMA("s" if k < 3 else "y", "dout", T.osc[4 * k:4 * k + 4, 0:64], T.sHQ3[32 * k:32 * k + 4, 0:64], [hq[1]])
    ym = MM(T.px[:, 0:128], T.cWQ[:, 0:128], T.sWQ[:, 0:128], T.cHQ3[:, 0:128], T.sHQ3[:, 0:128], True, True, hq + [K["wq"], d_h3, prev["ou"]])
    yc = V("copy", [ym], T.YS[:, :], T.px[:, 0:64])
    DMA("y", "dout", T.y[:, :], T.YS[:, :], [yc])
    for sem in ("dout", "ls", "cv", "cs", "ct", "cg", "dst", "dx", "dk0", "dk1", "dk2", "dnx", "dn0", "dno", "dnd", "dw", "dh3"):
        need("g", [(sem, count[sem])])
